import numpy as np
import ml_dtypes


def mxq(x, axis, fmt="e4m3"):
    dtype, down = {"e4m3": (ml_dtypes.float8_e4m3fn, 7), "e5m2": (ml_dtypes.float8_e5m2, 14)}[fmt]
    v = np.moveaxis(np.asarray(x, np.float32).astype(ml_dtypes.bfloat16).astype(np.float64), axis, -1)
    blocks = v.reshape(v.shape[:-1] + (-1, 32))
    amax = np.abs(blocks).max(-1, keepdims=True)
    byte = np.maximum(np.where(amax > 0, np.frexp(amax)[1] - 1 + 127, 0) - down, 1)
    scale = np.exp2(byte - 127.0)
    codes = (blocks / scale).astype(np.float32).astype(dtype).astype(np.float64)
    return np.moveaxis((codes * scale).reshape(v.shape), -1, axis)


WIDE = False


def mx_kscale(k):
    if not WIDE:
        return np.ones(k)
    levels = np.array([10, -10, 5, -5, 0])
    if k % 512:
        return np.exp2(np.random.permutation(np.resize(levels, k // 32))).repeat(32)
    a = np.empty((k // 512, 16))
    for p in range(k // 512):
        a[p, :8] = np.random.permutation(np.resize(levels, 8))
        for g in range(8):
            far = levels[np.abs(levels - a[p, g]) >= 10]
            a[p, g + 8] = far[np.random.randint(len(far))]
    return np.exp2(a.ravel()).repeat(32)


def f64(x):
    return np.asarray(x).astype(np.float64)


def striped(idx):
    return np.tile(idx.reshape(-1, 16).T, (8, 1)).astype(np.uint16)


def unstriped(offs):
    return offs[:16].T.reshape(-1).astype(np.int64)


E2M1 = np.array([0.0, 0.5, 1.0, 1.5, 2.0, 3.0, 4.0, 6.0, -0.0, -0.5, -1.0, -1.5, -2.0, -3.0, -4.0, -6.0])


def pack_weight(w, fmt):
    k, n = w.shape
    w = f64(np.asarray(w, np.float32).astype(ml_dtypes.bfloat16)).reshape(k // 32, 32, n)
    amax = np.abs(w).max(1)
    if fmt == "e4m3":
        byte = np.frexp(amax)[1] - 1 + 127 - 7
    else:
        mant, ex = np.frexp(amax / 6.0)
        byte = np.where(mant > 0.5, ex, ex - 1) + 127
    byte = np.clip(np.where(amax > 0, byte, 1), 1, 254)
    scaled = (w * np.exp2(127.0 - byte)[:, None, :]).reshape(k, n).astype(np.float32)
    by_word = np.ascontiguousarray(scaled.reshape(k // 512, 128, 4, n).transpose(0, 1, 3, 2))
    if fmt == "e4m3":
        words = by_word.astype(ml_dtypes.float8_e4m3fn).view(np.uint8)
    else:
        c = by_word.astype(ml_dtypes.float4_e2m1fn).view(np.uint8) & 0xF
        words = (c[..., 0::2] | (c[..., 1::2] << 4)).reshape(k // 512, 128, 2 * n)
    return np.ascontiguousarray(words), np.ascontiguousarray(byte.astype(np.uint8).reshape(k // 512, 16, n))


def unpack_weight(words, scales, fmt):
    g, _, n = scales.shape
    words = np.ascontiguousarray(words).reshape(g, 128, n, -1)
    if fmt == "e4m3":
        vals = words.view(ml_dtypes.float8_e4m3fn).astype(np.float64)
    else:
        nib = np.empty((g, 128, n, 4), np.uint8)
        nib[..., 0::2] = words & 0xF
        nib[..., 1::2] = words >> 4
        vals = E2M1[nib]
    vals = vals * np.repeat(np.exp2(scales.astype(np.float64) - 127.0), 8, axis=1)[..., None]
    return vals.transpose(0, 1, 3, 2).reshape(g * 512, n)


def gelu(v):
    return 0.5 * v * (1.0 + np.tanh(np.sqrt(2.0 / np.pi) * (v + 0.044715 * v**3)))


K, H, N, T, S, T2, P = 1024, 512, 384, 4096, 1024, 2048, 1024

def setup_inputs():
    n = np.random.standard_normal
    s = mx_kscale(K)[:, None]
    u = mx_kscale(H)[:, None]
    tab_words, tab_scales = pack_weight(n((K, T)) * s, "e4m3")
    w4_words, w4_scales = pack_weight(1.5 * n((K, H)) / np.sqrt(K) / s, "e2m1")
    w8_words, w8_scales = pack_weight(n((K, H)) / np.sqrt(K) / s * u.T, "e4m3")
    return {
        "tab_words": tab_words, "tab_scales": tab_scales,
        "offs": striped(np.random.permutation(T)[:S]),
        "w4_words": w4_words, "w4_scales": w4_scales,
        "w8_words": w8_words, "w8_scales": w8_scales,
        "w1": (n((K, H)) / np.sqrt(K) / s * u.T).astype(np.float32),
        "offs2": striped(np.random.permutation(T2)[:S]),
        "wgs": np.exp(0.3 * n((128, S))).astype(np.float32),
        "buf": (n((H, T2)) * u).astype(np.float32),
        "w2": (n((H, N)) / np.sqrt(H) / u).astype(np.float32),
        "offs3": striped(np.random.permutation(T2)[:P]),
        "offs4": striped(np.random.permutation(T2)[:P]),
        "wgo": np.exp(0.3 * n((128, P))).astype(np.float32),
    }

def reference(tab_words, tab_scales, offs, w4_words, w4_scales, w8_words, w8_scales, w1, offs2, wgs, buf, w2, offs3, offs4, wgo):
    v = unpack_weight(tab_words, tab_scales, "e4m3")[:, unstriped(offs)]
    ga = unpack_weight(w4_words, w4_scales, "e2m1").T @ v
    move = unpack_weight(w8_words, w8_scales, "e4m3").T @ v
    hold = mxq(f64(w1), 0, "e4m3").T @ v
    sg = 1.0 / (1.0 + np.exp(-ga))
    h = hold + sg * (move - hold)
    page = np.zeros((H, T2))
    page[:, unstriped(offs2)] = np.tile(f64(wgs), (H // 128, 1)) * h
    z = page + f64(buf)
    y = mxq(f64(w2), 0, "e4m3").T @ mxq(z, 0, "e4m3")
    x = np.tanh(y[:, unstriped(offs3)])
    out = np.zeros((N, T2))
    out[:, unstriped(offs4)] = np.tile(f64(wgo), (N // 128, 1)) * x
    return out

@@ -1,0 +1,318 @@
+from contextlib import ExitStack
+
+import concourse.mybir as mybir
+from concourse.masks import make_identity
+
+K, H, N, T, S, T2, P_OUT = 1024, 512, 384, 4096, 1024, 2048, 1024
+FLOPS = 2 * (3 * K * H * S + H * N * T2)
+
+F32 = mybir.dt.float32
+BF16 = mybir.dt.bfloat16
+I32 = mybir.dt.int32
+U32 = mybir.dt.uint32
+U16 = mybir.dt.uint16
+U8 = mybir.dt.uint8
+FP8X4 = mybir.dt.float8_e4m3fn_x4
+FP4X4 = mybir.dt.float4_e2m1fn_x4
+ALU = mybir.AluOpType
+ACT = mybir.ActivationFunctionType
+
+P = 128
+PASSES = K // 512
+SLICES = H // P
+CHUNK = 512
+CHUNKS = S // CHUNK
+BANK = 512
+USE_POOL = True
+
+
+def tile_list_tote_lane_features_kernel(
+    tc, tab_words, tab_scales, offs, w4_words, w4_scales, w8_words, w8_scales, w1, offs2, wgs, buf, w2, offs3, offs4, wgo, out
+):
+    nc = tc.nc
+    with ExitStack() as ctx:
+        keep = ctx.enter_context(tc.tile_pool(name="keep", bufs=1))
+        ring = ctx.enter_context(tc.tile_pool(name="ring", bufs=4))
+        psum = ctx.enter_context(tc.psum_pool(name="psum", bufs=1))
+
+        def held(name, shape, dtype, tag=None):
+            return keep.tile(shape, dtype, name=name, tag=tag or name, align_bytes=64)
+
+        def bank(b, name):
+            return psum.tile([P, BANK], F32, name=name, tag="bank%d" % b)
+
+        list1 = held("list1", [P, S // 16], U16)
+        list2 = held("list2", [P, S // 16], U16)
+        list3 = held("list3", [P, P_OUT // 16], U16)
+        list4 = held("list4", [P, P_OUT // 16], U16)
+        tab_s = held("tab_s", [P, T], U8, tag="early_a")
+        tab_w = [held("tab_w%d" % a, [P, T], U32, tag="big%d" % a) for a in range(PASSES)]
+        w4_s = held("w4_s", [P, PASSES, H], U8)
+        w8_s = held("w8_s", [P, PASSES, H], U8)
+        v_s = held("v_s", [P, PASSES, S], U8)
+        w1_raw0 = held("w1_raw0", [P, PASSES, 4, P], F32)
+        w1_raw = held("w1_raw", [P, PASSES, 4, H - P], F32, tag="w1_raw")
+        w8_c = held("w8_c", [P, PASSES, H], U32)
+        w4_c = held("w4_c", [P, PASSES, 2 * H], U8)
+        wgs_sb = held("wgs_sb", [P, S], F32)
+        wgo_sb = held("wgo_sb", [P, P_OUT], F32)
+        w2_raw = held("w2_raw", [P, 4, N], F32)
+
+        for plane in (w4_s, w8_s):
+            nc.vector.memset(plane[:].rearrange("p a c -> p (a c)").bitcast(I32), 0)
+        nc.vector.memset(tab_s[:].bitcast(I32)[32:64, :], 0)
+        nc.vector.memset(tab_s[:].bitcast(I32)[64:128, :], 0)
+        nc.vector.memset(v_s[:].rearrange("p a c -> p (a c)").bitcast(I32), 0)
+
+        warm = held("warm", [P, 2], F32)
+        nc.vector.memset(warm[:, 0:1], 0.0)
+        nc.scalar.activation(out=warm[:, 1:2], in_=warm[:, 0:1], func=ACT.Sigmoid)
+
+        nc.sync.dma_start(list1[:], offs)
+        nc.sync.dma_start(out=tab_s[:].bitcast(I32)[0:32, :], in_=tab_scales.rearrange("a q t -> (a q) t").bitcast(I32))
+        tab_words_i = tab_words.rearrange("a p t i -> a p (t i)").bitcast(I32)
+        nc.sync.dma_start(out=tab_w[0][:].bitcast(I32), in_=tab_words_i[0])
+        w1_rows = w1.rearrange("(a p j) c -> a p j c", a=PASSES, j=4)
+        for a in range(PASSES):
+            nc.sync.dma_start(out=w1_raw0[:, a, :, :], in_=w1_rows[a][:, :, 0:P])
+        w8_words_i = w8_words.rearrange("a p c i -> p a (c i)").bitcast(I32)
+        nc.sync.dma_start(out=w8_c[:].bitcast(I32)[:, :, 0:P], in_=w8_words_i[:, :, 0:P])
+        nc.sync.dma_start(out=w4_c[:].bitcast(I32), in_=w4_words.rearrange("a p c -> p a c").bitcast(I32))
+        nc.sync.dma_start(out=tab_w[1][:].bitcast(I32), in_=tab_words_i[1])
+        for q in range(4):
+            nc.gpsimd.dma_start(
+                out=w4_s[:].bitcast(I32)[32 * q : 32 * q + 4, :, :],
+                in_=w4_scales.rearrange("a r c -> r a c").bitcast(I32)[4 * q : 4 * q + 4, :, :],
+            )
+        for q in range(4):
+            nc.scalar.dma_start(
+                out=w8_s[:].bitcast(I32)[32 * q : 32 * q + 4, :, :],
+                in_=w8_scales.rearrange("a r c -> r a c").bitcast(I32)[4 * q : 4 * q + 4, :, :],
+            )
+        nc.sync.dma_start(out=wgs_sb[:], in_=wgs)
+        nc.sync.dma_start(list2[:], offs2)
+        for a in range(PASSES):
+            nc.sync.dma_start(out=w1_raw[:, a, :, :], in_=w1_rows[a][:, :, P:H])
+        nc.sync.dma_start(out=w8_c[:].bitcast(I32)[:, :, P:H], in_=w8_words_i[:, :, P:H])
+        nc.sync.dma_start(out=w2_raw[:], in_=w2.rearrange("(p j) n -> p j n", j=4))
+
+        ident = held("ident", [P, P], F32)
+        make_identity(nc, ident[:])
+
+        picked_s = held("picked_s", [P, S], U8, tag="early_b")
+        nc.vector.tensor_copy(picked_s[:], tab_s[:].indirect(list1[:]))
+        for a in range(PASSES):
+            for q in range(4):
+                nc.scalar.dma_start(
+                    out=v_s[:].bitcast(I32)[32 * q : 32 * q + 4, a, :],
+                    in_=picked_s[:].bitcast(I32)[16 * a + 4 * q : 16 * a + 4 * q + 4, :],
+                )
+        v_w = [held("v_w%d" % a, [P, S], U32) for a in range(PASSES)]
+        nc.vector.tensor_copy(v_w[0][:], tab_w[0][:].indirect(list1[:]))
+
+        w1_g = held("w1_g", [P, SLICES, PASSES, P, 4], BF16)
+        w1_c = held("w1_c", [P, SLICES, PASSES, P], U32)
+        w1_s = held("w1_s", [P, SLICES, PASSES, P], U8)
+
+        def round_w1(s):
+            for a in range(PASSES):
+                raw = w1_raw0[:, a, :, :] if s == 0 else w1_raw[:, a, :, (s - 1) * P : s * P]
+                nc.scalar.copy(
+                    out=w1_g[:, s, a, :, :].rearrange("p (c i) j -> p c j i", i=4),
+                    in_=raw.rearrange("p j (c i) -> p c j i", i=4),
+                )
+
+        def quantise_w1(s0, s1):
+            nc.vector.quantize_mx(
+                out=w1_c[:, s0:s1, :, :].rearrange("p s a c -> p (s a c)").bitcast(FP8X4),
+                scales=w1_s[:, s0:s1, :, :].rearrange("p s a c -> p (s a c)"),
+                in_=w1_g[:, s0:s1, :, :, :].rearrange("p s a c j -> p (s a c j)"),
+            )
+
+        round_w1(0)
+        quantise_w1(0, 1)
+
+        pages = [held("page%d" % s, [P, T2], F32) for s in range(SLICES)]
+        for s in range(2):
+            nc.vector.memset(pages[s][:], 0.0)
+        for s in range(2, SLICES):
+            for q in range(4):
+                nc.gpsimd.memset(pages[s][:, q * BANK : (q + 1) * BANK], 0.0)
+
+        cols16 = CHUNK // 16
+        for c in range(CHUNKS):
+            nc.vector.tensor_copy(v_w[1][:, c * CHUNK : (c + 1) * CHUNK], tab_w[1][:].indirect(list1[:, c * cols16 : (c + 1) * cols16]))
+
+        lanes = [
+            held("lanes0", [P, T2], F32, tag="early_a"),
+            held("lanes1", [P, T2], F32, tag="early_b"),
+        ]
+        for n in range(2):
+            for q in range(4):
+                nc.gpsimd.memset(lanes[n][:, q * BANK : (q + 1) * BANK], 0.0)
+
+        buf_sb = [held("buf_sb%d" % a, [P, 2, T2], F32, tag="big%d" % a) for a in range(2)]
+        for s in range(SLICES):
+            nc.sync.dma_start(out=buf_sb[s // 2][:, s % 2, :], in_=buf[s * P : (s + 1) * P, :])
+        nc.sync.dma_start(list3[:], offs3)
+        nc.sync.dma_start(list4[:], offs4)
+        nc.sync.dma_start(out=wgo_sb[:], in_=wgo)
+
+        ready = {}
+
+        def first_stage(k):
+            s, c = divmod(k, CHUNKS)
+            cols = slice(c * CHUNK, (c + 1) * CHUNK)
+            rows = slice(s * P, (s + 1) * P)
+            hold_ps = bank(0, "hold_ps")
+            move_ps = bank(2 + k % 2, "move_ps")
+            gate_ps = bank(1, "gate_ps")
+            products = (
+                (hold_ps, lambda a: (w1_c[:, s, a, :].bitcast(FP8X4), w1_s[:, s, a, :])),
+                (move_ps, lambda a: (w8_c[:, a, rows].bitcast(FP8X4), w8_s[:, a, rows])),
+                (gate_ps, lambda a: (w4_c[:, a, 2 * s * P : 2 * (s + 1) * P].bitcast(FP4X4), w4_s[:, a, rows])),
+            )
+            for a in range(PASSES):
+                for acc, weight in products:
+                    codes, scales = weight(a)
+                    nc.tensor.matmul_mx(
+                        out=acc[:], lhsT=codes, lhsT_scale=scales,
+                        rhs=v_w[a][:, cols].bitcast(FP8X4), rhs_scale=v_s[:, a, cols],
+                        start=(a == 0), stop=(a == PASSES - 1),
+                    )
+            hold = ring.tile([P, CHUNK], F32, name="hold")
+            gate = ring.tile([P, CHUNK], F32, name="gate")
+            h = ring.tile([P, CHUNK], F32, name="h")
+            nc.scalar.copy(out=hold[:], in_=hold_ps[:])
+            nc.scalar.activation(out=gate[:], in_=gate_ps[:], func=ACT.Sigmoid)
+            nc.vector.tensor_tensor(h[:], move_ps[:], hold[:], ALU.subtract)
+            eng = nc.gpsimd if (USE_POOL and k > 0) else nc.vector
+            eng.tensor_tensor(h[:], h[:], gate[:], ALU.mult)
+            eng.tensor_tensor(h[:], h[:], hold[:], ALU.add)
+            if USE_POOL:
+                eng.tensor_tensor(h[:], h[:], wgs_sb[:, cols], ALU.mult)
+            ready[k] = h
+
+        def place(k):
+            s, c = divmod(k, CHUNKS)
+            window = pages[s][:].indirect(list2[:, c * cols16 : (c + 1) * cols16])
+            if USE_POOL:
+                nc.vector.tensor_copy(window, ready[k][:])
+            else:
+                nc.vector.tensor_tensor(window, ready[k][:], wgs_sb[:, c * CHUNK : (c + 1) * CHUNK], ALU.mult)
+
+        QUARTERS = T2 // BANK
+        z_t = [held("z_t%d" % q, [P, 4, H], BF16) for q in range(QUARTERS)]
+        sums = {}
+
+        def turn_buf(s):
+            for q in range(QUARTERS):
+                acc = bank(4 + q, "z_ps")
+                sums[q] = acc
+                for b in range(4):
+                    c0 = q * BANK + b * P
+                    nc.tensor.matmul(out=acc[:, b * P : (b + 1) * P], lhsT=buf_sb[s // 2][:, s % 2, c0 : c0 + P], rhs=ident[:],
+                                     is_transpose=True, start=(b == 0), stop=False)
+
+        def turn_page(s, q, copy):
+            acc = sums[q]
+            for b in range(4):
+                c0 = q * BANK + b * P
+                nc.tensor.matmul(out=acc[:, b * P : (b + 1) * P], lhsT=pages[s][:, c0 : c0 + P], rhs=ident[:],
+                                 is_transpose=True, start=False, stop=(b == 3))
+            copy(
+                out=z_t[q][:].rearrange("c b (u p e) -> c b u p e", u=2, e=2)[:, :, :, 32 * s : 32 * (s + 1), :],
+                in_=acc[:].rearrange("c (b p u e) -> c b u p e", b=4, u=2, e=2),
+            )
+
+        w2_g = held("w2_g", [P, N, 4], BF16)
+        w2_c = held("w2_c", [P, N], U32)
+        w2_s = held("w2_s", [P, N], U8)
+
+        first_stage(0)
+        first_stage(1)
+        round_w1(1)
+        quantise_w1(1, 2)
+        round_w1(2)
+        round_w1(3)
+        for k in range(SLICES * CHUNKS):
+            s, c = divmod(k, CHUNKS)
+            place(k)
+            if k == 0:
+                quantise_w1(2, 4)
+            if k == 1:
+                nc.scalar.copy(
+                    out=w2_g[:].rearrange("p (c i) j -> p c j i", i=4),
+                    in_=w2_raw[:].rearrange("p j (c i) -> p c j i", i=4),
+                )
+            if k == 2:
+                for n0, n1 in ((0, 256), (256, N)):
+                    nc.vector.quantize_mx(out=w2_c[:, n0:n1].bitcast(FP8X4), scales=w2_s[:, n0:n1],
+                                          in_=w2_g[:, n0:n1, :].rearrange("p c j -> p (c j)"))
+            if k + 2 < SLICES * CHUNKS:
+                first_stage(k + 2)
+            if c == 0:
+                turn_buf(s)
+            if c == CHUNKS - 1 and s < SLICES - 1:
+                for q in range(QUARTERS):
+                    turn_page(s, q, nc.scalar.copy)
+
+        z_c = held("z_c", [P, T2], U32, tag="z_c")
+        z_s = held("z_s", [P, T2], U8)
+        ys = [
+            held("y0", [P, T2], F32, tag="big0"),
+            held("y1", [P, T2], F32, tag="big1"),
+            held("y2", [P, T2], F32, tag="w1_raw"),
+        ]
+
+        def second_product(n, q, b, copy):
+            cols = slice(q * BANK, (q + 1) * BANK)
+            y_ps = bank(b, "y_ps")
+            nc.tensor.matmul_mx(
+                out=y_ps[:], lhsT=w2_c[:, n * P : (n + 1) * P].bitcast(FP8X4), lhsT_scale=w2_s[:, n * P : (n + 1) * P],
+                rhs=z_c[:, cols].bitcast(FP8X4), rhs_scale=z_s[:, cols], start=True, stop=True,
+            )
+            copy(out=ys[n][:, cols], in_=y_ps[:])
+
+        for q in range(QUARTERS):
+            turn_page(SLICES - 1, q, nc.vector.tensor_copy if q % 2 == 0 else nc.scalar.copy)
+        for q in range(QUARTERS):
+            words = z_t[q][:].bitcast(F32)
+            for half in range(2):
+                back = bank((2 * q + half) % 4, "back_ps")
+                for b in range(2):
+                    for u in range(2):
+                        nc.tensor.transpose(back[:, (2 * b + u) * P : (2 * b + u + 1) * P],
+                                            words[:, 2 * half + b, u * P : (u + 1) * P], ident[:])
+                z_g = ring.tile([P, 2 * P * 4], BF16, name="z_g", align_bytes=64)
+                copy = nc.vector.tensor_copy if (2 * q + half) % 3 == 2 else nc.scalar.copy
+                copy(out=z_g[:].bitcast(F32).rearrange("p (b c u) -> p b c u", b=2, u=2),
+                     in_=back[:].rearrange("p (b u c) -> p b c u", b=2, u=2))
+                c0 = q * BANK + half * 2 * P
+                nc.vector.quantize_mx(out=z_c[:, c0 : c0 + 2 * P].bitcast(FP8X4), scales=z_s[:, c0 : c0 + 2 * P], in_=z_g[:])
+            second_product(0, q, 4 + q, nc.vector.tensor_copy if q == QUARTERS - 1 else nc.scalar.copy)
+        for n in range(1, N // P):
+            for q in range(QUARTERS):
+                second_product(n, q, (4 * (n - 1) + q) % 8, nc.scalar.copy)
+
+        lanes.append(held("lanes2", [P, T2], F32, tag="z_c"))
+        nc.gpsimd.memset(lanes[2][:], 0.0)
+
+        picked = []
+
+        def pick(n):
+            x = keep.tile([P, P_OUT], F32, name="x%d" % n)
+            nc.vector.tensor_copy(x[:], ys[n][:].indirect(list3[:]))
+            nc.scalar.activation(out=x[:], in_=x[:], func=ACT.Tanh)
+            picked.append(x)
+
+        def discharge(n):
+            nc.vector.tensor_tensor(lanes[n][:].indirect(list4[:]), picked[n][:], wgo_sb[:], ALU.mult)
+            nc.sync.dma_start(out=out[n * P : (n + 1) * P, :], in_=lanes[n][:])
+
+        pick(0)
+        pick(1)
+        discharge(0)
+        pick(2)
+        discharge(1)
+        discharge(2)

@@ -51,7 +51,8 @@ def tile_list_tote_lane_features_kernel(
         w8_s = held("w8_s", [P, PASSES, H], U8)
         v_s = held("v_s", [P, PASSES, S], U8)
         w1_raw0 = held("w1_raw0", [P, PASSES, 4, P], F32)
-        w1_raw = held("w1_raw", [P, PASSES, 4, H - P], F32, tag="w1_raw")
+        w1_raw1 = held("w1_raw1", [P, PASSES, 4, P], F32)
+        w1_raw = held("w1_raw", [P, PASSES, 4, 2 * P], F32, tag="w1_raw")
         w8_c = held("w8_c", [P, PASSES, H], U32)
         w4_c = held("w4_c", [P, PASSES, 2 * H], U8)
         wgs_sb = held("wgs_sb", [P, S], F32)
@@ -60,8 +61,7 @@ def tile_list_tote_lane_features_kernel(
 
         for plane in (w4_s, w8_s):
             nc.vector.memset(plane[:].rearrange("p a c -> p (a c)").bitcast(I32), 0)
-        nc.vector.memset(tab_s[:].bitcast(I32)[32:64, :], 0)
-        nc.vector.memset(tab_s[:].bitcast(I32)[64:128, :], 0)
+        nc.vector.memset(tab_s[:].bitcast(I32)[0:96, :], 0)
         nc.vector.memset(v_s[:].rearrange("p a c -> p (a c)").bitcast(I32), 0)
 
         warm = held("warm", [P, 2], F32)
@@ -69,7 +69,7 @@ def tile_list_tote_lane_features_kernel(
         nc.scalar.activation(out=warm[:, 1:2], in_=warm[:, 0:1], func=ACT.Sigmoid)
 
         nc.sync.dma_start(list1[:], offs)
-        nc.sync.dma_start(out=tab_s[:].bitcast(I32)[0:32, :], in_=tab_scales.rearrange("a q t -> (a q) t").bitcast(I32))
+        nc.sync.dma_start(out=tab_s[:].bitcast(I32)[96:128, :], in_=tab_scales.rearrange("a q t -> (a q) t").bitcast(I32))
         tab_words_i = tab_words.rearrange("a p t i -> a p (t i)").bitcast(I32)
         nc.sync.dma_start(out=tab_w[0][:].bitcast(I32), in_=tab_words_i[0])
         w1_rows = w1.rearrange("(a p j) c -> a p j c", a=PASSES, j=4)
@@ -89,11 +89,13 @@ def tile_list_tote_lane_features_kernel(
                 out=w8_s[:].bitcast(I32)[32 * q : 32 * q + 4, :, :],
                 in_=w8_scales.rearrange("a r c -> r a c").bitcast(I32)[4 * q : 4 * q + 4, :, :],
             )
+        for a in range(PASSES):
+            nc.sync.dma_start(out=w1_raw1[:, a, :, :], in_=w1_rows[a][:, :, P : 2 * P])
+        nc.sync.dma_start(out=w8_c[:].bitcast(I32)[:, :, P:H], in_=w8_words_i[:, :, P:H])
         nc.sync.dma_start(out=wgs_sb[:], in_=wgs)
         nc.sync.dma_start(list2[:], offs2)
         for a in range(PASSES):
-            nc.sync.dma_start(out=w1_raw[:, a, :, :], in_=w1_rows[a][:, :, P:H])
-        nc.sync.dma_start(out=w8_c[:].bitcast(I32)[:, :, P:H], in_=w8_words_i[:, :, P:H])
+            nc.sync.dma_start(out=w1_raw[:, a, :, :], in_=w1_rows[a][:, :, 2 * P : H])
         nc.sync.dma_start(out=w2_raw[:], in_=w2.rearrange("(p j) n -> p j n", j=4))
 
         ident = held("ident", [P, P], F32)
@@ -105,7 +107,7 @@ def tile_list_tote_lane_features_kernel(
             for q in range(4):
                 nc.scalar.dma_start(
                     out=v_s[:].bitcast(I32)[32 * q : 32 * q + 4, a, :],
-                    in_=picked_s[:].bitcast(I32)[16 * a + 4 * q : 16 * a + 4 * q + 4, :],
+                    in_=picked_s[:].bitcast(I32)[96 + 16 * a + 4 * q : 96 + 16 * a + 4 * q + 4, :],
                 )
         v_w = [held("v_w%d" % a, [P, S], U32) for a in range(PASSES)]
         nc.vector.tensor_copy(v_w[0][:], tab_w[0][:].indirect(list1[:]))
@@ -116,7 +118,7 @@ def tile_list_tote_lane_features_kernel(
 
         def round_w1(s):
             for a in range(PASSES):
-                raw = w1_raw0[:, a, :, :] if s == 0 else w1_raw[:, a, :, (s - 1) * P : s * P]
+                raw = (w1_raw0, w1_raw1)[s][:, a, :, :] if s < 2 else w1_raw[:, a, :, (s - 2) * P : (s - 1) * P]
                 nc.scalar.copy(
                     out=w1_g[:, s, a, :, :].rearrange("p (c i) j -> p c j i", i=4),
                     in_=raw.rearrange("p j (c i) -> p c j i", i=4),
@@ -229,10 +231,10 @@ def tile_list_tote_lane_features_kernel(
         w2_c = held("w2_c", [P, N], U32)
         w2_s = held("w2_s", [P, N], U8)
 
-        first_stage(0)
-        first_stage(1)
         round_w1(1)
         quantise_w1(1, 2)
+        first_stage(0)
+        first_stage(1)
         round_w1(2)
         round_w1(3)
         for k in range(SLICES * CHUNKS):
@@ -251,9 +253,9 @@ def tile_list_tote_lane_features_kernel(
                                           in_=w2_g[:, n0:n1, :].rearrange("p c j -> p (c j)"))
             if k + 2 < SLICES * CHUNKS:
                 first_stage(k + 2)
-            if c == 0:
-                turn_buf(s)
-            if c == CHUNKS - 1 and s < SLICES - 1:
+        for s in range(SLICES):
+            turn_buf(s)
+            if s < SLICES - 1:
                 for q in range(QUARTERS):
                     turn_page(s, q, nc.scalar.copy)
 

@@ -33,10 +33,14 @@ def tile_list_tote_lane_features_kernel(
     with ExitStack() as ctx:
         keep = ctx.enter_context(tc.tile_pool(name="keep", bufs=1))
         ring = ctx.enter_context(tc.tile_pool(name="ring", bufs=4))
+        arena = ctx.enter_context(tc.tile_pool(name="arena", bufs=1))
         psum = ctx.enter_context(tc.psum_pool(name="psum", bufs=1))
 
         def held(name, shape, dtype, tag=None):
             return keep.tile(shape, dtype, name=name, tag=tag or name, align_bytes=64)
+
+        def placed(name, shape, dtype, kib):
+            return arena.tile(shape, dtype, name=name, align_bytes=64, offset=kib * 1024)
 
         def bank(b, name):
             return psum.tile([P, BANK], F32, name=name, tag="bank%d" % b)
@@ -45,19 +49,13 @@ def tile_list_tote_lane_features_kernel(
         list2 = held("list2", [P, S // 16], U16)
         list3 = held("list3", [P, P_OUT // 16], U16)
         list4 = held("list4", [P, P_OUT // 16], U16)
-        tab_s = held("tab_s", [P, T], U8, tag="early_a")
-        tab_w = [held("tab_w%d" % a, [P, T], U32, tag="big%d" % a) for a in range(PASSES)]
+        tab_s = placed("tab_s", [P, T], U8, 20)
         w4_s = held("w4_s", [P, PASSES, H], U8)
         w8_s = held("w8_s", [P, PASSES, H], U8)
         v_s = held("v_s", [P, PASSES, S], U8)
         w1_raw0 = held("w1_raw0", [P, PASSES, 4, P], F32)
-        w1_raw1 = held("w1_raw1", [P, PASSES, 4, P], F32)
-        w1_raw = held("w1_raw", [P, PASSES, 4, 2 * P], F32, tag="w1_raw")
-        w8_c = held("w8_c", [P, PASSES, H], U32)
+        w8_lo = held("w8_lo", [P, PASSES, P], U32)
         w4_c = held("w4_c", [P, PASSES, 2 * H], U8)
-        wgs_sb = held("wgs_sb", [P, S], F32)
-        wgo_sb = held("wgo_sb", [P, P_OUT], F32)
-        w2_raw = held("w2_raw", [P, 4, N], F32)
 
         for plane in (w4_s, w8_s):
             nc.vector.memset(plane[:].rearrange("p a c -> p (a c)").bitcast(I32), 0)
@@ -68,40 +66,29 @@ def tile_list_tote_lane_features_kernel(
         nc.vector.memset(warm[:, 0:1], 0.0)
         nc.scalar.activation(out=warm[:, 1:2], in_=warm[:, 0:1], func=ACT.Sigmoid)
 
-        nc.sync.dma_start(list1[:], offs)
+        for tile, src in ((list1, offs), (list2, offs2), (list3, offs3), (list4, offs4)):
+            nc.sync.dma_start(tile[:], src)
         nc.sync.dma_start(out=tab_s[:].bitcast(I32)[96:128, :], in_=tab_scales.rearrange("a q t -> (a q) t").bitcast(I32))
         tab_words_i = tab_words.rearrange("a p t i -> a p (t i)").bitcast(I32)
-        nc.sync.dma_start(out=tab_w[0][:].bitcast(I32), in_=tab_words_i[0])
+        tab_w0 = placed("tab_w0", [P, T], U32, 0)
+        nc.sync.dma_start(out=tab_w0[:].bitcast(I32), in_=tab_words_i[0])
         w1_rows = w1.rearrange("(a p j) c -> a p j c", a=PASSES, j=4)
         for a in range(PASSES):
             nc.sync.dma_start(out=w1_raw0[:, a, :, :], in_=w1_rows[a][:, :, 0:P])
         w8_words_i = w8_words.rearrange("a p c i -> p a (c i)").bitcast(I32)
-        nc.sync.dma_start(out=w8_c[:].bitcast(I32)[:, :, 0:P], in_=w8_words_i[:, :, 0:P])
+        nc.sync.dma_start(out=w8_lo[:].bitcast(I32), in_=w8_words_i[:, :, 0:P])
         nc.sync.dma_start(out=w4_c[:].bitcast(I32), in_=w4_words.rearrange("a p c -> p a c").bitcast(I32))
-        nc.sync.dma_start(out=tab_w[1][:].bitcast(I32), in_=tab_words_i[1])
-        for q in range(4):
-            nc.gpsimd.dma_start(
-                out=w4_s[:].bitcast(I32)[32 * q : 32 * q + 4, :, :],
-                in_=w4_scales.rearrange("a r c -> r a c").bitcast(I32)[4 * q : 4 * q + 4, :, :],
-            )
-        for q in range(4):
-            nc.scalar.dma_start(
-                out=w8_s[:].bitcast(I32)[32 * q : 32 * q + 4, :, :],
-                in_=w8_scales.rearrange("a r c -> r a c").bitcast(I32)[4 * q : 4 * q + 4, :, :],
-            )
-        for a in range(PASSES):
-            nc.sync.dma_start(out=w1_raw1[:, a, :, :], in_=w1_rows[a][:, :, P : 2 * P])
-        nc.sync.dma_start(out=w8_c[:].bitcast(I32)[:, :, P:H], in_=w8_words_i[:, :, P:H])
-        nc.sync.dma_start(out=wgs_sb[:], in_=wgs)
-        nc.sync.dma_start(list2[:], offs2)
-        for a in range(PASSES):
-            nc.sync.dma_start(out=w1_raw[:, a, :, :], in_=w1_rows[a][:, :, 2 * P : H])
-        nc.sync.dma_start(out=w2_raw[:], in_=w2.rearrange("(p j) n -> p j n", j=4))
+        for plane, scales in ((w8_s, w8_scales), (w4_s, w4_scales)):
+            for q in range(4):
+                nc.gpsimd.dma_start(
+                    out=plane[:].bitcast(I32)[32 * q : 32 * q + 4, :, :],
+                    in_=scales.rearrange("a r c -> r a c").bitcast(I32)[4 * q : 4 * q + 4, :, :],
+                )
 
         ident = held("ident", [P, P], F32)
         make_identity(nc, ident[:])
 
-        picked_s = held("picked_s", [P, S], U8, tag="early_b")
+        picked_s = held("picked_s", [P, S], U8, tag="page0")
         nc.vector.tensor_copy(picked_s[:], tab_s[:].indirect(list1[:]))
         for a in range(PASSES):
             for q in range(4):
@@ -109,16 +96,26 @@ def tile_list_tote_lane_features_kernel(
                     out=v_s[:].bitcast(I32)[32 * q : 32 * q + 4, a, :],
                     in_=picked_s[:].bitcast(I32)[96 + 16 * a + 4 * q : 96 + 16 * a + 4 * q + 4, :],
                 )
+        tab_w1 = placed("tab_w1", [P, T], U32, 20)
+        nc.sync.dma_start(out=tab_w1[:].bitcast(I32), in_=tab_words_i[1])
         v_w = [held("v_w%d" % a, [P, S], U32) for a in range(PASSES)]
-        nc.vector.tensor_copy(v_w[0][:], tab_w[0][:].indirect(list1[:]))
+        nc.vector.tensor_copy(v_w[0][:], tab_w0[:].indirect(list1[:]))
+
+        w1_raw1 = placed("w1_raw1", [P, PASSES, 4, P], F32, 12)
+        w8_hi = placed("w8_hi", [P, PASSES, H - P], U32, 4)
+        wgs_sb = placed("wgs_sb", [P, S], F32, 0)
+        for a in range(PASSES):
+            nc.sync.dma_start(out=w1_raw1[:, a, :, :], in_=w1_rows[a][:, :, P : 2 * P])
+        nc.sync.dma_start(out=wgs_sb[:], in_=wgs)
+        nc.sync.dma_start(out=w8_hi[:].bitcast(I32), in_=w8_words_i[:, :, P:H])
 
         w1_g = held("w1_g", [P, SLICES, PASSES, P, 4], BF16)
         w1_c = held("w1_c", [P, SLICES, PASSES, P], U32)
         w1_s = held("w1_s", [P, SLICES, PASSES, P], U8)
 
-        def round_w1(s):
+        def round_w1(s, source, c0):
             for a in range(PASSES):
-                raw = (w1_raw0, w1_raw1)[s][:, a, :, :] if s < 2 else w1_raw[:, a, :, (s - 2) * P : (s - 1) * P]
+                raw = source[:, a, :, c0 : c0 + P]
                 nc.scalar.copy(
                     out=w1_g[:, s, a, :, :].rearrange("p (c i) j -> p c j i", i=4),
                     in_=raw.rearrange("p j (c i) -> p c j i", i=4),
@@ -131,10 +128,11 @@ def tile_list_tote_lane_features_kernel(
                 in_=w1_g[:, s0:s1, :, :, :].rearrange("p s a c j -> p (s a c j)"),
             )
 
-        round_w1(0)
+        round_w1(0, w1_raw0, 0)
         quantise_w1(0, 1)
 
-        pages = [held("page%d" % s, [P, T2], F32) for s in range(SLICES)]
+        page_tags = ("page0", "w1_raw0", "page2", "page3")
+        pages = [held("page%d" % s, [P, T2], F32, tag=page_tags[s]) for s in range(SLICES)]
         for s in range(2):
             nc.vector.memset(pages[s][:], 0.0)
         for s in range(2, SLICES):
@@ -143,22 +141,13 @@ def tile_list_tote_lane_features_kernel(
 
         cols16 = CHUNK // 16
         for c in range(CHUNKS):
-            nc.vector.tensor_copy(v_w[1][:, c * CHUNK : (c + 1) * CHUNK], tab_w[1][:].indirect(list1[:, c * cols16 : (c + 1) * cols16]))
+            nc.vector.tensor_copy(v_w[1][:, c * CHUNK : (c + 1) * CHUNK], tab_w1[:].indirect(list1[:, c * cols16 : (c + 1) * cols16]))
 
-        lanes = [
-            held("lanes0", [P, T2], F32, tag="early_a"),
-            held("lanes1", [P, T2], F32, tag="early_b"),
-        ]
-        for n in range(2):
-            for q in range(4):
-                nc.gpsimd.memset(lanes[n][:, q * BANK : (q + 1) * BANK], 0.0)
-
-        buf_sb = [held("buf_sb%d" % a, [P, 2, T2], F32, tag="big%d" % a) for a in range(2)]
-        for s in range(SLICES):
-            nc.sync.dma_start(out=buf_sb[s // 2][:, s % 2, :], in_=buf[s * P : (s + 1) * P, :])
-        nc.sync.dma_start(list3[:], offs3)
-        nc.sync.dma_start(list4[:], offs4)
-        nc.sync.dma_start(out=wgo_sb[:], in_=wgo)
+        w1_raw = placed("w1_raw", [P, PASSES, 4, 2 * P], F32, 20)
+        w2_raw = placed("w2_raw", [P, 4, N], F32, 28)
+        for a in range(PASSES):
+            nc.sync.dma_start(out=w1_raw[:, a, :, :], in_=w1_rows[a][:, :, 2 * P : H])
+        nc.sync.dma_start(out=w2_raw[:], in_=w2.rearrange("(p j) n -> p j n", j=4))
 
         ready = {}
 
@@ -171,7 +160,7 @@ def tile_list_tote_lane_features_kernel(
             gate_ps = bank(1, "gate_ps")
             products = (
                 (hold_ps, lambda a: (w1_c[:, s, a, :].bitcast(FP8X4), w1_s[:, s, a, :])),
-                (move_ps, lambda a: (w8_c[:, a, rows].bitcast(FP8X4), w8_s[:, a, rows])),
+                (move_ps, lambda a: ((w8_lo[:, a, :] if s == 0 else w8_hi[:, a, (s - 1) * P : s * P]).bitcast(FP8X4), w8_s[:, a, rows])),
                 (gate_ps, lambda a: (w4_c[:, a, 2 * s * P : 2 * (s + 1) * P].bitcast(FP4X4), w4_s[:, a, rows])),
             )
             for a in range(PASSES):
@@ -208,12 +197,14 @@ def tile_list_tote_lane_features_kernel(
         sums = {}
 
         def turn_buf(s):
+            state = placed("state%d" % s, [P, T2], F32, (12, 20, 28, 12)[s])
+            nc.sync.dma_start(out=state[:], in_=buf[s * P : (s + 1) * P, :])
             for q in range(QUARTERS):
                 acc = bank(4 + q, "z_ps")
                 sums[q] = acc
                 for b in range(4):
                     c0 = q * BANK + b * P
-                    nc.tensor.matmul(out=acc[:, b * P : (b + 1) * P], lhsT=buf_sb[s // 2][:, s % 2, c0 : c0 + P], rhs=ident[:],
+                    nc.tensor.matmul(out=acc[:, b * P : (b + 1) * P], lhsT=state[:, c0 : c0 + P], rhs=ident[:],
                                      is_transpose=True, start=(b == 0), stop=False)
 
         def turn_page(s, q, copy):
@@ -231,12 +222,12 @@ def tile_list_tote_lane_features_kernel(
         w2_c = held("w2_c", [P, N], U32)
         w2_s = held("w2_s", [P, N], U8)
 
-        round_w1(1)
+        round_w1(1, w1_raw1, 0)
         quantise_w1(1, 2)
         first_stage(0)
         first_stage(1)
-        round_w1(2)
-        round_w1(3)
+        round_w1(2, w1_raw, 0)
+        round_w1(3, w1_raw, P)
         for k in range(SLICES * CHUNKS):
             s, c = divmod(k, CHUNKS)
             place(k)
@@ -259,22 +250,27 @@ def tile_list_tote_lane_features_kernel(
                 for q in range(QUARTERS):
                     turn_page(s, q, nc.scalar.copy)
 
+        wgo_sb = placed("wgo_sb", [P, P_OUT], F32, 20)
+        nc.sync.dma_start(out=wgo_sb[:], in_=wgo)
+        lanes = [placed("lanes0", [P, T2], F32, 0)]
+        nc.gpsimd.memset(lanes[0][:], 0.0)
+
         z_c = held("z_c", [P, T2], U32, tag="z_c")
         z_s = held("z_s", [P, T2], U8)
         ys = [
-            held("y0", [P, T2], F32, tag="big0"),
-            held("y1", [P, T2], F32, tag="big1"),
-            held("y2", [P, T2], F32, tag="w1_raw"),
+            placed("y0", [P, T2], F32, 12),
+            placed("y1", [P, T2], F32, 28),
+            held("y2", [P, T2], F32),
         ]
 
-        def second_product(n, q, b, copy):
-            cols = slice(q * BANK, (q + 1) * BANK)
+        def second_product(n, c0, width, b, copy):
+            cols = slice(c0, c0 + width)
             y_ps = bank(b, "y_ps")
             nc.tensor.matmul_mx(
-                out=y_ps[:], lhsT=w2_c[:, n * P : (n + 1) * P].bitcast(FP8X4), lhsT_scale=w2_s[:, n * P : (n + 1) * P],
+                out=y_ps[:, 0:width], lhsT=w2_c[:, n * P : (n + 1) * P].bitcast(FP8X4), lhsT_scale=w2_s[:, n * P : (n + 1) * P],
                 rhs=z_c[:, cols].bitcast(FP8X4), rhs_scale=z_s[:, cols], start=True, stop=True,
             )
-            copy(out=ys[n][:, cols], in_=y_ps[:])
+            copy(out=ys[n][:, cols], in_=y_ps[:, 0:width])
 
         for q in range(QUARTERS):
             turn_page(SLICES - 1, q, nc.vector.tensor_copy if q % 2 == 0 else nc.scalar.copy)
@@ -287,18 +283,22 @@ def tile_list_tote_lane_features_kernel(
                         nc.tensor.transpose(back[:, (2 * b + u) * P : (2 * b + u + 1) * P],
                                             words[:, 2 * half + b, u * P : (u + 1) * P], ident[:])
                 z_g = ring.tile([P, 2 * P * 4], BF16, name="z_g", align_bytes=64)
-                copy = nc.vector.tensor_copy if (2 * q + half) % 3 == 2 else nc.scalar.copy
+                copy = nc.vector.tensor_copy if half == 1 else nc.scalar.copy
                 copy(out=z_g[:].bitcast(F32).rearrange("p (b c u) -> p b c u", b=2, u=2),
                      in_=back[:].rearrange("p (b u c) -> p b c u", b=2, u=2))
                 c0 = q * BANK + half * 2 * P
                 nc.vector.quantize_mx(out=z_c[:, c0 : c0 + 2 * P].bitcast(FP8X4), scales=z_s[:, c0 : c0 + 2 * P], in_=z_g[:])
-            second_product(0, q, 4 + q, nc.vector.tensor_copy if q == QUARTERS - 1 else nc.scalar.copy)
+        for q in range(QUARTERS - 1):
+            second_product(0, q * BANK, BANK, 4 + q, nc.scalar.copy)
+        second_product(0, T2 - BANK, BANK // 2, 7, nc.scalar.copy)
+        second_product(0, T2 - BANK // 2, BANK // 2, 0, nc.vector.tensor_copy)
         for n in range(1, N // P):
             for q in range(QUARTERS):
-                second_product(n, q, (4 * (n - 1) + q) % 8, nc.scalar.copy)
+                second_product(n, q * BANK, BANK, (4 * (n - 1) + q + 1) % 8, nc.scalar.copy)
 
-        lanes.append(held("lanes2", [P, T2], F32, tag="z_c"))
-        nc.gpsimd.memset(lanes[2][:], 0.0)
+        for n, tag in ((1, "w2_c"), (2, "z_c")):
+            lanes.append(held("lanes%d" % n, [P, T2], F32, tag=tag))
+            nc.gpsimd.memset(lanes[n][:], 0.0)
 
         picked = []
 

@@ -18,18 +18,36 @@ ALU = mybir.AluOpType
 ACT = mybir.ActivationFunctionType
 
 P = 128
-PASSES = K // 512
+PACK = 4
+PASSES = K // (P * PACK)
+QUADRANTS = 4
 SLICES = H // P
-CHUNK = 512
-CHUNKS = S // CHUNK
 BANK = 512
-USE_POOL = True
+HALF = BANK
+HALVES = S // HALF
+HALF_COLS = HALF // 16
+CHUNKS = SLICES * HALVES
+QUARTERS = T2 // BANK
+SCALE_ROW0 = P - PASSES * 16
+
+HOLD_BANK_FIRST = 0
+GATE_BANKS = (1, 7)
+MOVE_BANKS = (2, 3, 4)
+HOLD_BANKS_SECOND = (5, 6)
+
+AT_WORDS = (0, 20)
+AT_WGS, AT_W8, AT_W4 = 0, 4, 8
+AT_LOW = 12
+AT_MID = 20
+AT_HIGH = 28
 
 
 def tile_list_tote_lane_features_kernel(
     tc, tab_words, tab_scales, offs, w4_words, w4_scales, w8_words, w8_scales, w1, offs2, wgs, buf, w2, offs3, offs4, wgo, out
 ):
     nc = tc.nc
+    early_banks = (HOLD_BANK_FIRST,) + GATE_BANKS + MOVE_BANKS[2:]
+    late_banks = (HOLD_BANKS_SECOND[0], MOVE_BANKS[0], MOVE_BANKS[1], HOLD_BANKS_SECOND[1])
     with ExitStack() as ctx:
         keep = ctx.enter_context(tc.tile_pool(name="keep", bufs=1))
         ring = ctx.enter_context(tc.tile_pool(name="ring", bufs=4))
@@ -42,84 +60,85 @@ def tile_list_tote_lane_features_kernel(
         def placed(name, shape, dtype, kib):
             return arena.tile(shape, dtype, name=name, align_bytes=64, offset=kib * 1024)
 
-        def bank(b, name):
-            return psum.tile([P, BANK], F32, name=name, tag="bank%d" % b)
+        def bank(number, name):
+            return psum.tile([P, BANK], F32, name=name, tag="bank%d" % number)
+
+        def round_and_interleave(grouped, raw):
+            nc.scalar.copy(out=grouped.rearrange("p (c i) j -> p c j i", i=4), in_=raw.rearrange("p j (c i) -> p c j i", i=4))
 
         list1 = held("list1", [P, S // 16], U16)
         list2 = held("list2", [P, S // 16], U16)
         list3 = held("list3", [P, P_OUT // 16], U16)
         list4 = held("list4", [P, P_OUT // 16], U16)
-        tab_s = placed("tab_s", [P, T], U8, 20)
+        tab_s = placed("tab_s", [P, T], U8, AT_MID)
         w4_s = held("w4_s", [P, PASSES, H], U8)
         w8_s = held("w8_s", [P, PASSES, H], U8)
         v_s = held("v_s", [P, PASSES, S], U8)
-        w1_raw0 = held("w1_raw0", [P, PASSES, 4, P], F32)
+        w1_raw0 = held("w1_raw0", [P, PASSES, PACK, P], F32)
         w8_lo = held("w8_lo", [P, PASSES, P], U32)
-        w4_c = held("w4_c", [P, PASSES, 2 * H], U8)
+        w4_lo = held("w4_lo", [P, PASSES, 2 * P], U8)
 
         for plane in (w4_s, w8_s):
             nc.vector.memset(plane[:].rearrange("p a c -> p (a c)").bitcast(I32), 0)
-        nc.vector.memset(tab_s[:].bitcast(I32)[0:96, :], 0)
+        nc.vector.memset(tab_s[:].bitcast(I32)[0:SCALE_ROW0, :], 0)
         nc.vector.memset(v_s[:].rearrange("p a c -> p (a c)").bitcast(I32), 0)
 
         warm = held("warm", [P, 2], F32)
         nc.vector.memset(warm[:, 0:1], 0.0)
         nc.scalar.activation(out=warm[:, 1:2], in_=warm[:, 0:1], func=ACT.Sigmoid)
 
-        for tile, src in ((list1, offs), (list2, offs2), (list3, offs3), (list4, offs4)):
-            nc.sync.dma_start(tile[:], src)
-        nc.sync.dma_start(out=tab_s[:].bitcast(I32)[96:128, :], in_=tab_scales.rearrange("a q t -> (a q) t").bitcast(I32))
-        tab_words_i = tab_words.rearrange("a p t i -> a p (t i)").bitcast(I32)
-        tab_w0 = placed("tab_w0", [P, T], U32, 0)
-        nc.sync.dma_start(out=tab_w0[:].bitcast(I32), in_=tab_words_i[0])
-        w1_rows = w1.rearrange("(a p j) c -> a p j c", a=PASSES, j=4)
+        for list_tile, list_input in ((list1, offs), (list2, offs2), (list3, offs3), (list4, offs4)):
+            nc.sync.dma_start(list_tile[:], list_input)
+        nc.sync.dma_start(out=tab_s[:].bitcast(I32)[SCALE_ROW0:P, :], in_=tab_scales.rearrange("a g t -> (a g) t").bitcast(I32))
+        tab_words_i = tab_words.rearrange("a p t j -> a p (t j)").bitcast(I32)
+        w1_rows = w1.rearrange("(a p j) c -> a p j c", a=PASSES, j=PACK)
         for a in range(PASSES):
             nc.sync.dma_start(out=w1_raw0[:, a, :, :], in_=w1_rows[a][:, :, 0:P])
-        w8_words_i = w8_words.rearrange("a p c i -> p a (c i)").bitcast(I32)
+        w8_words_i = w8_words.rearrange("a p c j -> p a (c j)").bitcast(I32)
         nc.sync.dma_start(out=w8_lo[:].bitcast(I32), in_=w8_words_i[:, :, 0:P])
-        nc.sync.dma_start(out=w4_c[:].bitcast(I32), in_=w4_words.rearrange("a p c -> p a c").bitcast(I32))
-        for plane, scales in ((w8_s, w8_scales), (w4_s, w4_scales)):
-            for q in range(4):
-                nc.gpsimd.dma_start(
-                    out=plane[:].bitcast(I32)[32 * q : 32 * q + 4, :, :],
-                    in_=scales.rearrange("a r c -> r a c").bitcast(I32)[4 * q : 4 * q + 4, :, :],
+        w4_words_i = w4_words.rearrange("a p c -> p a c").bitcast(I32)
+        nc.sync.dma_start(out=w4_lo[:].bitcast(I32), in_=w4_words_i[:, :, 0 : P // 2])
+        tab_w0 = placed("tab_w0", [P, T], U32, AT_WORDS[0])
+        nc.sync.dma_start(out=tab_w0[:].bitcast(I32), in_=tab_words_i[0])
+        for plane, scale_input, queue in ((w8_s, w8_scales, nc.gpsimd), (w4_s, w4_scales, nc.scalar)):
+            for Q in range(QUADRANTS):
+                queue.dma_start(
+                    out=plane[:].bitcast(I32)[32 * Q : 32 * Q + 4, :, :],
+                    in_=scale_input.rearrange("a g c -> g a c").bitcast(I32)[4 * Q : 4 * Q + 4, :, :],
                 )
 
         ident = held("ident", [P, P], F32)
         make_identity(nc, ident[:])
 
-        picked_s = held("picked_s", [P, S], U8, tag="page0")
+        picked_s = held("picked_s", [P, S], U8)
         nc.vector.tensor_copy(picked_s[:], tab_s[:].indirect(list1[:]))
         for a in range(PASSES):
-            for q in range(4):
-                nc.scalar.dma_start(
-                    out=v_s[:].bitcast(I32)[32 * q : 32 * q + 4, a, :],
-                    in_=picked_s[:].bitcast(I32)[96 + 16 * a + 4 * q : 96 + 16 * a + 4 * q + 4, :],
-                )
-        tab_w1 = placed("tab_w1", [P, T], U32, 20)
+            for Q in range(QUADRANTS):
+                row = SCALE_ROW0 + 16 * a + 4 * Q
+                queue = nc.gpsimd if (a, Q) == (PASSES - 1, QUADRANTS - 1) else nc.scalar
+                queue.dma_start(out=v_s[:].bitcast(I32)[32 * Q : 32 * Q + 4, a, :], in_=picked_s[:].bitcast(I32)[row : row + 4, :])
+        tab_w1 = placed("tab_w1", [P, T], U32, AT_WORDS[1])
         nc.sync.dma_start(out=tab_w1[:].bitcast(I32), in_=tab_words_i[1])
         v_w = [held("v_w%d" % a, [P, S], U32) for a in range(PASSES)]
         nc.vector.tensor_copy(v_w[0][:], tab_w0[:].indirect(list1[:]))
 
-        w1_raw1 = placed("w1_raw1", [P, PASSES, 4, P], F32, 12)
-        w8_hi = placed("w8_hi", [P, PASSES, H - P], U32, 4)
-        wgs_sb = placed("wgs_sb", [P, S], F32, 0)
+        w1_raw1 = placed("w1_raw1", [P, PASSES, PACK, P], F32, AT_LOW)
+        w8_hi = placed("w8_hi", [P, PASSES, H - P], U32, AT_W8)
+        wgs_sb = placed("wgs_sb", [P, S], F32, AT_WGS)
         for a in range(PASSES):
             nc.sync.dma_start(out=w1_raw1[:, a, :, :], in_=w1_rows[a][:, :, P : 2 * P])
         nc.sync.dma_start(out=wgs_sb[:], in_=wgs)
         nc.sync.dma_start(out=w8_hi[:].bitcast(I32), in_=w8_words_i[:, :, P:H])
+        w4_hi = placed("w4_hi", [P, PASSES, 2 * (H - P)], U8, AT_W4)
+        nc.sync.dma_start(out=w4_hi[:].bitcast(I32), in_=w4_words_i[:, :, P // 2 : H // 2])
 
-        w1_g = held("w1_g", [P, SLICES, PASSES, P, 4], BF16)
+        w1_g = held("w1_g", [P, SLICES, PASSES, P, PACK], BF16)
         w1_c = held("w1_c", [P, SLICES, PASSES, P], U32)
         w1_s = held("w1_s", [P, SLICES, PASSES, P], U8)
 
-        def round_w1(s, source, c0):
+        def round_w1(s, raw, col0):
             for a in range(PASSES):
-                raw = source[:, a, :, c0 : c0 + P]
-                nc.scalar.copy(
-                    out=w1_g[:, s, a, :, :].rearrange("p (c i) j -> p c j i", i=4),
-                    in_=raw.rearrange("p j (c i) -> p c j i", i=4),
-                )
+                round_and_interleave(w1_g[:, s, a, :, :], raw[:, a, :, col0 : col0 + P])
 
         def quantise_w1(s0, s1):
             nc.vector.quantize_mx(
@@ -131,170 +150,160 @@ def tile_list_tote_lane_features_kernel(
         round_w1(0, w1_raw0, 0)
         quantise_w1(0, 1)
 
-        page_tags = ("page0", "w1_raw0", "page2", "page3")
-        pages = [held("page%d" % s, [P, T2], F32, tag=page_tags[s]) for s in range(SLICES)]
-        for s in range(2):
-            nc.vector.memset(pages[s][:], 0.0)
-        for s in range(2, SLICES):
-            for q in range(4):
+        pages = [held("page%d" % s, [P, T2], F32, tag="w1_raw0" if s == 0 else None) for s in range(SLICES)]
+        nc.vector.memset(pages[0][:], 0.0)
+        for s in range(1, SLICES):
+            for q in range(QUARTERS):
                 nc.gpsimd.memset(pages[s][:, q * BANK : (q + 1) * BANK], 0.0)
 
-        cols16 = CHUNK // 16
-        for c in range(CHUNKS):
-            nc.vector.tensor_copy(v_w[1][:, c * CHUNK : (c + 1) * CHUNK], tab_w1[:].indirect(list1[:, c * cols16 : (c + 1) * cols16]))
+        for half in range(HALVES):
+            offsets = list1[:, half * HALF_COLS : (half + 1) * HALF_COLS]
+            nc.vector.tensor_copy(v_w[1][:, half * HALF : (half + 1) * HALF], tab_w1[:].indirect(offsets))
 
-        w1_raw = placed("w1_raw", [P, PASSES, 4, 2 * P], F32, 20)
-        w2_raw = placed("w2_raw", [P, 4, N], F32, 28)
+        w1_raw23 = placed("w1_raw23", [P, PASSES, PACK, 2 * P], F32, AT_MID)
+        w2_raw = placed("w2_raw", [P, PACK, N], F32, AT_HIGH)
         for a in range(PASSES):
-            nc.sync.dma_start(out=w1_raw[:, a, :, :], in_=w1_rows[a][:, :, 2 * P : H])
-        nc.sync.dma_start(out=w2_raw[:], in_=w2.rearrange("(p j) n -> p j n", j=4))
+            nc.sync.dma_start(out=w1_raw23[:, a, :, :], in_=w1_rows[a][:, :, 2 * P : H])
+        nc.sync.dma_start(out=w2_raw[:], in_=w2.rearrange("(p j) n -> p j n", j=PACK))
 
-        ready = {}
+        weighted = {}
 
         def first_stage(k):
-            s, c = divmod(k, CHUNKS)
-            cols = slice(c * CHUNK, (c + 1) * CHUNK)
+            s, half = divmod(k, HALVES)
+            entries = slice(half * HALF, (half + 1) * HALF)
             rows = slice(s * P, (s + 1) * P)
-            hold_ps = bank(0, "hold_ps")
-            move_ps = bank(2 + k % 2, "move_ps")
-            gate_ps = bank(1, "gate_ps")
-            products = (
-                (hold_ps, lambda a: (w1_c[:, s, a, :].bitcast(FP8X4), w1_s[:, s, a, :])),
-                (move_ps, lambda a: ((w8_lo[:, a, :] if s == 0 else w8_hi[:, a, (s - 1) * P : s * P]).bitcast(FP8X4), w8_s[:, a, rows])),
-                (gate_ps, lambda a: (w4_c[:, a, 2 * s * P : 2 * (s + 1) * P].bitcast(FP4X4), w4_s[:, a, rows])),
-            )
+            hold_ps = bank(HOLD_BANK_FIRST if half == 0 else HOLD_BANKS_SECOND[s % len(HOLD_BANKS_SECOND)], "hold_ps")
+            move_ps = bank(MOVE_BANKS[k % len(MOVE_BANKS)], "move_ps")
+            gate_ps = bank(GATE_BANKS[half], "gate_ps")
             for a in range(PASSES):
-                for acc, weight in products:
-                    codes, scales = weight(a)
+                w4_codes = w4_lo[:, a, :] if s == 0 else w4_hi[:, a, 2 * (s - 1) * P : 2 * s * P]
+                w8_codes = w8_lo[:, a, :] if s == 0 else w8_hi[:, a, (s - 1) * P : s * P]
+                gate_pass = (gate_ps, w4_codes.bitcast(FP4X4), w4_s[:, a, rows])
+                hold_pass = (hold_ps, w1_c[:, s, a, :].bitcast(FP8X4), w1_s[:, s, a, :])
+                move_pass = (move_ps, w8_codes.bitcast(FP8X4), w8_s[:, a, rows])
+                for acc, codes, scales in (hold_pass, move_pass, gate_pass) if half == 0 else (gate_pass, hold_pass, move_pass):
                     nc.tensor.matmul_mx(
                         out=acc[:], lhsT=codes, lhsT_scale=scales,
-                        rhs=v_w[a][:, cols].bitcast(FP8X4), rhs_scale=v_s[:, a, cols],
+                        rhs=v_w[a][:, entries].bitcast(FP8X4), rhs_scale=v_s[:, a, entries],
                         start=(a == 0), stop=(a == PASSES - 1),
                     )
-            hold = ring.tile([P, CHUNK], F32, name="hold")
-            gate = ring.tile([P, CHUNK], F32, name="gate")
-            h = ring.tile([P, CHUNK], F32, name="h")
-            nc.scalar.copy(out=hold[:], in_=hold_ps[:])
-            nc.scalar.activation(out=gate[:], in_=gate_ps[:], func=ACT.Sigmoid)
-            nc.vector.tensor_tensor(h[:], move_ps[:], hold[:], ALU.subtract)
-            eng = nc.gpsimd if (USE_POOL and k > 0) else nc.vector
-            eng.tensor_tensor(h[:], h[:], gate[:], ALU.mult)
-            eng.tensor_tensor(h[:], h[:], hold[:], ALU.add)
-            if USE_POOL:
-                eng.tensor_tensor(h[:], h[:], wgs_sb[:, cols], ALU.mult)
-            ready[k] = h
-
-        def place(k):
-            s, c = divmod(k, CHUNKS)
-            window = pages[s][:].indirect(list2[:, c * cols16 : (c + 1) * cols16])
-            if USE_POOL:
-                nc.vector.tensor_copy(window, ready[k][:])
+            hold_term = ring.tile([P, HALF], F32, name="hold_term", bufs=CHUNKS)
+            gate = ring.tile([P, HALF], F32, name="gate", bufs=CHUNKS)
+            if k < CHUNKS - 1:
+                h = ring.tile([P, HALF], F32, name="h")
             else:
-                nc.vector.tensor_tensor(window, ready[k][:], wgs_sb[:, c * CHUNK : (c + 1) * CHUNK], ALU.mult)
+                h = held("h_last", [P, HALF], F32, tag="w2_c")
+            from_sbuf = nc.gpsimd if k > 0 else nc.vector
+            if half == 0:
+                nc.scalar.copy(out=hold_term[:], in_=hold_ps[:])
+                nc.scalar.activation(out=gate[:], in_=gate_ps[:], func=ACT.Sigmoid)
+                nc.vector.tensor_tensor(h[:], move_ps[:], hold_term[:], ALU.subtract)
+                from_sbuf.tensor_tensor(h[:], h[:], gate[:], ALU.mult)
+            else:
+                nc.scalar.activation(out=gate[:], in_=gate_ps[:], func=ACT.Sigmoid)
+                nc.scalar.activation(out=hold_term[:], in_=gate_ps[:], func=ACT.Sigmoid, scale=-1.0)
+                nc.vector.tensor_tensor(h[:], move_ps[:], gate[:], ALU.mult)
+                nc.vector.tensor_tensor(hold_term[:], hold_ps[:], hold_term[:], ALU.mult)
+            from_sbuf.tensor_tensor(h[:], h[:], hold_term[:], ALU.add)
+            from_sbuf.tensor_tensor(h[:], h[:], wgs_sb[:, entries], ALU.mult)
+            weighted[k] = h
 
-        QUARTERS = T2 // BANK
-        z_t = [held("z_t%d" % q, [P, 4, H], BF16) for q in range(QUARTERS)]
-        sums = {}
+        def scatter_to_page(k):
+            s, half = divmod(k, HALVES)
+            nc.vector.tensor_copy(pages[s][:].indirect(list2[:, half * HALF_COLS : (half + 1) * HALF_COLS]), weighted[k][:])
+
+        z_t = [held("z_t%d" % q, [P, BANK // P, H], BF16) for q in range(QUARTERS)]
+        open_sums = {}
 
         def turn_buf(s):
-            state = placed("state%d" % s, [P, T2], F32, (12, 20, 28, 12)[s])
+            state = placed("state%d" % s, [P, T2], F32, (AT_LOW, AT_MID, AT_HIGH)[s % 3])
             nc.sync.dma_start(out=state[:], in_=buf[s * P : (s + 1) * P, :])
             for q in range(QUARTERS):
-                acc = bank(4 + q, "z_ps")
-                sums[q] = acc
-                for b in range(4):
-                    c0 = q * BANK + b * P
-                    nc.tensor.matmul(out=acc[:, b * P : (b + 1) * P], lhsT=state[:, c0 : c0 + P], rhs=ident[:],
+                acc = bank((early_banks if s < SLICES - 1 else late_banks)[q], "z_ps")
+                open_sums[q] = acc
+                for b in range(BANK // P):
+                    col0 = q * BANK + b * P
+                    nc.tensor.matmul(out=acc[:, b * P : (b + 1) * P], lhsT=state[:, col0 : col0 + P], rhs=ident[:],
                                      is_transpose=True, start=(b == 0), stop=False)
 
         def turn_page(s, q, copy):
-            acc = sums[q]
-            for b in range(4):
-                c0 = q * BANK + b * P
-                nc.tensor.matmul(out=acc[:, b * P : (b + 1) * P], lhsT=pages[s][:, c0 : c0 + P], rhs=ident[:],
-                                 is_transpose=True, start=False, stop=(b == 3))
+            acc = open_sums[q]
+            for b in range(BANK // P):
+                col0 = q * BANK + b * P
+                nc.tensor.matmul(out=acc[:, b * P : (b + 1) * P], lhsT=pages[s][:, col0 : col0 + P], rhs=ident[:],
+                                 is_transpose=True, start=False, stop=(b == BANK // P - 1))
             copy(
-                out=z_t[q][:].rearrange("c b (u p e) -> c b u p e", u=2, e=2)[:, :, :, 32 * s : 32 * (s + 1), :],
-                in_=acc[:].rearrange("c (b p u e) -> c b u p e", b=4, u=2, e=2),
+                out=z_t[q][:].rearrange("t b (u p e) -> t b u p e", u=2, e=2)[:, :, :, 32 * s : 32 * (s + 1), :],
+                in_=acc[:].rearrange("t (b p u e) -> t b u p e", b=BANK // P, u=2, e=2),
             )
 
-        w2_g = held("w2_g", [P, N, 4], BF16)
-        w2_c = held("w2_c", [P, N], U32)
-        w2_s = held("w2_s", [P, N], U8)
+        w2_g = held("w2_g", [P, N, PACK], BF16)
 
         round_w1(1, w1_raw1, 0)
         quantise_w1(1, 2)
         first_stage(0)
         first_stage(1)
-        round_w1(2, w1_raw, 0)
-        round_w1(3, w1_raw, P)
-        for k in range(SLICES * CHUNKS):
-            s, c = divmod(k, CHUNKS)
-            place(k)
-            if k == 0:
-                quantise_w1(2, 4)
-            if k == 1:
-                nc.scalar.copy(
-                    out=w2_g[:].rearrange("p (c i) j -> p c j i", i=4),
-                    in_=w2_raw[:].rearrange("p j (c i) -> p c j i", i=4),
-                )
-            if k == 2:
-                for n0, n1 in ((0, 256), (256, N)):
-                    nc.vector.quantize_mx(out=w2_c[:, n0:n1].bitcast(FP8X4), scales=w2_s[:, n0:n1],
-                                          in_=w2_g[:, n0:n1, :].rearrange("p c j -> p (c j)"))
-            if k + 2 < SLICES * CHUNKS:
-                first_stage(k + 2)
-        for s in range(SLICES):
+        round_w1(2, w1_raw23, 0)
+        round_w1(3, w1_raw23, P)
+        scatter_to_page(0)
+        quantise_w1(2, SLICES)
+        first_stage(2)
+        scatter_to_page(1)
+        round_and_interleave(w2_g[:], w2_raw[:])
+        for k in range(2, CHUNKS):
+            if k + 1 < CHUNKS:
+                first_stage(k + 1)
+            scatter_to_page(k)
+        for s in range(SLICES - 1):
             turn_buf(s)
-            if s < SLICES - 1:
-                for q in range(QUARTERS):
-                    turn_page(s, q, nc.scalar.copy)
+            for q in range(QUARTERS):
+                turn_page(s, q, nc.scalar.copy)
+        turn_buf(SLICES - 1)
 
-        wgo_sb = placed("wgo_sb", [P, P_OUT], F32, 20)
+        wgo_sb = placed("wgo_sb", [P, P_OUT], F32, AT_MID)
         nc.sync.dma_start(out=wgo_sb[:], in_=wgo)
-        lanes = [placed("lanes0", [P, T2], F32, 0)]
+        lanes = [placed("lanes0", [P, T2], F32, AT_WGS)]
         nc.gpsimd.memset(lanes[0][:], 0.0)
 
-        z_c = held("z_c", [P, T2], U32, tag="z_c")
+        w2_c = held("w2_c", [P, N], U32)
+        w2_s = held("w2_s", [P, N], U8)
+        for n0, n1 in ((0, 2 * P), (2 * P, N)):
+            nc.vector.quantize_mx(out=w2_c[:, n0:n1].bitcast(FP8X4), scales=w2_s[:, n0:n1],
+                                  in_=w2_g[:, n0:n1, :].rearrange("p c j -> p (c j)"))
+        z_c = held("z_c", [P, T2], U32)
         z_s = held("z_s", [P, T2], U8)
-        ys = [
-            placed("y0", [P, T2], F32, 12),
-            placed("y1", [P, T2], F32, 28),
-            held("y2", [P, T2], F32),
-        ]
+        ys = [placed("y0", [P, T2], F32, AT_LOW), placed("y1", [P, T2], F32, AT_HIGH), held("y2", [P, T2], F32)]
 
-        def second_product(n, c0, width, b, copy):
-            cols = slice(c0, c0 + width)
-            y_ps = bank(b, "y_ps")
+        copies = (nc.scalar.copy, nc.vector.tensor_copy)
+        for q in range(QUARTERS):
+            turn_page(SLICES - 1, q, copies[q % 2])
+        piece = 2 * P
+        for turn in range(T2 // piece):
+            q, b0 = divmod(2 * turn, BANK // P)
+            pairs = z_t[q][:].bitcast(F32)
+            back = bank(early_banks[turn % len(early_banks)], "back_ps")
+            for b in range(2):
+                for u in range(2):
+                    nc.tensor.transpose(back[:, (2 * b + u) * P : (2 * b + u + 1) * P], pairs[:, b0 + b, u * P : (u + 1) * P], ident[:])
+            z_g = ring.tile([P, piece * PACK], BF16, name="z_g", align_bytes=64)
+            copies[turn % 2](out=z_g[:].bitcast(F32).rearrange("p (b t u) -> p b t u", b=2, u=2),
+                             in_=back[:].rearrange("p (b u t) -> p b t u", b=2, u=2))
+            cols = slice(turn * piece, (turn + 1) * piece)
+            nc.vector.quantize_mx(out=z_c[:, cols].bitcast(FP8X4), scales=z_s[:, cols], in_=z_g[:])
+
+        y_banks = late_banks + early_banks
+        spans = [(q * BANK, BANK) for q in range(QUARTERS)]
+        first_spans = spans[:-1] + [(T2 - 2 * piece, piece), (T2 - piece, piece)]
+        work = [(n, span) for n in range(N // P) for span in (first_spans if n == 0 else spans)]
+        for count, (n, (col0, width)) in enumerate(work):
+            cols = slice(col0, col0 + width)
+            y_ps = bank(y_banks[count % len(y_banks)], "y_ps")
             nc.tensor.matmul_mx(
                 out=y_ps[:, 0:width], lhsT=w2_c[:, n * P : (n + 1) * P].bitcast(FP8X4), lhsT_scale=w2_s[:, n * P : (n + 1) * P],
                 rhs=z_c[:, cols].bitcast(FP8X4), rhs_scale=z_s[:, cols], start=True, stop=True,
             )
+            copy = nc.vector.tensor_copy if n == 0 and col0 + width == T2 else nc.scalar.copy
             copy(out=ys[n][:, cols], in_=y_ps[:, 0:width])
-
-        for q in range(QUARTERS):
-            turn_page(SLICES - 1, q, nc.vector.tensor_copy if q % 2 == 0 else nc.scalar.copy)
-        for q in range(QUARTERS):
-            words = z_t[q][:].bitcast(F32)
-            for half in range(2):
-                back = bank((2 * q + half) % 4, "back_ps")
-                for b in range(2):
-                    for u in range(2):
-                        nc.tensor.transpose(back[:, (2 * b + u) * P : (2 * b + u + 1) * P],
-                                            words[:, 2 * half + b, u * P : (u + 1) * P], ident[:])
-                z_g = ring.tile([P, 2 * P * 4], BF16, name="z_g", align_bytes=64)
-                copy = nc.vector.tensor_copy if half == 1 else nc.scalar.copy
-                copy(out=z_g[:].bitcast(F32).rearrange("p (b c u) -> p b c u", b=2, u=2),
-                     in_=back[:].rearrange("p (b u c) -> p b c u", b=2, u=2))
-                c0 = q * BANK + half * 2 * P
-                nc.vector.quantize_mx(out=z_c[:, c0 : c0 + 2 * P].bitcast(FP8X4), scales=z_s[:, c0 : c0 + 2 * P], in_=z_g[:])
-        for q in range(QUARTERS - 1):
-            second_product(0, q * BANK, BANK, 4 + q, nc.scalar.copy)
-        second_product(0, T2 - BANK, BANK // 2, 7, nc.scalar.copy)
-        second_product(0, T2 - BANK // 2, BANK // 2, 0, nc.vector.tensor_copy)
-        for n in range(1, N // P):
-            for q in range(QUARTERS):
-                second_product(n, q * BANK, BANK, (4 * (n - 1) + q + 1) % 8, nc.scalar.copy)
 
         for n, tag in ((1, "w2_c"), (2, "z_c")):
             lanes.append(held("lanes%d" % n, [P, T2], F32, tag=tag))
@@ -308,13 +317,9 @@ def tile_list_tote_lane_features_kernel(
             nc.scalar.activation(out=x[:], in_=x[:], func=ACT.Tanh)
             picked.append(x)
 
-        def discharge(n):
+        pick(0)
+        for n in range(N // P):
+            if n + 1 < N // P:
+                pick(n + 1)
             nc.vector.tensor_tensor(lanes[n][:].indirect(list4[:]), picked[n][:], wgo_sb[:], ALU.mult)
             nc.sync.dma_start(out=out[n * P : (n + 1) * P, :], in_=lanes[n][:])
-
-        pick(0)
-        pick(1)
-        discharge(0)
-        pick(2)
-        discharge(1)
-        discharge(2)

@@ -30,10 +30,11 @@ CHUNKS = SLICES * HALVES
 QUARTERS = T2 // BANK
 SCALE_ROW0 = P - PASSES * 16
 
-HOLD_BANK_FIRST = 0
-GATE_BANKS = (1, 7)
-MOVE_BANKS = (2, 3, 4)
-HOLD_BANKS_SECOND = (5, 6)
+WEIGHED_ON_GPSIMD = (6,)
+
+WGS_BANKS = (0, 1)
+PRODUCT_BANKS = (2, 3, 4, 5)
+SUM_BANKS = (6, 7)
 
 AT_WORDS = (0, 20)
 AT_WGS, AT_W8, AT_W4 = 0, 4, 8
@@ -46,8 +47,6 @@ def tile_list_tote_lane_features_kernel(
     tc, tab_words, tab_scales, offs, w4_words, w4_scales, w8_words, w8_scales, w1, offs2, wgs, buf, w2, offs3, offs4, wgo, out
 ):
     nc = tc.nc
-    early_banks = (HOLD_BANK_FIRST,) + GATE_BANKS + MOVE_BANKS[2:]
-    late_banks = (HOLD_BANKS_SECOND[0], MOVE_BANKS[0], MOVE_BANKS[1], HOLD_BANKS_SECOND[1])
     with ExitStack() as ctx:
         keep = ctx.enter_context(tc.tile_pool(name="keep", bufs=1))
         ring = ctx.enter_context(tc.tile_pool(name="ring", bufs=4))
@@ -87,10 +86,8 @@ def tile_list_tote_lane_features_kernel(
         nc.vector.memset(warm[:, 0:1], 0.0)
         nc.scalar.activation(out=warm[:, 1:2], in_=warm[:, 0:1], func=ACT.Sigmoid)
 
-        for list_tile, list_input in ((list1, offs), (list2, offs2), (list3, offs3), (list4, offs4)):
-            nc.sync.dma_start(list_tile[:], list_input)
-        nc.sync.dma_start(out=tab_s[:].bitcast(I32)[SCALE_ROW0:P, :], in_=tab_scales.rearrange("a g t -> (a g) t").bitcast(I32))
-        tab_words_i = tab_words.rearrange("a p t j -> a p (t j)").bitcast(I32)
+        nc.sync.dma_start(list1[:], offs)
+        nc.sync.dma_start(out=tab_s[:].bitcast(I32)[SCALE_ROW0:P, :], in_=tab_scales.bitcast(I32).rearrange("a g t -> g a t"))
         w1_rows = w1.rearrange("(a p j) c -> a p j c", a=PASSES, j=PACK)
         for a in range(PASSES):
             nc.sync.dma_start(out=w1_raw0[:, a, :, :], in_=w1_rows[a][:, :, 0:P])
@@ -98,9 +95,13 @@ def tile_list_tote_lane_features_kernel(
         nc.sync.dma_start(out=w8_lo[:].bitcast(I32), in_=w8_words_i[:, :, 0:P])
         w4_words_i = w4_words.rearrange("a p c -> p a c").bitcast(I32)
         nc.sync.dma_start(out=w4_lo[:].bitcast(I32), in_=w4_words_i[:, :, 0 : P // 2])
+        nc.sync.dma_start(list2[:], offs2)
+        nc.sync.dma_start(list3[:], offs3)
+        tab_words_i = tab_words.rearrange("a p t j -> a p (t j)").bitcast(I32)
         tab_w0 = placed("tab_w0", [P, T], U32, AT_WORDS[0])
         nc.sync.dma_start(out=tab_w0[:].bitcast(I32), in_=tab_words_i[0])
-        for plane, scale_input, queue in ((w8_s, w8_scales, nc.gpsimd), (w4_s, w4_scales, nc.scalar)):
+        nc.sync.dma_start(list4[:], offs4)
+        for plane, scale_input, queue in ((w8_s, w8_scales, nc.gpsimd), (w4_s, w4_scales, nc.gpsimd)):
             for Q in range(QUADRANTS):
                 queue.dma_start(
                     out=plane[:].bitcast(I32)[32 * Q : 32 * Q + 4, :, :],
@@ -112,11 +113,9 @@ def tile_list_tote_lane_features_kernel(
 
         picked_s = held("picked_s", [P, S], U8)
         nc.vector.tensor_copy(picked_s[:], tab_s[:].indirect(list1[:]))
-        for a in range(PASSES):
-            for Q in range(QUADRANTS):
-                row = SCALE_ROW0 + 16 * a + 4 * Q
-                queue = nc.gpsimd if (a, Q) == (PASSES - 1, QUADRANTS - 1) else nc.scalar
-                queue.dma_start(out=v_s[:].bitcast(I32)[32 * Q : 32 * Q + 4, a, :], in_=picked_s[:].bitcast(I32)[row : row + 4, :])
+        for Q in range(QUADRANTS):
+            row = SCALE_ROW0 + 8 * Q
+            nc.scalar.dma_start(out=v_s[:].rearrange("p a c -> p (a c)").bitcast(I32)[32 * Q : 32 * Q + 4, :], in_=picked_s[:].bitcast(I32)[row : row + 8, :])
         tab_w1 = placed("tab_w1", [P, T], U32, AT_WORDS[1])
         nc.sync.dma_start(out=tab_w1[:].bitcast(I32), in_=tab_words_i[1])
         v_w = [held("v_w%d" % a, [P, S], U32) for a in range(PASSES)]
@@ -167,145 +166,191 @@ def tile_list_tote_lane_features_kernel(
         nc.sync.dma_start(out=w2_raw[:], in_=w2.rearrange("(p j) n -> p j n", j=PACK))
 
         weighted = {}
+        wgs_ps = []
 
         def first_stage(k):
             s, half = divmod(k, HALVES)
             entries = slice(half * HALF, (half + 1) * HALF)
             rows = slice(s * P, (s + 1) * P)
-            hold_ps = bank(HOLD_BANK_FIRST if half == 0 else HOLD_BANKS_SECOND[s % len(HOLD_BANKS_SECOND)], "hold_ps")
-            move_ps = bank(MOVE_BANKS[k % len(MOVE_BANKS)], "move_ps")
-            gate_ps = bank(GATE_BANKS[half], "gate_ps")
+            if k == 1:
+                numbers = PRODUCT_BANKS[3:] + SUM_BANKS
+            else:
+                numbers = [PRODUCT_BANKS[(3 * k + i) % len(PRODUCT_BANKS)] for i in range(3)]
+            hold_ps, move_ps, gate_ps = [bank(number, name) for number, name in zip(numbers, ("hold_ps", "move_ps", "gate_ps"))]
+            passes = []
             for a in range(PASSES):
                 w4_codes = w4_lo[:, a, :] if s == 0 else w4_hi[:, a, 2 * (s - 1) * P : 2 * s * P]
                 w8_codes = w8_lo[:, a, :] if s == 0 else w8_hi[:, a, (s - 1) * P : s * P]
-                gate_pass = (gate_ps, w4_codes.bitcast(FP4X4), w4_s[:, a, rows])
-                hold_pass = (hold_ps, w1_c[:, s, a, :].bitcast(FP8X4), w1_s[:, s, a, :])
-                move_pass = (move_ps, w8_codes.bitcast(FP8X4), w8_s[:, a, rows])
-                for acc, codes, scales in (hold_pass, move_pass, gate_pass) if half == 0 else (gate_pass, hold_pass, move_pass):
-                    nc.tensor.matmul_mx(
-                        out=acc[:], lhsT=codes, lhsT_scale=scales,
-                        rhs=v_w[a][:, entries].bitcast(FP8X4), rhs_scale=v_s[:, a, entries],
-                        start=(a == 0), stop=(a == PASSES - 1),
-                    )
-            hold_term = ring.tile([P, HALF], F32, name="hold_term", bufs=CHUNKS)
+                passes.append((0, a, hold_ps, w1_c[:, s, a, :].bitcast(FP8X4), w1_s[:, s, a, :]))
+                passes.append((1, a, move_ps, w8_codes.bitcast(FP8X4), w8_s[:, a, rows]))
+                passes.append((2, a, gate_ps, w4_codes.bitcast(FP4X4), w4_s[:, a, rows]))
+            if s > 0:
+                passes = [entry for product in range(3) for entry in passes if entry[0] == product]
+            for product, a, acc, codes, scales in passes:
+                nc.tensor.matmul_mx(
+                    out=acc[:], lhsT=codes, lhsT_scale=scales,
+                    rhs=v_w[a][:, entries].bitcast(FP8X4), rhs_scale=v_s[:, a, entries],
+                    start=(a == 0), stop=(a == PASSES - 1),
+                )
+            hold = ring.tile([P, HALF], F32, name="hold", bufs=CHUNKS)
             gate = ring.tile([P, HALF], F32, name="gate", bufs=CHUNKS)
-            if k < CHUNKS - 1:
-                h = ring.tile([P, HALF], F32, name="h")
-            else:
-                h = held("h_last", [P, HALF], F32, tag="w2_c")
-            from_sbuf = nc.gpsimd if k > 0 else nc.vector
-            if half == 0:
-                nc.scalar.copy(out=hold_term[:], in_=hold_ps[:])
+            h = held("h%d" % k, [P, HALF], F32)
+            nc.scalar.copy(out=hold[:], in_=hold_ps[:])
+            if k == 0:
                 nc.scalar.activation(out=gate[:], in_=gate_ps[:], func=ACT.Sigmoid)
-                nc.vector.tensor_tensor(h[:], move_ps[:], hold_term[:], ALU.subtract)
-                from_sbuf.tensor_tensor(h[:], h[:], gate[:], ALU.mult)
+                for first, other, op in ((move_ps, hold, ALU.subtract), (h, gate, ALU.mult), (h, hold, ALU.add), (h, wgs_sb, ALU.mult)):
+                    for cols in (slice(0, HALF // 2), slice(HALF // 2, HALF)):
+                        nc.vector.tensor_tensor(h[:, cols], first[:, cols], other[:, cols], op)
             else:
+                nc.scalar.copy(out=h[:], in_=move_ps[:])
                 nc.scalar.activation(out=gate[:], in_=gate_ps[:], func=ACT.Sigmoid)
-                nc.scalar.activation(out=hold_term[:], in_=gate_ps[:], func=ACT.Sigmoid, scale=-1.0)
-                nc.vector.tensor_tensor(h[:], move_ps[:], gate[:], ALU.mult)
-                nc.vector.tensor_tensor(hold_term[:], hold_ps[:], hold_term[:], ALU.mult)
-            from_sbuf.tensor_tensor(h[:], h[:], hold_term[:], ALU.add)
-            from_sbuf.tensor_tensor(h[:], h[:], wgs_sb[:, entries], ALU.mult)
+                nc.gpsimd.tensor_tensor(h[:], h[:], hold[:], ALU.subtract)
+                nc.gpsimd.tensor_tensor(h[:], h[:], gate[:], ALU.mult)
+                nc.gpsimd.tensor_tensor(h[:], h[:], hold[:], ALU.add)
+                if k in WEIGHED_ON_GPSIMD:
+                    nc.gpsimd.tensor_tensor(h[:], h[:], wgs_sb[:, entries], ALU.mult)
             weighted[k] = h
+
+        def wgs_to_psum():
+            wgs_t = held("wgs_t", [P, S], F32)
+            for half in range(HALVES):
+                turned = bank(WGS_BANKS[half], "wgs_turned")
+                for b in range(HALF // P):
+                    col0 = half * HALF + b * P
+                    nc.tensor.transpose(turned[:, b * P : (b + 1) * P], wgs_sb[:, col0 : col0 + P], ident[:])
+                nc.scalar.copy(out=wgs_t[:, half * HALF : (half + 1) * HALF], in_=turned[:])
+                wgs_ps.append(bank(WGS_BANKS[half], "wgs_ps"))
+                for b in range(HALF // P):
+                    col0 = half * HALF + b * P
+                    nc.tensor.transpose(wgs_ps[half][:, b * P : (b + 1) * P], wgs_t[:, col0 : col0 + P], ident[:])
 
         def scatter_to_page(k):
             s, half = divmod(k, HALVES)
-            nc.vector.tensor_copy(pages[s][:].indirect(list2[:, half * HALF_COLS : (half + 1) * HALF_COLS]), weighted[k][:])
+            window = pages[s][:].indirect(list2[:, half * HALF_COLS : (half + 1) * HALF_COLS])
+            if k < CHUNKS - 1:
+                if k > 0 and k not in WEIGHED_ON_GPSIMD:
+                    nc.vector.tensor_tensor(weighted[k][:], weighted[k][:], wgs_ps[half][:], ALU.mult)
+                nc.vector.tensor_copy(window, weighted[k][:])
+            else:
+                nc.vector.tensor_tensor(window, weighted[k][:], wgs_sb[:, half * HALF : (half + 1) * HALF], ALU.mult)
 
-        z_t = [held("z_t%d" % q, [P, BANK // P, H], BF16) for q in range(QUARTERS)]
-        open_sums = {}
+        states = {}
 
-        def turn_buf(s):
-            state = placed("state%d" % s, [P, T2], F32, (AT_LOW, AT_MID, AT_HIGH)[s % 3])
-            nc.sync.dma_start(out=state[:], in_=buf[s * P : (s + 1) * P, :])
+        def load_buf(s):
+            states[s] = placed("state%d" % s, [P, T2], F32, (AT_LOW, AT_MID, AT_HIGH)[s % 3])
+            nc.sync.dma_start(out=states[s][:], in_=buf[s * P : (s + 1) * P, :])
+
+        def turn(acc, source, s, b, opens):
+            for g in range(QUADRANTS):
+                col0 = (g - s) % QUARTERS * BANK + b * P
+                nc.tensor.matmul(out=acc[:, g * P : (g + 1) * P], lhsT=source[:, col0 : col0 + P], rhs=ident[:],
+                                 is_transpose=True, start=(opens and g == 0), stop=(not opens and g == QUADRANTS - 1))
+
+        def round_sum(acc, copy):
+            z_t = ring.tile([P, BANK], BF16, name="z_t")
+            copy(out=z_t[:].rearrange("t (u p e) -> t u p e", u=2, e=2), in_=acc[:].rearrange("t (p u e) -> t u p e", u=2, e=2))
+            return z_t
+
+        def turn_back(number, turned, z_g):
+            back = bank(number, "back_ps")
+            for b, z_t in enumerate(turned):
+                for u in range(2):
+                    nc.tensor.transpose(back[:, (2 * b + u) * P : (2 * b + u + 1) * P], z_t[:].bitcast(F32)[:, u * P : (u + 1) * P], ident[:])
+            nc.scalar.copy(out=z_g.bitcast(F32).rearrange("p (b t u) -> p b t u", b=2, u=2),
+                           in_=back[:].rearrange("p (b u t) -> p b t u", b=2, u=2))
+
+        def codes_of(tile, width, c0, c1):
+            return tile[:, c0:c1].bitcast(FP8X4)
+
+        def scales_of(tile, width, c0, c1):
+            return tile[:].bitcast(U8)[:, PACK * width + c0 : PACK * width + c1]
+
+        def quantise(tile, width, c0, c1, grouped):
+            nc.vector.quantize_mx(out=codes_of(tile, width, c0, c1), scales=scales_of(tile, width, c0, c1), in_=grouped)
+
+        z_q = [held("z_q%d" % q, [P, BANK + BANK // PACK], U32) for q in range(QUARTERS)]
+
+        def deal(z_made, s, move):
             for q in range(QUARTERS):
-                acc = bank((early_banks if s < SLICES - 1 else late_banks)[q], "z_ps")
-                open_sums[q] = acc
-                for b in range(BANK // P):
-                    col0 = q * BANK + b * P
-                    nc.tensor.matmul(out=acc[:, b * P : (b + 1) * P], lhsT=state[:, col0 : col0 + P], rhs=ident[:],
-                                     is_transpose=True, start=(b == 0), stop=False)
-
-        def turn_page(s, q, copy):
-            acc = open_sums[q]
-            for b in range(BANK // P):
-                col0 = q * BANK + b * P
-                nc.tensor.matmul(out=acc[:, b * P : (b + 1) * P], lhsT=pages[s][:, col0 : col0 + P], rhs=ident[:],
-                                 is_transpose=True, start=False, stop=(b == BANK // P - 1))
-            copy(
-                out=z_t[q][:].rearrange("t b (u p e) -> t b u p e", u=2, e=2)[:, :, :, 32 * s : 32 * (s + 1), :],
-                in_=acc[:].rearrange("t (b p u e) -> t b u p e", b=BANK // P, u=2, e=2),
-            )
+                g = (s + q) % QUADRANTS
+                move(out=z_q[q][:].bitcast(I32)[32 * g : 32 * (g + 1), :], in_=z_made[:].bitcast(I32)[32 * g : 32 * (g + 1), :])
 
         w2_g = held("w2_g", [P, N, PACK], BF16)
 
+        first_stage(0)
         round_w1(1, w1_raw1, 0)
         quantise_w1(1, 2)
-        first_stage(0)
         first_stage(1)
+        wgs_to_psum()
+        scatter_to_page(0)
+        first_stage(2)
         round_w1(2, w1_raw23, 0)
         round_w1(3, w1_raw23, P)
-        scatter_to_page(0)
         quantise_w1(2, SLICES)
-        first_stage(2)
         scatter_to_page(1)
-        round_and_interleave(w2_g[:], w2_raw[:])
-        for k in range(2, CHUNKS):
-            if k + 1 < CHUNKS:
-                first_stage(k + 1)
+        for k in range(2, CHUNKS - 1):
+            first_stage(k + 1)
             scatter_to_page(k)
+        round_and_interleave(w2_g[:], w2_raw[:])
+        scatter_to_page(CHUNKS - 1)
+        w2_q = [held("w2_q%d" % q, [P, N + N // PACK], U32, tag="h1" if q == 0 else None) for q in range(QUARTERS)]
+        for n0, n1 in ((0, 2 * P), (2 * P, N)):
+            quantise(w2_q[0], N, n0, n1, w2_g[:, n0:n1, :].rearrange("p c j -> p (c j)"))
+        for q in range(1, QUARTERS):
+            nc.sync.dma_start(out=w2_q[q][:].bitcast(I32)[32 * q : P, :], in_=w2_q[0][:].bitcast(I32)[0 : P - 32 * q, :])
+            nc.sync.dma_start(out=w2_q[q][:].bitcast(I32)[0 : 32 * q, :], in_=w2_q[0][:].bitcast(I32)[P - 32 * q : P, :])
+        blocks = BANK // P
         for s in range(SLICES - 1):
-            turn_buf(s)
-            for q in range(QUARTERS):
-                turn_page(s, q, nc.scalar.copy)
-        turn_buf(SLICES - 1)
+            load_buf(s)
+            turned = []
+            for b in range(blocks):
+                acc = bank(PRODUCT_BANKS[b], "z_ps")
+                turn(acc, states[s], s, b, True)
+                turn(acc, pages[s], s, b, False)
+                turned.append(round_sum(acc, nc.scalar.copy))
+            z_g = held("z_g%d" % s, [P, BANK * PACK], BF16)
+            for pair in range(2):
+                turn_back(SUM_BANKS[pair], turned[2 * pair : 2 * pair + 2], z_g[:, pair * 2 * BANK : (pair + 1) * 2 * BANK])
+            z_made = held("z_made", [P, BANK + BANK // PACK], U32, tag="h%d" % (CHUNKS - SLICES + 1 + s))
+            quantise(z_made, BANK, 0, BANK, z_g[:])
+            deal(z_made, s, nc.sync.dma_start)
+        last = SLICES - 1
+        load_buf(last)
+        open_sums = [bank(PRODUCT_BANKS[b], "z_ps") for b in range(blocks)]
+        for b in range(blocks):
+            turn(open_sums[b], states[last], last, b, True)
 
         wgo_sb = placed("wgo_sb", [P, P_OUT], F32, AT_MID)
         nc.sync.dma_start(out=wgo_sb[:], in_=wgo)
-        lanes = [placed("lanes0", [P, T2], F32, AT_WGS)]
+        lanes = [held("lanes0", [P, T2], F32, tag="page2")]
         nc.gpsimd.memset(lanes[0][:], 0.0)
 
-        w2_c = held("w2_c", [P, N], U32)
-        w2_s = held("w2_s", [P, N], U8)
-        for n0, n1 in ((0, 2 * P), (2 * P, N)):
-            nc.vector.quantize_mx(out=w2_c[:, n0:n1].bitcast(FP8X4), scales=w2_s[:, n0:n1],
-                                  in_=w2_g[:, n0:n1, :].rearrange("p c j -> p (c j)"))
-        z_c = held("z_c", [P, T2], U32)
-        z_s = held("z_s", [P, T2], U8)
         ys = [placed("y0", [P, T2], F32, AT_LOW), placed("y1", [P, T2], F32, AT_HIGH), held("y2", [P, T2], F32)]
 
         copies = (nc.scalar.copy, nc.vector.tensor_copy)
-        for q in range(QUARTERS):
-            turn_page(SLICES - 1, q, copies[q % 2])
-        piece = 2 * P
-        for turn in range(T2 // piece):
-            q, b0 = divmod(2 * turn, BANK // P)
-            pairs = z_t[q][:].bitcast(F32)
-            back = bank(early_banks[turn % len(early_banks)], "back_ps")
-            for b in range(2):
-                for u in range(2):
-                    nc.tensor.transpose(back[:, (2 * b + u) * P : (2 * b + u + 1) * P], pairs[:, b0 + b, u * P : (u + 1) * P], ident[:])
-            z_g = ring.tile([P, piece * PACK], BF16, name="z_g", align_bytes=64)
-            copies[turn % 2](out=z_g[:].bitcast(F32).rearrange("p (b t u) -> p b t u", b=2, u=2),
-                             in_=back[:].rearrange("p (b u t) -> p b t u", b=2, u=2))
-            cols = slice(turn * piece, (turn + 1) * piece)
-            nc.vector.quantize_mx(out=z_c[:, cols].bitcast(FP8X4), scales=z_s[:, cols], in_=z_g[:])
+        turned = []
+        for b in range(blocks):
+            turn(open_sums[b], pages[last], last, b, False)
+            turned.append(round_sum(open_sums[b], copies[b % 2]))
+        z_made = held("z_made_last", [P, BANK + BANK // PACK], U32)
+        for pair in range(2):
+            z_g = held("z_g_last%d" % pair, [P, 2 * BANK], BF16)
+            turn_back(SUM_BANKS[pair], turned[2 * pair : 2 * pair + 2], z_g[:])
+            quantise(z_made, BANK, pair * 2 * P, (pair + 1) * 2 * P, z_g[:])
+        deal(z_made, last, nc.vector.tensor_copy)
 
-        y_banks = late_banks + early_banks
-        spans = [(q * BANK, BANK) for q in range(QUARTERS)]
-        first_spans = spans[:-1] + [(T2 - 2 * piece, piece), (T2 - piece, piece)]
-        work = [(n, span) for n in range(N // P) for span in (first_spans if n == 0 else spans)]
-        for count, (n, (col0, width)) in enumerate(work):
-            cols = slice(col0, col0 + width)
+        y_banks = WGS_BANKS + PRODUCT_BANKS + SUM_BANKS
+        work = [(n, q) for n in range(N // P) for q in range(QUARTERS)]
+        for count, (n, q) in enumerate(work):
             y_ps = bank(y_banks[count % len(y_banks)], "y_ps")
             nc.tensor.matmul_mx(
-                out=y_ps[:, 0:width], lhsT=w2_c[:, n * P : (n + 1) * P].bitcast(FP8X4), lhsT_scale=w2_s[:, n * P : (n + 1) * P],
-                rhs=z_c[:, cols].bitcast(FP8X4), rhs_scale=z_s[:, cols], start=True, stop=True,
+                out=y_ps[:], lhsT=codes_of(w2_q[q], N, n * P, (n + 1) * P), lhsT_scale=scales_of(w2_q[q], N, n * P, (n + 1) * P),
+                rhs=codes_of(z_q[q], BANK, 0, BANK), rhs_scale=scales_of(z_q[q], BANK, 0, BANK), start=True, stop=True,
             )
-            copy = nc.vector.tensor_copy if n == 0 and col0 + width == T2 else nc.scalar.copy
-            copy(out=ys[n][:, cols], in_=y_ps[:, 0:width])
+            copy = nc.vector.tensor_copy if (n, q) == (0, QUARTERS - 1) else nc.scalar.copy
+            copy(out=ys[n][:, q * BANK : (q + 1) * BANK], in_=y_ps[:])
 
-        for n, tag in ((1, "w2_c"), (2, "z_c")):
+        for n, tag in ((1, "z_q0"), (2, "z_q1")):
             lanes.append(held("lanes%d" % n, [P, T2], F32, tag=tag))
             nc.gpsimd.memset(lanes[n][:], 0.0)
 

@@ -28,9 +28,11 @@ HALVES = S // HALF
 HALF_COLS = HALF // 16
 CHUNKS = SLICES * HALVES
 QUARTERS = T2 // BANK
+PIECE = 2 * P
+PIECE_WORDS = PIECE + PIECE // PACK
 SCALE_ROW0 = P - PASSES * 16
 
-WEIGHED_ON_GPSIMD = (6,)
+DIFFERENCE_IN_PSUM = (1, 2, 3)
 
 WGS_BANKS = (0, 1)
 PRODUCT_BANKS = (2, 3, 4, 5)
@@ -41,6 +43,9 @@ AT_WGS, AT_W8, AT_W4 = 0, 4, 8
 AT_LOW = 12
 AT_MID = 20
 AT_HIGH = 28
+AT_LATE_H = {5: 37}
+AT_W2_CODES = 36
+AT_Z_MADE = 38
 
 
 def tile_list_tote_lane_features_kernel(
@@ -62,8 +67,9 @@ def tile_list_tote_lane_features_kernel(
         def bank(number, name):
             return psum.tile([P, BANK], F32, name=name, tag="bank%d" % number)
 
-        def round_and_interleave(grouped, raw):
-            nc.scalar.copy(out=grouped.rearrange("p (c i) j -> p c j i", i=4), in_=raw.rearrange("p j (c i) -> p c j i", i=4))
+        def round_and_interleave(grouped, raw, sign):
+            nc.scalar.activation(out=grouped.rearrange("p (c i) j -> p c j i", i=4), in_=raw.rearrange("p j (c i) -> p c j i", i=4),
+                                 func=ACT.Copy, scale=sign)
 
         list1 = held("list1", [P, S // 16], U16)
         list2 = held("list2", [P, S // 16], U16)
@@ -137,7 +143,7 @@ def tile_list_tote_lane_features_kernel(
 
         def round_w1(s, raw, col0):
             for a in range(PASSES):
-                round_and_interleave(w1_g[:, s, a, :, :], raw[:, a, :, col0 : col0 + P])
+                round_and_interleave(w1_g[:, s, a, :, :], raw[:, a, :, col0 : col0 + P], -1.0)
 
         def quantise_w1(s0, s1):
             nc.vector.quantize_mx(
@@ -181,34 +187,42 @@ def tile_list_tote_lane_features_kernel(
             for a in range(PASSES):
                 w4_codes = w4_lo[:, a, :] if s == 0 else w4_hi[:, a, 2 * (s - 1) * P : 2 * s * P]
                 w8_codes = w8_lo[:, a, :] if s == 0 else w8_hi[:, a, (s - 1) * P : s * P]
-                passes.append((0, a, hold_ps, w1_c[:, s, a, :].bitcast(FP8X4), w1_s[:, s, a, :]))
-                passes.append((1, a, move_ps, w8_codes.bitcast(FP8X4), w8_s[:, a, rows]))
-                passes.append((2, a, gate_ps, w4_codes.bitcast(FP4X4), w4_s[:, a, rows]))
+                first, final = a == 0, a == PASSES - 1
+                passes.append((0, a, hold_ps, w1_c[:, s, a, :].bitcast(FP8X4), w1_s[:, s, a, :], first, final))
+                if k in DIFFERENCE_IN_PSUM:
+                    passes.append((1, a, move_ps, w1_c[:, s, a, :].bitcast(FP8X4), w1_s[:, s, a, :], first, False))
+                    first = False
+                passes.append((1, a, move_ps, w8_codes.bitcast(FP8X4), w8_s[:, a, rows], first, final))
+                passes.append((2, a, gate_ps, w4_codes.bitcast(FP4X4), w4_s[:, a, rows], a == 0, final))
             if s > 0:
                 passes = [entry for product in range(3) for entry in passes if entry[0] == product]
-            for product, a, acc, codes, scales in passes:
+            for product, a, acc, codes, scales, first, final in passes:
                 nc.tensor.matmul_mx(
                     out=acc[:], lhsT=codes, lhsT_scale=scales,
                     rhs=v_w[a][:, entries].bitcast(FP8X4), rhs_scale=v_s[:, a, entries],
-                    start=(a == 0), stop=(a == PASSES - 1),
+                    start=first, stop=final,
                 )
             hold = ring.tile([P, HALF], F32, name="hold", bufs=CHUNKS)
             gate = ring.tile([P, HALF], F32, name="gate", bufs=CHUNKS)
-            h = held("h%d" % k, [P, HALF], F32)
-            nc.scalar.copy(out=hold[:], in_=hold_ps[:])
+            if k in AT_LATE_H:
+                h = placed("h%d" % k, [P, HALF], F32, AT_LATE_H[k])
+            else:
+                h = held("h%d" % k, [P, HALF], F32)
+            nc.scalar.activation(out=hold[:], in_=hold_ps[:], func=ACT.Copy, scale=-1.0)
             if k == 0:
                 nc.scalar.activation(out=gate[:], in_=gate_ps[:], func=ACT.Sigmoid)
-                for first, other, op in ((move_ps, hold, ALU.subtract), (h, gate, ALU.mult), (h, hold, ALU.add), (h, wgs_sb, ALU.mult)):
+                part = held("part", [P, HALF], F32)
+                for target, first, other, op in ((part, move_ps, hold, ALU.subtract), (part, part, gate, ALU.mult), (part, part, hold, ALU.add), (h, part, wgs_sb, ALU.mult)):
                     for cols in (slice(0, HALF // 2), slice(HALF // 2, HALF)):
-                        nc.vector.tensor_tensor(h[:, cols], first[:, cols], other[:, cols], op)
+                        nc.vector.tensor_tensor(target[:, cols], first[:, cols], other[:, cols], op)
             else:
                 nc.scalar.copy(out=h[:], in_=move_ps[:])
                 nc.scalar.activation(out=gate[:], in_=gate_ps[:], func=ACT.Sigmoid)
-                nc.gpsimd.tensor_tensor(h[:], h[:], hold[:], ALU.subtract)
-                nc.gpsimd.tensor_tensor(h[:], h[:], gate[:], ALU.mult)
-                nc.gpsimd.tensor_tensor(h[:], h[:], hold[:], ALU.add)
-                if k in WEIGHED_ON_GPSIMD:
-                    nc.gpsimd.tensor_tensor(h[:], h[:], wgs_sb[:, entries], ALU.mult)
+                if k not in DIFFERENCE_IN_PSUM:
+                    nc.gpsimd.tensor_tensor(h[:], h[:], hold[:], ALU.subtract)
+                part = held("part1", [P, HALF], F32, tag="part") if k == 1 else h
+                nc.gpsimd.tensor_tensor(part[:], h[:], gate[:], ALU.mult)
+                nc.gpsimd.tensor_tensor(h[:], part[:], hold[:], ALU.add)
             weighted[k] = h
 
         def wgs_to_psum():
@@ -228,9 +242,12 @@ def tile_list_tote_lane_features_kernel(
             s, half = divmod(k, HALVES)
             window = pages[s][:].indirect(list2[:, half * HALF_COLS : (half + 1) * HALF_COLS])
             if k < CHUNKS - 1:
-                if k > 0 and k not in WEIGHED_ON_GPSIMD:
-                    nc.vector.tensor_tensor(weighted[k][:], weighted[k][:], wgs_ps[half][:], ALU.mult)
-                nc.vector.tensor_copy(window, weighted[k][:])
+                source = weighted[k]
+                if k == CHUNKS - 2:
+                    source = held("h_weighted", [P, HALF], F32, tag="z_g1")
+                if k > 0:
+                    nc.vector.tensor_tensor(source[:], weighted[k][:], wgs_ps[half][:], ALU.mult)
+                nc.vector.tensor_copy(window, source[:])
             else:
                 nc.vector.tensor_tensor(window, weighted[k][:], wgs_sb[:, half * HALF : (half + 1) * HALF], ALU.mult)
 
@@ -263,17 +280,20 @@ def tile_list_tote_lane_features_kernel(
             return tile[:, c0:c1].bitcast(FP8X4)
 
         def scales_of(tile, width, c0, c1):
-            return tile[:].bitcast(U8)[:, PACK * width + c0 : PACK * width + c1]
+            return tile.bitcast(U8)[:, PACK * width + c0 : PACK * width + c1]
 
         def quantise(tile, width, c0, c1, grouped):
             nc.vector.quantize_mx(out=codes_of(tile, width, c0, c1), scales=scales_of(tile, width, c0, c1), in_=grouped)
 
-        z_q = [held("z_q%d" % q, [P, BANK + BANK // PACK], U32) for q in range(QUARTERS)]
+        z_q = [held("z_q%d" % q, [P, 2 * PIECE_WORDS], U32) for q in range(QUARTERS)]
 
-        def deal(z_made, s, move):
+        def piece_of(tile, pair):
+            return tile[:, pair * PIECE_WORDS : (pair + 1) * PIECE_WORDS]
+
+        def deal(s, move, target, source):
             for q in range(QUARTERS):
                 g = (s + q) % QUADRANTS
-                move(out=z_q[q][:].bitcast(I32)[32 * g : 32 * (g + 1), :], in_=z_made[:].bitcast(I32)[32 * g : 32 * (g + 1), :])
+                move(out=target(z_q[q]).bitcast(I32)[32 * g : 32 * (g + 1), :], in_=source.bitcast(I32)[32 * g : 32 * (g + 1), :])
 
         w2_g = held("w2_g", [P, N, PACK], BF16)
 
@@ -288,19 +308,21 @@ def tile_list_tote_lane_features_kernel(
         round_w1(3, w1_raw23, P)
         quantise_w1(2, SLICES)
         scatter_to_page(1)
-        for k in range(2, CHUNKS - 1):
+        for k in range(2, CHUNKS - 2):
             first_stage(k + 1)
             scatter_to_page(k)
-        round_and_interleave(w2_g[:], w2_raw[:])
-        scatter_to_page(CHUNKS - 1)
-        w2_q = [held("w2_q%d" % q, [P, N + N // PACK], U32, tag="h1" if q == 0 else None) for q in range(QUARTERS)]
+        first_stage(CHUNKS - 1)
+        round_and_interleave(w2_g[:], w2_raw[:], 1.0)
+        w2_q = [placed("w2_q0", [P, N + N // PACK], U32, AT_W2_CODES)]
+        w2_q.extend(held("w2_q%d" % q, [P, N + N // PACK], U32) for q in range(1, QUARTERS))
         for n0, n1 in ((0, 2 * P), (2 * P, N)):
-            quantise(w2_q[0], N, n0, n1, w2_g[:, n0:n1, :].rearrange("p c j -> p (c j)"))
+            quantise(w2_q[0][:], N, n0, n1, w2_g[:, n0:n1, :].rearrange("p c j -> p (c j)"))
         for q in range(1, QUARTERS):
             nc.sync.dma_start(out=w2_q[q][:].bitcast(I32)[32 * q : P, :], in_=w2_q[0][:].bitcast(I32)[0 : P - 32 * q, :])
             nc.sync.dma_start(out=w2_q[q][:].bitcast(I32)[0 : 32 * q, :], in_=w2_q[0][:].bitcast(I32)[P - 32 * q : P, :])
         blocks = BANK // P
-        for s in range(SLICES - 1):
+
+        def finish_slice(s):
             load_buf(s)
             turned = []
             for b in range(blocks):
@@ -311,9 +333,19 @@ def tile_list_tote_lane_features_kernel(
             z_g = held("z_g%d" % s, [P, BANK * PACK], BF16)
             for pair in range(2):
                 turn_back(SUM_BANKS[pair], turned[2 * pair : 2 * pair + 2], z_g[:, pair * 2 * BANK : (pair + 1) * 2 * BANK])
-            z_made = held("z_made", [P, BANK + BANK // PACK], U32, tag="h%d" % (CHUNKS - SLICES + 1 + s))
-            quantise(z_made, BANK, 0, BANK, z_g[:])
-            deal(z_made, s, nc.sync.dma_start)
+            if s == 0:
+                z_made = placed("z_made0", [P, 2 * PIECE_WORDS], U32, AT_Z_MADE)
+            else:
+                z_made = held("z_made%d" % s, [P, 2 * PIECE_WORDS], U32)
+            for pair in range(2):
+                quantise(piece_of(z_made, pair), PIECE, 0, PIECE, z_g[:, pair * 2 * BANK : (pair + 1) * 2 * BANK])
+            deal(s, nc.sync.dma_start, lambda tile: tile[:], z_made[:])
+
+        finish_slice(0)
+        finish_slice(1)
+        scatter_to_page(CHUNKS - 2)
+        scatter_to_page(CHUNKS - 1)
+        finish_slice(2)
         last = SLICES - 1
         load_buf(last)
         open_sums = [bank(PRODUCT_BANKS[b], "z_ps") for b in range(blocks)]
@@ -322,8 +354,6 @@ def tile_list_tote_lane_features_kernel(
 
         wgo_sb = placed("wgo_sb", [P, P_OUT], F32, AT_MID)
         nc.sync.dma_start(out=wgo_sb[:], in_=wgo)
-        lanes = [held("lanes0", [P, T2], F32, tag="page2")]
-        nc.gpsimd.memset(lanes[0][:], 0.0)
 
         ys = [placed("y0", [P, T2], F32, AT_LOW), placed("y1", [P, T2], F32, AT_HIGH), held("y2", [P, T2], F32)]
 
@@ -332,25 +362,29 @@ def tile_list_tote_lane_features_kernel(
         for b in range(blocks):
             turn(open_sums[b], pages[last], last, b, False)
             turned.append(round_sum(open_sums[b], copies[b % 2]))
-        z_made = held("z_made_last", [P, BANK + BANK // PACK], U32)
         for pair in range(2):
             z_g = held("z_g_last%d" % pair, [P, 2 * BANK], BF16)
             turn_back(SUM_BANKS[pair], turned[2 * pair : 2 * pair + 2], z_g[:])
-            quantise(z_made, BANK, pair * 2 * P, (pair + 1) * 2 * P, z_g[:])
-        deal(z_made, last, nc.vector.tensor_copy)
+            z_made = held("z_made_last%d" % pair, [P, PIECE_WORDS], U32)
+            quantise(z_made[:], PIECE, 0, PIECE, z_g[:])
+            deal(last, nc.vector.tensor_copy, lambda tile: piece_of(tile, pair), z_made[:])
 
         y_banks = WGS_BANKS + PRODUCT_BANKS + SUM_BANKS
-        work = [(n, q) for n in range(N // P) for q in range(QUARTERS)]
-        for count, (n, q) in enumerate(work):
+        work = [(n, pair, q0) for n in range(N // P) for pair in range(2) for q0 in (0, 2)]
+        for count, (n, pair, q0) in enumerate(work):
             y_ps = bank(y_banks[count % len(y_banks)], "y_ps")
-            nc.tensor.matmul_mx(
-                out=y_ps[:], lhsT=codes_of(w2_q[q], N, n * P, (n + 1) * P), lhsT_scale=scales_of(w2_q[q], N, n * P, (n + 1) * P),
-                rhs=codes_of(z_q[q], BANK, 0, BANK), rhs_scale=scales_of(z_q[q], BANK, 0, BANK), start=True, stop=True,
-            )
-            copy = nc.vector.tensor_copy if (n, q) == (0, QUARTERS - 1) else nc.scalar.copy
-            copy(out=ys[n][:, q * BANK : (q + 1) * BANK], in_=y_ps[:])
+            for i in range(2):
+                weights, piece = w2_q[q0 + i][:], piece_of(z_q[q0 + i], pair)
+                nc.tensor.matmul_mx(
+                    out=y_ps[:, i * PIECE : (i + 1) * PIECE],
+                    lhsT=codes_of(weights, N, n * P, (n + 1) * P), lhsT_scale=scales_of(weights, N, n * P, (n + 1) * P),
+                    rhs=codes_of(piece, PIECE, 0, PIECE), rhs_scale=scales_of(piece, PIECE, 0, PIECE), start=True, stop=True,
+                )
+            copy = nc.vector.tensor_copy if count == 3 else nc.scalar.copy
+            copy(out=ys[n][:].rearrange("p (q h c) -> p q h c", q=QUARTERS, h=2)[:, q0 : q0 + 2, pair, :], in_=y_ps[:].rearrange("p (i c) -> p i c", i=2))
 
-        for n, tag in ((1, "z_q0"), (2, "z_q1")):
+        lanes = []
+        for n, tag in enumerate(("z_made_last1", "z_q0", "z_q1")):
             lanes.append(held("lanes%d" % n, [P, T2], F32, tag=tag))
             nc.gpsimd.memset(lanes[n][:], 0.0)
 

@@ -28,8 +28,6 @@ HALVES = S // HALF
 HALF_COLS = HALF // 16
 CHUNKS = SLICES * HALVES
 QUARTERS = T2 // BANK
-PIECE = 2 * P
-PIECE_WORDS = PIECE + PIECE // PACK
 SCALE_ROW0 = P - PASSES * 16
 
 DIFFERENCE_IN_PSUM = (1, 2, 3)
@@ -43,9 +41,6 @@ AT_WGS, AT_W8, AT_W4 = 0, 4, 8
 AT_LOW = 12
 AT_MID = 20
 AT_HIGH = 28
-AT_LATE_H = {5: 37}
-AT_W2_CODES = 36
-AT_Z_MADE = 38
 
 
 def tile_list_tote_lane_features_kernel(
@@ -202,12 +197,12 @@ def tile_list_tote_lane_features_kernel(
                     rhs=v_w[a][:, entries].bitcast(FP8X4), rhs_scale=v_s[:, a, entries],
                     start=first, stop=final,
                 )
-            hold = ring.tile([P, HALF], F32, name="hold", bufs=CHUNKS)
-            gate = ring.tile([P, HALF], F32, name="gate", bufs=CHUNKS)
-            if k in AT_LATE_H:
-                h = placed("h%d" % k, [P, HALF], F32, AT_LATE_H[k])
+            if k < CHUNKS - 1:
+                hold = ring.tile([P, HALF], F32, name="hold", bufs=CHUNKS - 1)
             else:
-                h = held("h%d" % k, [P, HALF], F32)
+                hold = held("hold_last", [P, HALF], F32)
+            gate = ring.tile([P, HALF], F32, name="gate", bufs=CHUNKS)
+            h = held("h%d" % k, [P, HALF], F32)
             nc.scalar.activation(out=hold[:], in_=hold_ps[:], func=ACT.Copy, scale=-1.0)
             if k == 0:
                 nc.scalar.activation(out=gate[:], in_=gate_ps[:], func=ACT.Sigmoid)
@@ -242,12 +237,9 @@ def tile_list_tote_lane_features_kernel(
             s, half = divmod(k, HALVES)
             window = pages[s][:].indirect(list2[:, half * HALF_COLS : (half + 1) * HALF_COLS])
             if k < CHUNKS - 1:
-                source = weighted[k]
-                if k == CHUNKS - 2:
-                    source = held("h_weighted", [P, HALF], F32, tag="z_g1")
                 if k > 0:
-                    nc.vector.tensor_tensor(source[:], weighted[k][:], wgs_ps[half][:], ALU.mult)
-                nc.vector.tensor_copy(window, source[:])
+                    nc.vector.tensor_tensor(weighted[k][:], weighted[k][:], wgs_ps[half][:], ALU.mult)
+                nc.vector.tensor_copy(window, weighted[k][:])
             else:
                 nc.vector.tensor_tensor(window, weighted[k][:], wgs_sb[:, half * HALF : (half + 1) * HALF], ALU.mult)
 
@@ -257,43 +249,19 @@ def tile_list_tote_lane_features_kernel(
             states[s] = placed("state%d" % s, [P, T2], F32, (AT_LOW, AT_MID, AT_HIGH)[s % 3])
             nc.sync.dma_start(out=states[s][:], in_=buf[s * P : (s + 1) * P, :])
 
-        def turn(acc, source, s, b, opens):
-            for g in range(QUADRANTS):
-                col0 = (g - s) % QUARTERS * BANK + b * P
-                nc.tensor.matmul(out=acc[:, g * P : (g + 1) * P], lhsT=source[:, col0 : col0 + P], rhs=ident[:],
-                                 is_transpose=True, start=(opens and g == 0), stop=(not opens and g == QUADRANTS - 1))
+        z_t = [held("z_t%d" % q, [P, BANK // P, H], BF16) for q in range(QUARTERS)]
 
-        def round_sum(acc, copy):
-            z_t = ring.tile([P, BANK], BF16, name="z_t")
-            copy(out=z_t[:].rearrange("t (u p e) -> t u p e", u=2, e=2), in_=acc[:].rearrange("t (p u e) -> t u p e", u=2, e=2))
-            return z_t
+        def turn(acc, source, q, opens):
+            for b in range(BANK // P):
+                col0 = q * BANK + b * P
+                nc.tensor.matmul(out=acc[:, b * P : (b + 1) * P], lhsT=source[:, col0 : col0 + P], rhs=ident[:],
+                                 is_transpose=True, start=(opens and b == 0), stop=(not opens and b == BANK // P - 1))
 
-        def turn_back(number, turned, z_g):
-            back = bank(number, "back_ps")
-            for b, z_t in enumerate(turned):
-                for u in range(2):
-                    nc.tensor.transpose(back[:, (2 * b + u) * P : (2 * b + u + 1) * P], z_t[:].bitcast(F32)[:, u * P : (u + 1) * P], ident[:])
-            nc.scalar.copy(out=z_g.bitcast(F32).rearrange("p (b t u) -> p b t u", b=2, u=2),
-                           in_=back[:].rearrange("p (b u t) -> p b t u", b=2, u=2))
-
-        def codes_of(tile, width, c0, c1):
-            return tile[:, c0:c1].bitcast(FP8X4)
-
-        def scales_of(tile, width, c0, c1):
-            return tile.bitcast(U8)[:, PACK * width + c0 : PACK * width + c1]
-
-        def quantise(tile, width, c0, c1, grouped):
-            nc.vector.quantize_mx(out=codes_of(tile, width, c0, c1), scales=scales_of(tile, width, c0, c1), in_=grouped)
-
-        z_q = [held("z_q%d" % q, [P, 2 * PIECE_WORDS], U32) for q in range(QUARTERS)]
-
-        def piece_of(tile, pair):
-            return tile[:, pair * PIECE_WORDS : (pair + 1) * PIECE_WORDS]
-
-        def deal(s, move, target, source):
-            for q in range(QUARTERS):
-                g = (s + q) % QUADRANTS
-                move(out=target(z_q[q]).bitcast(I32)[32 * g : 32 * (g + 1), :], in_=source.bitcast(I32)[32 * g : 32 * (g + 1), :])
+        def round_sum(acc, s, q, copy):
+            copy(
+                out=z_t[q][:].rearrange("t b (u p e) -> t b u p e", u=2, e=2)[:, :, :, 32 * s : 32 * (s + 1), :],
+                in_=acc[:].rearrange("t (b p u e) -> t b u p e", b=BANK // P, u=2, e=2),
+            )
 
         w2_g = held("w2_g", [P, N, PACK], BF16)
 
@@ -308,85 +276,70 @@ def tile_list_tote_lane_features_kernel(
         round_w1(3, w1_raw23, P)
         quantise_w1(2, SLICES)
         scatter_to_page(1)
-        for k in range(2, CHUNKS - 2):
+        for k in range(2, CHUNKS - 1):
             first_stage(k + 1)
             scatter_to_page(k)
-        first_stage(CHUNKS - 1)
         round_and_interleave(w2_g[:], w2_raw[:], 1.0)
-        w2_q = [placed("w2_q0", [P, N + N // PACK], U32, AT_W2_CODES)]
-        w2_q.extend(held("w2_q%d" % q, [P, N + N // PACK], U32) for q in range(1, QUARTERS))
+        w2_c = held("w2_c", [P, N], U32, tag="h%d" % (CHUNKS - 2))
+        w2_s = held("w2_s", [P, N], U8)
         for n0, n1 in ((0, 2 * P), (2 * P, N)):
-            quantise(w2_q[0][:], N, n0, n1, w2_g[:, n0:n1, :].rearrange("p c j -> p (c j)"))
-        for q in range(1, QUARTERS):
-            nc.sync.dma_start(out=w2_q[q][:].bitcast(I32)[32 * q : P, :], in_=w2_q[0][:].bitcast(I32)[0 : P - 32 * q, :])
-            nc.sync.dma_start(out=w2_q[q][:].bitcast(I32)[0 : 32 * q, :], in_=w2_q[0][:].bitcast(I32)[P - 32 * q : P, :])
-        blocks = BANK // P
-
-        def finish_slice(s):
-            load_buf(s)
-            turned = []
-            for b in range(blocks):
-                acc = bank(PRODUCT_BANKS[b], "z_ps")
-                turn(acc, states[s], s, b, True)
-                turn(acc, pages[s], s, b, False)
-                turned.append(round_sum(acc, nc.scalar.copy))
-            z_g = held("z_g%d" % s, [P, BANK * PACK], BF16)
-            for pair in range(2):
-                turn_back(SUM_BANKS[pair], turned[2 * pair : 2 * pair + 2], z_g[:, pair * 2 * BANK : (pair + 1) * 2 * BANK])
-            if s == 0:
-                z_made = placed("z_made0", [P, 2 * PIECE_WORDS], U32, AT_Z_MADE)
-            else:
-                z_made = held("z_made%d" % s, [P, 2 * PIECE_WORDS], U32)
-            for pair in range(2):
-                quantise(piece_of(z_made, pair), PIECE, 0, PIECE, z_g[:, pair * 2 * BANK : (pair + 1) * 2 * BANK])
-            deal(s, nc.sync.dma_start, lambda tile: tile[:], z_made[:])
-
-        finish_slice(0)
-        finish_slice(1)
-        scatter_to_page(CHUNKS - 2)
+            nc.vector.quantize_mx(out=w2_c[:, n0:n1].bitcast(FP8X4), scales=w2_s[:, n0:n1],
+                                  in_=w2_g[:, n0:n1, :].rearrange("p c j -> p (c j)"))
         scatter_to_page(CHUNKS - 1)
-        finish_slice(2)
         last = SLICES - 1
-        load_buf(last)
-        open_sums = [bank(PRODUCT_BANKS[b], "z_ps") for b in range(blocks)]
-        for b in range(blocks):
-            turn(open_sums[b], states[last], last, b, True)
+        open_sums = {}
+        for s in range(SLICES):
+            load_buf(s)
+            for q in range(QUARTERS):
+                open_sums[q] = bank(PRODUCT_BANKS[q], "z_ps")
+                turn(open_sums[q], states[s], q, True)
+                if s < last:
+                    turn(open_sums[q], pages[s], q, False)
+                    round_sum(open_sums[q], s, q, nc.scalar.copy)
 
         wgo_sb = placed("wgo_sb", [P, P_OUT], F32, AT_MID)
         nc.sync.dma_start(out=wgo_sb[:], in_=wgo)
 
+        lanes = [held("lanes0", [P, T2], F32, tag="hold_last")]
+        for q in range(QUARTERS):
+            nc.gpsimd.memset(lanes[0][:, q * BANK : (q + 1) * BANK], 0.0)
+
+        z_c = held("z_c", [P, T2], U32)
+        z_s = held("z_s", [P, T2], U8)
         ys = [placed("y0", [P, T2], F32, AT_LOW), placed("y1", [P, T2], F32, AT_HIGH), held("y2", [P, T2], F32)]
 
         copies = (nc.scalar.copy, nc.vector.tensor_copy)
-        turned = []
-        for b in range(blocks):
-            turn(open_sums[b], pages[last], last, b, False)
-            turned.append(round_sum(open_sums[b], copies[b % 2]))
-        for pair in range(2):
-            z_g = held("z_g_last%d" % pair, [P, 2 * BANK], BF16)
-            turn_back(SUM_BANKS[pair], turned[2 * pair : 2 * pair + 2], z_g[:])
-            z_made = held("z_made_last%d" % pair, [P, PIECE_WORDS], U32)
-            quantise(z_made[:], PIECE, 0, PIECE, z_g[:])
-            deal(last, nc.vector.tensor_copy, lambda tile: piece_of(tile, pair), z_made[:])
+        for q in range(QUARTERS):
+            turn(open_sums[q], pages[SLICES - 1], q, False)
+            round_sum(open_sums[q], SLICES - 1, q, copies[q % 2])
+        back_banks = SUM_BANKS + WGS_BANKS
+        piece = 2 * P
+        for step in range(T2 // piece):
+            q, b0 = divmod(2 * step, BANK // P)
+            pairs = z_t[q][:].bitcast(F32)
+            back = bank(back_banks[step % len(back_banks)], "back_ps")
+            for b in range(2):
+                for u in range(2):
+                    nc.tensor.transpose(back[:, (2 * b + u) * P : (2 * b + u + 1) * P], pairs[:, b0 + b, u * P : (u + 1) * P], ident[:])
+            z_g = ring.tile([P, piece * PACK], BF16, name="z_g", align_bytes=64)
+            copies[step % 2](out=z_g[:].bitcast(F32).rearrange("p (b t u) -> p b t u", b=2, u=2),
+                             in_=back[:].rearrange("p (b u t) -> p b t u", b=2, u=2))
+            cols = slice(step * piece, (step + 1) * piece)
+            nc.vector.quantize_mx(out=z_c[:, cols].bitcast(FP8X4), scales=z_s[:, cols], in_=z_g[:])
 
-        y_banks = WGS_BANKS + PRODUCT_BANKS + SUM_BANKS
-        work = [(n, pair, q0) for n in range(N // P) for pair in range(2) for q0 in (0, 2)]
-        for count, (n, pair, q0) in enumerate(work):
+        y_banks = PRODUCT_BANKS + back_banks
+        spans = [(q * BANK, BANK) for q in range(QUARTERS)]
+        first_spans = spans[:-1] + [(T2 - 2 * piece, piece), (T2 - piece, piece)]
+        work = [(n, span) for n in range(N // P) for span in (first_spans if n == 0 else spans)]
+        for count, (n, (col0, width)) in enumerate(work):
+            cols = slice(col0, col0 + width)
             y_ps = bank(y_banks[count % len(y_banks)], "y_ps")
-            for i in range(2):
-                weights, piece = w2_q[q0 + i][:], piece_of(z_q[q0 + i], pair)
-                nc.tensor.matmul_mx(
-                    out=y_ps[:, i * PIECE : (i + 1) * PIECE],
-                    lhsT=codes_of(weights, N, n * P, (n + 1) * P), lhsT_scale=scales_of(weights, N, n * P, (n + 1) * P),
-                    rhs=codes_of(piece, PIECE, 0, PIECE), rhs_scale=scales_of(piece, PIECE, 0, PIECE), start=True, stop=True,
-                )
-            copy = nc.vector.tensor_copy if count == 3 else nc.scalar.copy
-            copy(out=ys[n][:].rearrange("p (q h c) -> p q h c", q=QUARTERS, h=2)[:, q0 : q0 + 2, pair, :], in_=y_ps[:].rearrange("p (i c) -> p i c", i=2))
-
-        lanes = []
-        for n, tag in enumerate(("z_made_last1", "z_q0", "z_q1")):
-            lanes.append(held("lanes%d" % n, [P, T2], F32, tag=tag))
-            nc.gpsimd.memset(lanes[n][:], 0.0)
+            nc.tensor.matmul_mx(
+                out=y_ps[:, 0:width], lhsT=w2_c[:, n * P : (n + 1) * P].bitcast(FP8X4), lhsT_scale=w2_s[:, n * P : (n + 1) * P],
+                rhs=z_c[:, cols].bitcast(FP8X4), rhs_scale=z_s[:, cols], start=True, stop=True,
+            )
+            copy = nc.vector.tensor_copy if n == 0 and col0 + width == T2 else nc.scalar.copy
+            copy(out=ys[n][:, cols], in_=y_ps[:, 0:width])
 
         picked = []
 
@@ -395,6 +348,9 @@ def tile_list_tote_lane_features_kernel(
             nc.vector.tensor_copy(x[:], ys[n][:].indirect(list3[:]))
             nc.scalar.activation(out=x[:], in_=x[:], func=ACT.Tanh)
             picked.append(x)
+            if n > 0:
+                lanes.append(placed("lanes1", [P, T2], F32, AT_HIGH) if n == 1 else held("lanes2", [P, T2], F32, tag="y2"))
+                nc.gpsimd.memset(lanes[n][:], 0.0)
 
         pick(0)
         for n in range(N // P):

@@ -279,19 +279,20 @@ def tile_list_tote_lane_features_kernel(
         for k in range(2, CHUNKS - 1):
             first_stage(k + 1)
             scatter_to_page(k)
+        scatter_to_page(CHUNKS - 1)
         round_and_interleave(w2_g[:], w2_raw[:], 1.0)
-        w2_c = held("w2_c", [P, N], U32, tag="h%d" % (CHUNKS - 2))
+        w2_c = held("w2_c", [P, N], U32, tag="h%d" % (CHUNKS - 1))
         w2_s = held("w2_s", [P, N], U8)
         for n0, n1 in ((0, 2 * P), (2 * P, N)):
             nc.vector.quantize_mx(out=w2_c[:, n0:n1].bitcast(FP8X4), scales=w2_s[:, n0:n1],
                                   in_=w2_g[:, n0:n1, :].rearrange("p c j -> p (c j)"))
-        scatter_to_page(CHUNKS - 1)
         last = SLICES - 1
         open_sums = {}
+        last_banks = SUM_BANKS + PRODUCT_BANKS[:2]
         for s in range(SLICES):
             load_buf(s)
             for q in range(QUARTERS):
-                open_sums[q] = bank(PRODUCT_BANKS[q], "z_ps")
+                open_sums[q] = bank((PRODUCT_BANKS if s < last else last_banks)[q], "z_ps")
                 turn(open_sums[q], states[s], q, True)
                 if s < last:
                     turn(open_sums[q], pages[s], q, False)
@@ -312,7 +313,7 @@ def tile_list_tote_lane_features_kernel(
         for q in range(QUARTERS):
             turn(open_sums[q], pages[SLICES - 1], q, False)
             round_sum(open_sums[q], SLICES - 1, q, copies[q % 2])
-        back_banks = SUM_BANKS + WGS_BANKS
+        back_banks = PRODUCT_BANKS[2:] + WGS_BANKS
         piece = 2 * P
         for step in range(T2 // piece):
             q, b0 = divmod(2 * step, BANK // P)
@@ -322,12 +323,12 @@ def tile_list_tote_lane_features_kernel(
                 for u in range(2):
                     nc.tensor.transpose(back[:, (2 * b + u) * P : (2 * b + u + 1) * P], pairs[:, b0 + b, u * P : (u + 1) * P], ident[:])
             z_g = ring.tile([P, piece * PACK], BF16, name="z_g", align_bytes=64)
-            copies[step % 2](out=z_g[:].bitcast(F32).rearrange("p (b t u) -> p b t u", b=2, u=2),
+            copies[step % 2 if step < T2 // piece - 1 else 0](out=z_g[:].bitcast(F32).rearrange("p (b t u) -> p b t u", b=2, u=2),
                              in_=back[:].rearrange("p (b u t) -> p b t u", b=2, u=2))
             cols = slice(step * piece, (step + 1) * piece)
             nc.vector.quantize_mx(out=z_c[:, cols].bitcast(FP8X4), scales=z_s[:, cols], in_=z_g[:])
 
-        y_banks = PRODUCT_BANKS + back_banks
+        y_banks = last_banks + back_banks
         spans = [(q * BANK, BANK) for q in range(QUARTERS)]
         first_spans = spans[:-1] + [(T2 - 2 * piece, piece), (T2 - piece, piece)]
         work = [(n, span) for n in range(N // P) for span in (first_spans if n == 0 else spans)]

@@ -120,7 +120,9 @@ def tile_list_tote_lane_features_kernel(
         tab_w1 = placed("tab_w1", [P, T], U32, AT_WORDS[1])
         nc.sync.dma_start(out=tab_w1[:].bitcast(I32), in_=tab_words_i[1])
         v_w = [held("v_w%d" % a, [P, S], U32) for a in range(PASSES)]
-        nc.vector.tensor_copy(v_w[0][:], tab_w0[:].indirect(list1[:]))
+        for half in range(HALVES):
+            offsets = list1[:, half * HALF_COLS : (half + 1) * HALF_COLS]
+            nc.vector.tensor_copy(v_w[0][:, half * HALF : (half + 1) * HALF], tab_w0[:].indirect(offsets))
 
         w1_raw1 = placed("w1_raw1", [P, PASSES, PACK, P], F32, AT_LOW)
         w8_hi = placed("w8_hi", [P, PASSES, H - P], U32, AT_W8)
@@ -150,9 +152,8 @@ def tile_list_tote_lane_features_kernel(
         round_w1(0, w1_raw0, 0)
         quantise_w1(0, 1)
 
-        pages = [held("page%d" % s, [P, T2], F32, tag="w1_raw0" if s == 0 else None) for s in range(SLICES)]
-        nc.vector.memset(pages[0][:], 0.0)
-        for s in range(1, SLICES):
+        pages = [held("page%d" % s, [P, T2], F32) for s in range(SLICES)]
+        for s in range(SLICES):
             for q in range(QUARTERS):
                 nc.gpsimd.memset(pages[s][:, q * BANK : (q + 1) * BANK], 0.0)
 
@@ -221,7 +222,7 @@ def tile_list_tote_lane_features_kernel(
             weighted[k] = h
 
         def wgs_to_psum():
-            wgs_t = held("wgs_t", [P, S], F32)
+            wgs_t = held("wgs_t", [P, S], F32, tag="w1_raw0")
             for half in range(HALVES):
                 turned = bank(WGS_BANKS[half], "wgs_turned")
                 for b in range(HALF // P):

@@ -30,7 +30,9 @@ CHUNKS = SLICES * HALVES
 QUARTERS = T2 // BANK
 SCALE_ROW0 = P - PASSES * 16
 
-DIFFERENCE_IN_PSUM = (1, 2, 3)
+DIFFERENCE_IN_PSUM = (1, 6, 7)
+
+WEIGHED_ON_GPSIMD = 6
 
 WGS_BANKS = (0, 1)
 PRODUCT_BANKS = (2, 3, 4, 5)
@@ -214,11 +216,17 @@ def tile_list_tote_lane_features_kernel(
             else:
                 nc.scalar.copy(out=h[:], in_=move_ps[:])
                 nc.scalar.activation(out=gate[:], in_=gate_ps[:], func=ACT.Sigmoid)
-                if k not in DIFFERENCE_IN_PSUM:
-                    nc.gpsimd.tensor_tensor(h[:], h[:], hold[:], ALU.subtract)
-                part = held("part1", [P, HALF], F32, tag="part") if k == 1 else h
-                nc.gpsimd.tensor_tensor(part[:], h[:], gate[:], ALU.mult)
-                nc.gpsimd.tensor_tensor(h[:], part[:], hold[:], ALU.add)
+                part = held("part%d" % k, [P, HALF], F32, tag="part") if k == 1 or k >= WEIGHED_ON_GPSIMD else h
+                if k in DIFFERENCE_IN_PSUM:
+                    nc.gpsimd.tensor_tensor(part[:], h[:], gate[:], ALU.mult)
+                else:
+                    nc.gpsimd.tensor_tensor(part[:], h[:], hold[:], ALU.subtract)
+                    nc.gpsimd.tensor_tensor(part[:], part[:], gate[:], ALU.mult)
+                if k == WEIGHED_ON_GPSIMD:
+                    nc.gpsimd.tensor_tensor(part[:], part[:], hold[:], ALU.add)
+                    nc.gpsimd.tensor_tensor(h[:], part[:], wgs_sb[:, entries], ALU.mult)
+                else:
+                    nc.gpsimd.tensor_tensor(h[:], part[:], hold[:], ALU.add)
             weighted[k] = h
 
         def wgs_to_psum():
@@ -238,7 +246,7 @@ def tile_list_tote_lane_features_kernel(
             s, half = divmod(k, HALVES)
             window = pages[s][:].indirect(list2[:, half * HALF_COLS : (half + 1) * HALF_COLS])
             if k < CHUNKS - 1:
-                if k > 0:
+                if k not in (0, WEIGHED_ON_GPSIMD):
                     nc.vector.tensor_tensor(weighted[k][:], weighted[k][:], wgs_ps[half][:], ALU.mult)
                 nc.vector.tensor_copy(window, weighted[k][:])
             else:

@@ -38,11 +38,12 @@ WGS_BANKS = (0, 1)
 PRODUCT_BANKS = (2, 3, 4, 5)
 SUM_BANKS = (6, 7)
 
-AT_WORDS = (0, 20)
-AT_WGS, AT_W8, AT_W4 = 0, 4, 8
-AT_LOW = 12
-AT_MID = 20
-AT_HIGH = 28
+AT_WORDS = (8, 32)
+AT_W1 = (None, 8, 16, 32)
+AT_WGS, AT_W8_MID, AT_W4_MID, AT_W8_HI, AT_W4_HI = 12, 20, 21, 21.5, 23.5
+AT_W2 = 40
+AT_BUF = (4, 32, 40, 4)
+AT_Y0, AT_Y1, AT_WGO = AT_BUF[3], AT_BUF[2], AT_BUF[1]
 
 
 def tile_list_tote_lane_features_kernel(
@@ -59,7 +60,7 @@ def tile_list_tote_lane_features_kernel(
             return keep.tile(shape, dtype, name=name, tag=tag or name, align_bytes=64)
 
         def placed(name, shape, dtype, kib):
-            return arena.tile(shape, dtype, name=name, align_bytes=64, offset=kib * 1024)
+            return arena.tile(shape, dtype, name=name, align_bytes=64, offset=int(kib * 1024))
 
         def bank(number, name):
             return psum.tile([P, BANK], F32, name=name, tag="bank%d" % number)
@@ -72,7 +73,7 @@ def tile_list_tote_lane_features_kernel(
         list2 = held("list2", [P, S // 16], U16)
         list3 = held("list3", [P, P_OUT // 16], U16)
         list4 = held("list4", [P, P_OUT // 16], U16)
-        tab_s = placed("tab_s", [P, T], U8, AT_MID)
+        tab_s = placed("tab_s", [P, T], U8, AT_WORDS[1])
         w4_s = held("w4_s", [P, PASSES, H], U8)
         w8_s = held("w8_s", [P, PASSES, H], U8)
         v_s = held("v_s", [P, PASSES, S], U8)
@@ -126,33 +127,44 @@ def tile_list_tote_lane_features_kernel(
             offsets = list1[:, half * HALF_COLS : (half + 1) * HALF_COLS]
             nc.vector.tensor_copy(v_w[0][:, half * HALF : (half + 1) * HALF], tab_w0[:].indirect(offsets))
 
-        w1_raw1 = placed("w1_raw1", [P, PASSES, PACK, P], F32, AT_LOW)
-        w8_hi = placed("w8_hi", [P, PASSES, H - P], U32, AT_W8)
-        wgs_sb = placed("wgs_sb", [P, S], F32, AT_WGS)
-        for a in range(PASSES):
-            nc.sync.dma_start(out=w1_raw1[:, a, :, :], in_=w1_rows[a][:, :, P : 2 * P])
-        nc.sync.dma_start(out=wgs_sb[:], in_=wgs)
-        nc.sync.dma_start(out=w8_hi[:].bitcast(I32), in_=w8_words_i[:, :, P:H])
-        w4_hi = placed("w4_hi", [P, PASSES, 2 * (H - P)], U8, AT_W4)
-        nc.sync.dma_start(out=w4_hi[:].bitcast(I32), in_=w4_words_i[:, :, P // 2 : H // 2])
+        w1_raw = [w1_raw0]
 
-        w1_g = held("w1_g", [P, SLICES, PASSES, P, PACK], BF16)
-        w1_c = held("w1_c", [P, SLICES, PASSES, P], U32)
+        def load_w1(s):
+            w1_raw.append(placed("w1_raw%d" % s, [P, PASSES, PACK, P], F32, AT_W1[s]))
+            for a in range(PASSES):
+                nc.sync.dma_start(out=w1_raw[s][:, a, :, :], in_=w1_rows[a][:, :, s * P : (s + 1) * P])
+
+        load_w1(1)
+        wgs_sb = placed("wgs_sb", [P, S], F32, AT_WGS)
+        nc.sync.dma_start(out=wgs_sb[:], in_=wgs)
+        w8_mid = placed("w8_mid", [P, PASSES, P], U32, AT_W8_MID)
+        nc.sync.dma_start(out=w8_mid[:].bitcast(I32), in_=w8_words_i[:, :, P : 2 * P])
+        w4_mid = placed("w4_mid", [P, PASSES, 2 * P], U8, AT_W4_MID)
+        nc.sync.dma_start(out=w4_mid[:].bitcast(I32), in_=w4_words_i[:, :, P // 2 : P])
+        load_w1(2)
+        w8_hi = placed("w8_hi", [P, PASSES, 2 * P], U32, AT_W8_HI)
+        nc.sync.dma_start(out=w8_hi[:].bitcast(I32), in_=w8_words_i[:, :, 2 * P : H])
+        w4_hi = placed("w4_hi", [P, PASSES, 4 * P], U8, AT_W4_HI)
+        nc.sync.dma_start(out=w4_hi[:].bitcast(I32), in_=w4_words_i[:, :, P : H // 2])
+
+        w1_g, w1_c = {}, {}
         w1_s = held("w1_s", [P, SLICES, PASSES, P], U8)
 
-        def round_w1(s, raw, col0):
+        def round_w1(s):
+            w1_g[s] = held("w1_g%d" % s, [P, PASSES, P, PACK], BF16)
             for a in range(PASSES):
-                round_and_interleave(w1_g[:, s, a, :, :], raw[:, a, :, col0 : col0 + P], -1.0)
+                round_and_interleave(w1_g[s][:, a, :, :], w1_raw[s][:, a, :, :], -1.0)
 
-        def quantise_w1(s0, s1):
+        def quantise_w1(s, tag=None):
+            w1_c[s] = held("w1_c%d" % s, [P, PASSES, P], U32, tag=tag)
             nc.vector.quantize_mx(
-                out=w1_c[:, s0:s1, :, :].rearrange("p s a c -> p (s a c)").bitcast(FP8X4),
-                scales=w1_s[:, s0:s1, :, :].rearrange("p s a c -> p (s a c)"),
-                in_=w1_g[:, s0:s1, :, :, :].rearrange("p s a c j -> p (s a c j)"),
+                out=w1_c[s][:].rearrange("p a c -> p (a c)").bitcast(FP8X4),
+                scales=w1_s[:, s, :, :].rearrange("p a c -> p (a c)"),
+                in_=w1_g[s][:].rearrange("p a c j -> p (a c j)"),
             )
 
-        round_w1(0, w1_raw0, 0)
-        quantise_w1(0, 1)
+        round_w1(0)
+        quantise_w1(0)
 
         pages = [held("page%d" % s, [P, T2], F32) for s in range(SLICES)]
         for s in range(SLICES):
@@ -163,14 +175,13 @@ def tile_list_tote_lane_features_kernel(
             offsets = list1[:, half * HALF_COLS : (half + 1) * HALF_COLS]
             nc.vector.tensor_copy(v_w[1][:, half * HALF : (half + 1) * HALF], tab_w1[:].indirect(offsets))
 
-        w1_raw23 = placed("w1_raw23", [P, PASSES, PACK, 2 * P], F32, AT_MID)
-        w2_raw = placed("w2_raw", [P, PACK, N], F32, AT_HIGH)
-        for a in range(PASSES):
-            nc.sync.dma_start(out=w1_raw23[:, a, :, :], in_=w1_rows[a][:, :, 2 * P : H])
+        load_w1(3)
+        w2_raw = placed("w2_raw", [P, PACK, N], F32, AT_W2)
         nc.sync.dma_start(out=w2_raw[:], in_=w2.rearrange("(p j) n -> p j n", j=PACK))
 
         weighted = {}
-        wgs_ps = []
+        wgs_ps = {}
+        wgs_t = held("wgs_t", [P, S], F32, tag="w1_raw0")
 
         def first_stage(k):
             s, half = divmod(k, HALVES)
@@ -183,12 +194,12 @@ def tile_list_tote_lane_features_kernel(
             hold_ps, move_ps, gate_ps = [bank(number, name) for number, name in zip(numbers, ("hold_ps", "move_ps", "gate_ps"))]
             passes = []
             for a in range(PASSES):
-                w4_codes = w4_lo[:, a, :] if s == 0 else w4_hi[:, a, 2 * (s - 1) * P : 2 * s * P]
-                w8_codes = w8_lo[:, a, :] if s == 0 else w8_hi[:, a, (s - 1) * P : s * P]
+                w4_codes = (w4_lo[:, a, :], w4_mid[:, a, :], w4_hi[:, a, 0 : 2 * P], w4_hi[:, a, 2 * P : 4 * P])[s]
+                w8_codes = (w8_lo[:, a, :], w8_mid[:, a, :], w8_hi[:, a, 0:P], w8_hi[:, a, P : 2 * P])[s]
                 first, final = a == 0, a == PASSES - 1
-                passes.append((0, a, hold_ps, w1_c[:, s, a, :].bitcast(FP8X4), w1_s[:, s, a, :], first, final))
+                passes.append((0, a, hold_ps, w1_c[s][:, a, :].bitcast(FP8X4), w1_s[:, s, a, :], first, final))
                 if k in DIFFERENCE_IN_PSUM:
-                    passes.append((1, a, move_ps, w1_c[:, s, a, :].bitcast(FP8X4), w1_s[:, s, a, :], first, False))
+                    passes.append((1, a, move_ps, w1_c[s][:, a, :].bitcast(FP8X4), w1_s[:, s, a, :], first, False))
                     first = False
                 passes.append((1, a, move_ps, w8_codes.bitcast(FP8X4), w8_s[:, a, rows], first, final))
                 passes.append((2, a, gate_ps, w4_codes.bitcast(FP4X4), w4_s[:, a, rows], a == 0, final))
@@ -229,18 +240,16 @@ def tile_list_tote_lane_features_kernel(
                     nc.gpsimd.tensor_tensor(h[:], part[:], hold[:], ALU.add)
             weighted[k] = h
 
-        def wgs_to_psum():
-            wgs_t = held("wgs_t", [P, S], F32, tag="w1_raw0")
-            for half in range(HALVES):
-                turned = bank(WGS_BANKS[half], "wgs_turned")
-                for b in range(HALF // P):
-                    col0 = half * HALF + b * P
-                    nc.tensor.transpose(turned[:, b * P : (b + 1) * P], wgs_sb[:, col0 : col0 + P], ident[:])
-                nc.scalar.copy(out=wgs_t[:, half * HALF : (half + 1) * HALF], in_=turned[:])
-                wgs_ps.append(bank(WGS_BANKS[half], "wgs_ps"))
-                for b in range(HALF // P):
-                    col0 = half * HALF + b * P
-                    nc.tensor.transpose(wgs_ps[half][:, b * P : (b + 1) * P], wgs_t[:, col0 : col0 + P], ident[:])
+        def wgs_to_psum(half):
+            turned = bank(WGS_BANKS[half], "wgs_turned")
+            for b in range(HALF // P):
+                col0 = half * HALF + b * P
+                nc.tensor.transpose(turned[:, b * P : (b + 1) * P], wgs_sb[:, col0 : col0 + P], ident[:])
+            nc.scalar.copy(out=wgs_t[:, half * HALF : (half + 1) * HALF], in_=turned[:])
+            wgs_ps[half] = bank(WGS_BANKS[half], "wgs_ps")
+            for b in range(HALF // P):
+                col0 = half * HALF + b * P
+                nc.tensor.transpose(wgs_ps[half][:, b * P : (b + 1) * P], wgs_t[:, col0 : col0 + P], ident[:])
 
         def scatter_to_page(k):
             s, half = divmod(k, HALVES)
@@ -255,7 +264,7 @@ def tile_list_tote_lane_features_kernel(
         states = {}
 
         def load_buf(s):
-            states[s] = placed("state%d" % s, [P, T2], F32, (AT_LOW, AT_MID, AT_HIGH)[s % 3])
+            states[s] = placed("state%d" % s, [P, T2], F32, AT_BUF[s])
             nc.sync.dma_start(out=states[s][:], in_=buf[s * P : (s + 1) * P, :])
 
         z_t = [held("z_t%d" % q, [P, BANK // P, H], BF16) for q in range(QUARTERS)]
@@ -275,16 +284,18 @@ def tile_list_tote_lane_features_kernel(
         w2_g = held("w2_g", [P, N, PACK], BF16)
 
         first_stage(0)
-        round_w1(1, w1_raw1, 0)
-        quantise_w1(1, 2)
+        round_w1(1)
+        quantise_w1(1)
         first_stage(1)
-        wgs_to_psum()
+        wgs_to_psum(1)
         scatter_to_page(0)
+        round_w1(2)
+        quantise_w1(2, tag="h0")
         first_stage(2)
-        round_w1(2, w1_raw23, 0)
-        round_w1(3, w1_raw23, P)
-        quantise_w1(2, SLICES)
+        wgs_to_psum(0)
         scatter_to_page(1)
+        round_w1(3)
+        quantise_w1(3, tag="h1")
         for k in range(2, CHUNKS - 1):
             first_stage(k + 1)
             scatter_to_page(k)
@@ -307,7 +318,7 @@ def tile_list_tote_lane_features_kernel(
                     turn(open_sums[q], pages[s], q, False)
                     round_sum(open_sums[q], s, q, nc.scalar.copy)
 
-        wgo_sb = placed("wgo_sb", [P, P_OUT], F32, AT_MID)
+        wgo_sb = placed("wgo_sb", [P, P_OUT], F32, AT_WGO)
         nc.sync.dma_start(out=wgo_sb[:], in_=wgo)
 
         lanes = [held("lanes0", [P, T2], F32, tag="hold_last")]
@@ -316,7 +327,7 @@ def tile_list_tote_lane_features_kernel(
 
         z_c = held("z_c", [P, T2], U32)
         z_s = held("z_s", [P, T2], U8)
-        ys = [placed("y0", [P, T2], F32, AT_LOW), placed("y1", [P, T2], F32, AT_HIGH), held("y2", [P, T2], F32)]
+        ys = [placed("y0", [P, T2], F32, AT_Y0), placed("y1", [P, T2], F32, AT_Y1), held("y2", [P, T2], F32)]
 
         copies = (nc.scalar.copy, nc.vector.tensor_copy)
         for q in range(QUARTERS):
@@ -359,7 +370,7 @@ def tile_list_tote_lane_features_kernel(
             nc.scalar.activation(out=x[:], in_=x[:], func=ACT.Tanh)
             picked.append(x)
             if n > 0:
-                lanes.append(placed("lanes1", [P, T2], F32, AT_HIGH) if n == 1 else held("lanes2", [P, T2], F32, tag="y2"))
+                lanes.append(placed("lanes1", [P, T2], F32, AT_Y1) if n == 1 else held("lanes2", [P, T2], F32, tag="y2"))
                 nc.gpsimd.memset(lanes[n][:], 0.0)
 
         pick(0)

@@ -211,10 +211,7 @@ def tile_list_tote_lane_features_kernel(
                     rhs=v_w[a][:, entries].bitcast(FP8X4), rhs_scale=v_s[:, a, entries],
                     start=first, stop=final,
                 )
-            if k < CHUNKS - 1:
-                hold = ring.tile([P, HALF], F32, name="hold", bufs=CHUNKS - 1)
-            else:
-                hold = held("hold_last", [P, HALF], F32)
+            hold = held("hold%d" % k, [P, HALF], F32)
             gate = ring.tile([P, HALF], F32, name="gate", bufs=CHUNKS)
             h = held("h%d" % k, [P, HALF], F32)
             nc.scalar.activation(out=hold[:], in_=hold_ps[:], func=ACT.Copy, scale=-1.0)
@@ -257,6 +254,8 @@ def tile_list_tote_lane_features_kernel(
             if k < CHUNKS - 1:
                 if k not in (0, WEIGHED_ON_GPSIMD):
                     nc.vector.tensor_tensor(weighted[k][:], weighted[k][:], wgs_ps[half][:], ALU.mult)
+                if 1 <= k < SLICES - 1:
+                    quantise_w1(k + 1, tag="hold%d" % k)
                 nc.vector.tensor_copy(window, weighted[k][:])
             else:
                 nc.vector.tensor_tensor(window, weighted[k][:], wgs_sb[:, half * HALF : (half + 1) * HALF], ALU.mult)
@@ -290,12 +289,10 @@ def tile_list_tote_lane_features_kernel(
         wgs_to_psum(1)
         scatter_to_page(0)
         round_w1(2)
-        quantise_w1(2, tag="h0")
         first_stage(2)
         wgs_to_psum(0)
         scatter_to_page(1)
         round_w1(3)
-        quantise_w1(3, tag="h1")
         for k in range(2, CHUNKS - 1):
             first_stage(k + 1)
             scatter_to_page(k)
@@ -308,11 +305,11 @@ def tile_list_tote_lane_features_kernel(
                                   in_=w2_g[:, n0:n1, :].rearrange("p c j -> p (c j)"))
         last = SLICES - 1
         open_sums = {}
-        last_banks = SUM_BANKS + PRODUCT_BANKS[:2]
+        last_banks = SUM_BANKS + WGS_BANKS
         for s in range(SLICES):
             load_buf(s)
             for q in range(QUARTERS):
-                open_sums[q] = bank((PRODUCT_BANKS if s < last else last_banks)[q], "z_ps")
+                open_sums[q] = bank((2 * SUM_BANKS, PRODUCT_BANKS, PRODUCT_BANKS, last_banks)[s][q], "z_ps")
                 turn(open_sums[q], states[s], q, True)
                 if s < last:
                     turn(open_sums[q], pages[s], q, False)
@@ -321,7 +318,7 @@ def tile_list_tote_lane_features_kernel(
         wgo_sb = placed("wgo_sb", [P, P_OUT], F32, AT_WGO)
         nc.sync.dma_start(out=wgo_sb[:], in_=wgo)
 
-        lanes = [held("lanes0", [P, T2], F32, tag="hold_last")]
+        lanes = [held("lanes0", [P, T2], F32, tag="hold%d" % (CHUNKS - 1))]
         for q in range(QUARTERS):
             nc.gpsimd.memset(lanes[0][:, q * BANK : (q + 1) * BANK], 0.0)
 
@@ -333,7 +330,7 @@ def tile_list_tote_lane_features_kernel(
         for q in range(QUARTERS):
             turn(open_sums[q], pages[SLICES - 1], q, False)
             round_sum(open_sums[q], SLICES - 1, q, copies[q % 2])
-        back_banks = PRODUCT_BANKS[2:] + WGS_BANKS
+        back_banks = PRODUCT_BANKS
         piece = 2 * P
         for step in range(T2 // piece):
             q, b0 = divmod(2 * step, BANK // P)

@@ -30,7 +30,9 @@ CHUNKS = SLICES * HALVES
 QUARTERS = T2 // BANK
 SCALE_ROW0 = P - PASSES * 16
 
-DIFFERENCE_IN_PSUM = (1, 6, 7)
+ORDER = ((0, 0), (0, 1), (1, 0), (1, 1), (2, 0), (3, 0), (2, 1), (3, 1))
+
+DIFFERENCE_IN_PSUM = (1, 3, 6)
 
 WEIGHED_ON_GPSIMD = 6
 
@@ -184,7 +186,7 @@ def tile_list_tote_lane_features_kernel(
         wgs_t = held("wgs_t", [P, S], F32, tag="w1_raw0")
 
         def first_stage(k):
-            s, half = divmod(k, HALVES)
+            s, half = ORDER[k]
             entries = slice(half * HALF, (half + 1) * HALF)
             rows = slice(s * P, (s + 1) * P)
             if k == 1:
@@ -249,7 +251,7 @@ def tile_list_tote_lane_features_kernel(
                 nc.tensor.transpose(wgs_ps[half][:, b * P : (b + 1) * P], wgs_t[:, col0 : col0 + P], ident[:])
 
         def scatter_to_page(k):
-            s, half = divmod(k, HALVES)
+            s, half = ORDER[k]
             window = pages[s][:].indirect(list2[:, half * HALF_COLS : (half + 1) * HALF_COLS])
             if k < CHUNKS - 1:
                 if k not in (0, WEIGHED_ON_GPSIMD):

@@ -88,25 +88,26 @@ def tile_list_tote_lane_features_kernel(
         nc.vector.memset(tab_s[:].bitcast(I32)[0:SCALE_ROW0, :], 0)
         nc.vector.memset(v_s[:].rearrange("p a c -> p (a c)").bitcast(I32), 0)
 
-        warm = held("warm", [P, 2], F32)
-        nc.vector.memset(warm[:, 0:1], 0.0)
-        nc.scalar.activation(out=warm[:, 1:2], in_=warm[:, 0:1], func=ACT.Sigmoid)
-
         nc.sync.dma_start(list1[:], offs)
         nc.sync.dma_start(out=tab_s[:].bitcast(I32)[SCALE_ROW0:P, :], in_=tab_scales.bitcast(I32).rearrange("a g t -> g a t"))
         w1_rows = w1.rearrange("(a p j) c -> a p j c", a=PASSES, j=PACK)
         for a in range(PASSES):
-            nc.sync.dma_start(out=w1_raw0[:, a, :, :], in_=w1_rows[a][:, :, 0:P])
+            nc.scalar.dma_start(out=w1_raw0[:, a, :, :], in_=w1_rows[a][:, :, 0:P])
         w8_words_i = w8_words.rearrange("a p c j -> p a (c j)").bitcast(I32)
-        nc.sync.dma_start(out=w8_lo[:].bitcast(I32), in_=w8_words_i[:, :, 0:P])
+        nc.scalar.dma_start(out=w8_lo[:].bitcast(I32), in_=w8_words_i[:, :, 0:P])
         w4_words_i = w4_words.rearrange("a p c -> p a c").bitcast(I32)
-        nc.sync.dma_start(out=w4_lo[:].bitcast(I32), in_=w4_words_i[:, :, 0 : P // 2])
         nc.sync.dma_start(list2[:], offs2)
-        nc.sync.dma_start(list3[:], offs3)
+        nc.sync.dma_start(out=w4_lo[:].bitcast(I32), in_=w4_words_i[:, :, 0 : P // 2])
         tab_words_i = tab_words.rearrange("a p t j -> a p (t j)").bitcast(I32)
         tab_w0 = placed("tab_w0", [P, T], U32, AT_WORDS[0])
         nc.sync.dma_start(out=tab_w0[:].bitcast(I32), in_=tab_words_i[0])
+        nc.sync.dma_start(list3[:], offs3)
         nc.sync.dma_start(list4[:], offs4)
+
+        warm = held("warm", [P, 2], F32)
+        nc.vector.memset(warm[:, 0:1], 0.0)
+        nc.scalar.activation(out=warm[:, 1:2], in_=warm[:, 0:1], func=ACT.Sigmoid)
+
         for plane, scale_input, queue in ((w8_s, w8_scales, nc.gpsimd), (w4_s, w4_scales, nc.gpsimd)):
             for Q in range(QUADRANTS):
                 queue.dma_start(

@@ -348,13 +348,14 @@ def tile_list_tote_lane_features_kernel(
             cols = slice(step * piece, (step + 1) * piece)
             nc.vector.quantize_mx(out=z_c[:, cols].bitcast(FP8X4), scales=z_s[:, cols], in_=z_g[:])
 
-        y_banks = last_banks + back_banks
+        b0, b1, b2, b3 = back_banks
+        y_banks = (b0, b1, b2) + last_banks[:2] + (b3, b0, b1, b2) + last_banks[:2] + (b3, b0)
         spans = [(q * BANK, BANK) for q in range(QUARTERS)]
         first_spans = spans[:-1] + [(T2 - 2 * piece, piece), (T2 - piece, piece)]
         work = [(n, span) for n in range(N // P) for span in (first_spans if n == 0 else spans)]
         for count, (n, (col0, width)) in enumerate(work):
             cols = slice(col0, col0 + width)
-            y_ps = bank(y_banks[count % len(y_banks)], "y_ps")
+            y_ps = bank(y_banks[count], "y_ps")
             nc.tensor.matmul_mx(
                 out=y_ps[:, 0:width], lhsT=w2_c[:, n * P : (n + 1) * P].bitcast(FP8X4), lhsT_scale=w2_s[:, n * P : (n + 1) * P],
                 rhs=z_c[:, cols].bitcast(FP8X4), rhs_scale=z_s[:, cols], start=True, stop=True,

@@ -41,6 +41,7 @@ PRODUCT_BANKS = (2, 3, 4, 5)
 SUM_BANKS = (6, 7)
 
 AT_WORDS = (8, 32)
+AT_SCALES = 31
 AT_W1 = (None, 8, 16, 32)
 AT_WGS, AT_W8_MID, AT_W4_MID, AT_W8_HI, AT_W4_HI = 12, 20, 21, 21.5, 23.5
 AT_W2 = 40
@@ -75,13 +76,12 @@ def tile_list_tote_lane_features_kernel(
         list2 = held("list2", [P, S // 16], U16)
         list3 = held("list3", [P, P_OUT // 16], U16)
         list4 = held("list4", [P, P_OUT // 16], U16)
-        tab_s = placed("tab_s", [P, T], U8, AT_WORDS[1])
+        tab_s = placed("tab_s", [P, T], U8, AT_SCALES)
         w4_s = held("w4_s", [P, PASSES, H], U8)
         w8_s = held("w8_s", [P, PASSES, H], U8)
         v_s = held("v_s", [P, PASSES, S], U8)
         w1_raw0 = held("w1_raw0", [P, PASSES, PACK, P], F32)
         w8_lo = held("w8_lo", [P, PASSES, P], U32)
-        w4_lo = held("w4_lo", [P, PASSES, 2 * P], U8)
 
         for plane in (w4_s, w8_s):
             nc.vector.memset(plane[:].rearrange("p a c -> p (a c)").bitcast(I32), 0)
@@ -97,11 +97,10 @@ def tile_list_tote_lane_features_kernel(
         nc.scalar.dma_start(out=w8_lo[:].bitcast(I32), in_=w8_words_i[:, :, 0:P])
         w4_words_i = w4_words.rearrange("a p c -> p a c").bitcast(I32)
         nc.sync.dma_start(list2[:], offs2)
-        nc.sync.dma_start(out=w4_lo[:].bitcast(I32), in_=w4_words_i[:, :, 0 : P // 2])
+        nc.sync.dma_start(list3[:], offs3)
         tab_words_i = tab_words.rearrange("a p t j -> a p (t j)").bitcast(I32)
         tab_w0 = placed("tab_w0", [P, T], U32, AT_WORDS[0])
         nc.sync.dma_start(out=tab_w0[:].bitcast(I32), in_=tab_words_i[0])
-        nc.sync.dma_start(list3[:], offs3)
         nc.sync.dma_start(list4[:], offs4)
 
         warm = held("warm", [P, 2], F32)
@@ -125,6 +124,8 @@ def tile_list_tote_lane_features_kernel(
             nc.scalar.dma_start(out=v_s[:].rearrange("p a c -> p (a c)").bitcast(I32)[32 * Q : 32 * Q + 4, :], in_=picked_s[:].bitcast(I32)[row : row + 8, :])
         tab_w1 = placed("tab_w1", [P, T], U32, AT_WORDS[1])
         nc.sync.dma_start(out=tab_w1[:].bitcast(I32), in_=tab_words_i[1])
+        w4_lo = placed("w4_lo", [P, PASSES, 2 * P], U8, AT_SCALES)
+        nc.sync.dma_start(out=w4_lo[:].bitcast(I32), in_=w4_words_i[:, :, 0 : P // 2])
         v_w = [held("v_w%d" % a, [P, S], U32) for a in range(PASSES)]
         for half in range(HALVES):
             offsets = list1[:, half * HALF_COLS : (half + 1) * HALF_COLS]

@@ -119,11 +119,17 @@ def tile_list_tote_lane_features_kernel(
 
         picked_s = held("picked_s", [P, S], U8)
         nc.vector.tensor_copy(picked_s[:], tab_s[:].indirect(list1[:]))
-        for Q in range(QUADRANTS):
+
+        def move_scale_rows(Q, queue):
             row = SCALE_ROW0 + 8 * Q
-            nc.scalar.dma_start(out=v_s[:].rearrange("p a c -> p (a c)").bitcast(I32)[32 * Q : 32 * Q + 4, :], in_=picked_s[:].bitcast(I32)[row : row + 8, :])
+            queue.dma_start(out=v_s[:].rearrange("p a c -> p (a c)").bitcast(I32)[32 * Q : 32 * Q + 4, :], in_=picked_s[:].bitcast(I32)[row : row + 8, :])
+
+        for Q in range(QUADRANTS - 1):
+            move_scale_rows(Q, nc.scalar)
         tab_w1 = placed("tab_w1", [P, T], U32, AT_WORDS[1])
-        nc.sync.dma_start(out=tab_w1[:].bitcast(I32), in_=tab_words_i[1])
+        nc.sync.dma_start(out=tab_w1[:].bitcast(I32)[:, 0 : T // 2], in_=tab_words_i[1][:, 0 : T // 2])
+        move_scale_rows(QUADRANTS - 1, nc.sync)
+        nc.sync.dma_start(out=tab_w1[:].bitcast(I32)[:, T // 2 : T], in_=tab_words_i[1][:, T // 2 : T])
         w4_lo = placed("w4_lo", [P, PASSES, 2 * P], U8, AT_SCALES)
         nc.sync.dma_start(out=w4_lo[:].bitcast(I32), in_=w4_words_i[:, :, 0 : P // 2])
         v_w = [held("v_w%d" % a, [P, S], U32) for a in range(PASSES)]

@@ -41,9 +41,11 @@ PRODUCT_BANKS = (2, 3, 4, 5)
 SUM_BANKS = (6, 7)
 
 AT_WORDS = (8, 32)
-AT_SCALES = 31
-AT_W1 = (None, 8, 16, 32)
-AT_WGS, AT_W8_MID, AT_W4_MID, AT_W8_HI, AT_W4_HI = 12, 20, 21, 21.5, 23.5
+AT_SCALES = 28.5
+AT_W4_LO = 31.5
+AT_W1 = (None, 25, 16, 32)
+AT_WGS = (29, 12)
+AT_W8_MID, AT_W4_MID, AT_W8_HI, AT_W4_HI = 8, 9, 21.5, 23.5
 AT_W2 = 40
 AT_BUF = (4, 32, 40, 4)
 AT_Y0, AT_Y1, AT_WGO = AT_BUF[3], AT_BUF[2], AT_BUF[1]
@@ -130,7 +132,7 @@ def tile_list_tote_lane_features_kernel(
         nc.sync.dma_start(out=tab_w1[:].bitcast(I32)[:, 0 : T // 2], in_=tab_words_i[1][:, 0 : T // 2])
         move_scale_rows(QUADRANTS - 1, nc.sync)
         nc.sync.dma_start(out=tab_w1[:].bitcast(I32)[:, T // 2 : T], in_=tab_words_i[1][:, T // 2 : T])
-        w4_lo = placed("w4_lo", [P, PASSES, 2 * P], U8, AT_SCALES)
+        w4_lo = placed("w4_lo", [P, PASSES, 2 * P], U8, AT_W4_LO)
         nc.sync.dma_start(out=w4_lo[:].bitcast(I32), in_=w4_words_i[:, :, 0 : P // 2])
         v_w = [held("v_w%d" % a, [P, S], U32) for a in range(PASSES)]
         for half in range(HALVES):
@@ -145,8 +147,9 @@ def tile_list_tote_lane_features_kernel(
                 nc.sync.dma_start(out=w1_raw[s][:, a, :, :], in_=w1_rows[a][:, :, s * P : (s + 1) * P])
 
         load_w1(1)
-        wgs_sb = placed("wgs_sb", [P, S], F32, AT_WGS)
-        nc.sync.dma_start(out=wgs_sb[:], in_=wgs)
+        wgs_sb = [placed("wgs_sb%d" % half, [P, HALF], F32, AT_WGS[half]) for half in range(HALVES)]
+        for half in range(HALVES):
+            nc.sync.dma_start(out=wgs_sb[half][:], in_=wgs[:, half * HALF : (half + 1) * HALF])
         w8_mid = placed("w8_mid", [P, PASSES, P], U32, AT_W8_MID)
         nc.sync.dma_start(out=w8_mid[:].bitcast(I32), in_=w8_words_i[:, :, P : 2 * P])
         w4_mid = placed("w4_mid", [P, PASSES, 2 * P], U8, AT_W4_MID)
@@ -176,10 +179,11 @@ def tile_list_tote_lane_features_kernel(
         round_w1(0)
         quantise_w1(0)
 
-        pages = [held("page%d" % s, [P, T2], F32) for s in range(SLICES)]
-        for s in range(SLICES):
+        pages = [held("page%d" % s, [P, T2], F32, tag="w1_g0" if s == SLICES - 1 else None) for s in range(SLICES)]
+        for s in range(SLICES - 1):
             for q in range(QUARTERS):
                 nc.gpsimd.memset(pages[s][:, q * BANK : (q + 1) * BANK], 0.0)
+        nc.vector.memset(pages[SLICES - 1][:].bitcast(I32), 0)
 
         for half in range(HALVES):
             offsets = list1[:, half * HALF_COLS : (half + 1) * HALF_COLS]
@@ -228,7 +232,7 @@ def tile_list_tote_lane_features_kernel(
             if k == 0:
                 nc.scalar.activation(out=gate[:], in_=gate_ps[:], func=ACT.Sigmoid)
                 part = held("part", [P, HALF], F32)
-                for target, first, other, op in ((part, move_ps, hold, ALU.subtract), (part, part, gate, ALU.mult), (part, part, hold, ALU.add), (h, part, wgs_sb, ALU.mult)):
+                for target, first, other, op in ((part, move_ps, hold, ALU.subtract), (part, part, gate, ALU.mult), (part, part, hold, ALU.add), (h, part, wgs_sb[half], ALU.mult)):
                     for cols in (slice(0, HALF // 2), slice(HALF // 2, HALF)):
                         nc.vector.tensor_tensor(target[:, cols], first[:, cols], other[:, cols], op)
             else:
@@ -242,7 +246,7 @@ def tile_list_tote_lane_features_kernel(
                     nc.gpsimd.tensor_tensor(part[:], part[:], gate[:], ALU.mult)
                 if k == WEIGHED_ON_GPSIMD:
                     nc.gpsimd.tensor_tensor(part[:], part[:], hold[:], ALU.add)
-                    nc.gpsimd.tensor_tensor(h[:], part[:], wgs_sb[:, entries], ALU.mult)
+                    nc.gpsimd.tensor_tensor(h[:], part[:], wgs_sb[half][:], ALU.mult)
                 else:
                     nc.gpsimd.tensor_tensor(h[:], part[:], hold[:], ALU.add)
             weighted[k] = h
@@ -250,8 +254,7 @@ def tile_list_tote_lane_features_kernel(
         def wgs_to_psum(half):
             turned = bank(WGS_BANKS[half], "wgs_turned")
             for b in range(HALF // P):
-                col0 = half * HALF + b * P
-                nc.tensor.transpose(turned[:, b * P : (b + 1) * P], wgs_sb[:, col0 : col0 + P], ident[:])
+                nc.tensor.transpose(turned[:, b * P : (b + 1) * P], wgs_sb[half][:, b * P : (b + 1) * P], ident[:])
             nc.scalar.copy(out=wgs_t[:, half * HALF : (half + 1) * HALF], in_=turned[:])
             wgs_ps[half] = bank(WGS_BANKS[half], "wgs_ps")
             for b in range(HALF // P):
@@ -268,7 +271,7 @@ def tile_list_tote_lane_features_kernel(
                     quantise_w1(k + 1, tag="hold%d" % k)
                 nc.vector.tensor_copy(window, weighted[k][:])
             else:
-                nc.vector.tensor_tensor(window, weighted[k][:], wgs_sb[:, half * HALF : (half + 1) * HALF], ALU.mult)
+                nc.vector.tensor_tensor(window, weighted[k][:], wgs_sb[half][:], ALU.mult)
 
         states = {}
 

@@ -41,10 +41,11 @@ PRODUCT_BANKS = (2, 3, 4, 5)
 SUM_BANKS = (6, 7)
 
 AT_WORDS = (8, 32)
-AT_SCALES = 28.5
+AT_SCALES = 28.25
 AT_W4_LO = 31.5
-AT_W1 = (None, 25, 16, 32)
-AT_WGS = (29, 12)
+AT_W8_LO = 30.5
+AT_W1 = (None, 24.5, 16, 32)
+AT_WGS = (28.5, 12)
 AT_W8_MID, AT_W4_MID, AT_W8_HI, AT_W4_HI = 8, 9, 21.5, 23.5
 AT_W2 = 40
 AT_BUF = (4, 32, 40, 4)
@@ -83,7 +84,6 @@ def tile_list_tote_lane_features_kernel(
         w8_s = held("w8_s", [P, PASSES, H], U8)
         v_s = held("v_s", [P, PASSES, S], U8)
         w1_raw0 = held("w1_raw0", [P, PASSES, PACK, P], F32)
-        w8_lo = held("w8_lo", [P, PASSES, P], U32)
 
         for plane in (w4_s, w8_s):
             nc.vector.memset(plane[:].rearrange("p a c -> p (a c)").bitcast(I32), 0)
@@ -96,7 +96,6 @@ def tile_list_tote_lane_features_kernel(
         for a in range(PASSES):
             nc.scalar.dma_start(out=w1_raw0[:, a, :, :], in_=w1_rows[a][:, :, 0:P])
         w8_words_i = w8_words.rearrange("a p c j -> p a (c j)").bitcast(I32)
-        nc.scalar.dma_start(out=w8_lo[:].bitcast(I32), in_=w8_words_i[:, :, 0:P])
         w4_words_i = w4_words.rearrange("a p c -> p a c").bitcast(I32)
         nc.sync.dma_start(list2[:], offs2)
         nc.sync.dma_start(list3[:], offs3)
@@ -132,6 +131,8 @@ def tile_list_tote_lane_features_kernel(
         nc.sync.dma_start(out=tab_w1[:].bitcast(I32)[:, 0 : T // 2], in_=tab_words_i[1][:, 0 : T // 2])
         move_scale_rows(QUADRANTS - 1, nc.sync)
         nc.sync.dma_start(out=tab_w1[:].bitcast(I32)[:, T // 2 : T], in_=tab_words_i[1][:, T // 2 : T])
+        w8_lo = placed("w8_lo", [P, PASSES, P], U32, AT_W8_LO)
+        nc.sync.dma_start(out=w8_lo[:].bitcast(I32), in_=w8_words_i[:, :, 0:P])
         w4_lo = placed("w4_lo", [P, PASSES, 2 * P], U8, AT_W4_LO)
         nc.sync.dma_start(out=w4_lo[:].bitcast(I32), in_=w4_words_i[:, :, 0 : P // 2])
         v_w = [held("v_w%d" % a, [P, S], U32) for a in range(PASSES)]
@@ -197,7 +198,7 @@ def tile_list_tote_lane_features_kernel(
         wgs_ps = {}
         wgs_t = held("wgs_t", [P, S], F32, tag="w1_raw0")
 
-        def first_stage(k):
+        def plan(k):
             s, half = ORDER[k]
             entries = slice(half * HALF, (half + 1) * HALF)
             rows = slice(s * P, (s + 1) * P)
@@ -219,12 +220,22 @@ def tile_list_tote_lane_features_kernel(
                 passes.append((2, a, gate_ps, w4_codes.bitcast(FP4X4), w4_s[:, a, rows], a == 0, final))
             if s > 0:
                 passes = [entry for product in range(3) for entry in passes if entry[0] == product]
-            for product, a, acc, codes, scales, first, final in passes:
+            return (hold_ps, move_ps, gate_ps), [entry + (entries,) for entry in passes]
+
+        def run(passes):
+            for product, a, acc, codes, scales, first, final, entries in passes:
                 nc.tensor.matmul_mx(
                     out=acc[:], lhsT=codes, lhsT_scale=scales,
                     rhs=v_w[a][:, entries].bitcast(FP8X4), rhs_scale=v_s[:, a, entries],
                     start=first, stop=final,
                 )
+
+        begun = {}
+
+        def first_stage(k):
+            s, half = ORDER[k]
+            (hold_ps, move_ps, gate_ps), passes = begun[k] if k in begun else plan(k)
+            run(passes)
             hold = held("hold%d" % k, [P, HALF], F32)
             gate = ring.tile([P, HALF], F32, name="gate", bufs=CHUNKS)
             h = held("h%d" % k, [P, HALF], F32)
@@ -295,6 +306,12 @@ def tile_list_tote_lane_features_kernel(
 
         w2_g = held("w2_g", [P, N, PACK], BF16)
 
+        for k, early in ((0, 1), (1, 2)):
+            banks, passes = plan(k)
+            run(passes[:early])
+            begun[k] = banks, passes[early:]
+        banks, passes = begun[0]
+        begun[0] = banks, [passes[n] for n in (0, 2, 3, 1, 4)]
         first_stage(0)
         round_w1(1)
         quantise_w1(1)

@@ -47,9 +47,10 @@ AT_W8_LO = 30.5
 AT_W1 = (None, 24.5, 16, 32)
 AT_WGS = (28.5, 12)
 AT_W8_MID, AT_W4_MID, AT_W8_HI, AT_W4_HI = 8, 9, 21.5, 23.5
-AT_W2 = 40
-AT_BUF = (4, 32, 40, 4)
-AT_Y0, AT_Y1, AT_WGO = AT_BUF[3], AT_BUF[2], AT_BUF[1]
+AT_W2 = 41.5
+AT_BUF = (4, 31.75, 39.75, 47.75)
+AT_Y0, AT_Y1, AT_WGO = AT_BUF[0], AT_BUF[3], AT_BUF[1]
+AT_LAST_H = AT_BUF[2]
 
 
 def tile_list_tote_lane_features_kernel(
@@ -196,6 +197,7 @@ def tile_list_tote_lane_features_kernel(
 
         weighted = {}
         wgs_ps = {}
+        last_step = []
         wgs_t = held("wgs_t", [P, S], F32, tag="w1_raw0")
 
         def plan(k):
@@ -258,8 +260,10 @@ def tile_list_tote_lane_features_kernel(
                 if k == WEIGHED_ON_GPSIMD:
                     nc.gpsimd.tensor_tensor(part[:], part[:], hold[:], ALU.add)
                     nc.gpsimd.tensor_tensor(h[:], part[:], wgs_sb[half][:], ALU.mult)
-                else:
+                elif k < CHUNKS - 1:
                     nc.gpsimd.tensor_tensor(h[:], part[:], hold[:], ALU.add)
+                else:
+                    last_step.extend((part, hold))
             weighted[k] = h
 
         def wgs_to_psum(half):
@@ -326,24 +330,47 @@ def tile_list_tote_lane_features_kernel(
         for k in range(2, CHUNKS - 1):
             first_stage(k + 1)
             scatter_to_page(k)
-        scatter_to_page(CHUNKS - 1)
         round_and_interleave(w2_g[:], w2_raw[:], 1.0)
-        w2_c = held("w2_c", [P, N], U32, tag="h%d" % (CHUNKS - 1))
+        last = SLICES - 1
+        open_sums = {}
+        last_banks = SUM_BANKS + (WGS_BANKS[1], PRODUCT_BANKS[0])
+        back_banks = PRODUCT_BANKS[1:] + WGS_BANKS[:1]
+        sums = {}
+
+        def open_sum(s, q, number):
+            sums[s, q] = bank(number, "z_ps")
+            turn(sums[s, q], states[s], q, True)
+
+        def close_sum(s, q):
+            turn(sums[s, q], pages[s], q, False)
+            round_sum(sums[s, q], s, q, nc.scalar.copy)
+
+        for s in (0, 1, last, last - 1):
+            load_buf(s)
+        for q in range(QUARTERS):
+            open_sum(0, q, SUM_BANKS[q % 2])
+            close_sum(0, q)
+        for q in range(QUARTERS - 1):
+            open_sum(1, q, back_banks[q])
+        for q in range(QUARTERS):
+            open_sum(last, q, last_banks[q])
+            open_sums[q] = sums[last, q]
+        close_sum(1, 0)
+        open_sum(1, QUARTERS - 1, back_banks[0])
+        for q in range(1, QUARTERS):
+            close_sum(1, q)
+        for q in range(QUARTERS):
+            open_sum(last - 1, q, back_banks[q])
+        for q in range(QUARTERS):
+            close_sum(last - 1, q)
+        weighted[CHUNKS - 1] = placed("h_last", [P, HALF], F32, AT_LAST_H)
+        nc.gpsimd.tensor_tensor(weighted[CHUNKS - 1][:], last_step[0][:], last_step[1][:], ALU.add)
+        scatter_to_page(CHUNKS - 1)
+        w2_c = placed("w2_c", [P, N], U32, AT_LAST_H)
         w2_s = held("w2_s", [P, N], U8)
         for n0, n1 in ((0, 2 * P), (2 * P, N)):
             nc.vector.quantize_mx(out=w2_c[:, n0:n1].bitcast(FP8X4), scales=w2_s[:, n0:n1],
                                   in_=w2_g[:, n0:n1, :].rearrange("p c j -> p (c j)"))
-        last = SLICES - 1
-        open_sums = {}
-        last_banks = SUM_BANKS + WGS_BANKS
-        for s in range(SLICES):
-            load_buf(s)
-            for q in range(QUARTERS):
-                open_sums[q] = bank((2 * SUM_BANKS, PRODUCT_BANKS, PRODUCT_BANKS, last_banks)[s][q], "z_ps")
-                turn(open_sums[q], states[s], q, True)
-                if s < last:
-                    turn(open_sums[q], pages[s], q, False)
-                    round_sum(open_sums[q], s, q, nc.scalar.copy)
 
         wgo_sb = placed("wgo_sb", [P, P_OUT], F32, AT_WGO)
         nc.sync.dma_start(out=wgo_sb[:], in_=wgo)
@@ -360,7 +387,6 @@ def tile_list_tote_lane_features_kernel(
         for q in range(QUARTERS):
             turn(open_sums[q], pages[SLICES - 1], q, False)
             round_sum(open_sums[q], SLICES - 1, q, copies[q % 2])
-        back_banks = PRODUCT_BANKS
         piece = 2 * P
         for step in range(T2 // piece):
             q, b0 = divmod(2 * step, BANK // P)

@@ -391,18 +391,17 @@ def tile_list_tote_lane_features_kernel(
         for step in range(T2 // piece):
             q, b0 = divmod(2 * step, BANK // P)
             pairs = z_t[q][:].bitcast(F32)
-            back = bank(back_banks[step % len(back_banks)], "back_ps")
+            back = bank((back_banks + last_banks)[step], "back_ps")
             for b in range(2):
                 for u in range(2):
                     nc.tensor.transpose(back[:, (2 * b + u) * P : (2 * b + u + 1) * P], pairs[:, b0 + b, u * P : (u + 1) * P], ident[:])
             z_g = ring.tile([P, piece * PACK], BF16, name="z_g", align_bytes=64)
-            copies[step % 2 if step < T2 // piece - 1 else 0](out=z_g[:].bitcast(F32).rearrange("p (b t u) -> p b t u", b=2, u=2),
+            copies[step in (1, 3)](out=z_g[:].bitcast(F32).rearrange("p (b t u) -> p b t u", b=2, u=2),
                              in_=back[:].rearrange("p (b u t) -> p b t u", b=2, u=2))
             cols = slice(step * piece, (step + 1) * piece)
             nc.vector.quantize_mx(out=z_c[:, cols].bitcast(FP8X4), scales=z_s[:, cols], in_=z_g[:])
 
-        b0, b1, b2, b3 = back_banks
-        y_banks = (b0, b1, b2) + last_banks[:2] + (b3, b0, b1, b2) + last_banks[:2] + (b3, b0)
+        y_banks = 2 * (back_banks + last_banks)
         spans = [(q * BANK, BANK) for q in range(QUARTERS)]
         first_spans = spans[:-1] + [(T2 - 2 * piece, piece), (T2 - piece, piece)]
         work = [(n, span) for n in range(N // P) for span in (first_spans if n == 0 else spans)]
@@ -413,7 +412,7 @@ def tile_list_tote_lane_features_kernel(
                 out=y_ps[:, 0:width], lhsT=w2_c[:, n * P : (n + 1) * P].bitcast(FP8X4), lhsT_scale=w2_s[:, n * P : (n + 1) * P],
                 rhs=z_c[:, cols].bitcast(FP8X4), rhs_scale=z_s[:, cols], start=True, stop=True,
             )
-            copy = nc.vector.tensor_copy if n == 0 and col0 + width == T2 else nc.scalar.copy
+            copy = copies[n == 0 and count not in (0, 2)]
             copy(out=ys[n][:, cols], in_=y_ps[:, 0:width])
 
         picked = []

@@ -47,9 +47,9 @@ AT_W8_LO = 30.5
 AT_W1 = (None, 24.5, 16, 32)
 AT_WGS = (28.5, 12)
 AT_W8_MID, AT_W4_MID, AT_W8_HI, AT_W4_HI = 8, 9, 21.5, 23.5
-AT_W2 = 41.5
-AT_BUF = (4, 31.75, 39.75, 47.75)
-AT_Y0, AT_Y1, AT_WGO = AT_BUF[0], AT_BUF[3], AT_BUF[1]
+AT_W2 = 30.5
+AT_BUF = (37, 4, 37, 47.75)
+AT_Y0, AT_Y1, AT_WGO = AT_BUF[1], AT_BUF[3], AT_W2
 AT_LAST_H = AT_BUF[2]
 
 
@@ -200,7 +200,7 @@ def tile_list_tote_lane_features_kernel(
         last_step = []
         wgs_t = held("wgs_t", [P, S], F32, tag="w1_raw0")
 
-        def plan(k):
+        def plan(k, only=None, number=None):
             s, half = ORDER[k]
             entries = slice(half * HALF, (half + 1) * HALF)
             rows = slice(s * P, (s + 1) * P)
@@ -208,7 +208,10 @@ def tile_list_tote_lane_features_kernel(
                 numbers = PRODUCT_BANKS[3:] + SUM_BANKS
             else:
                 numbers = [PRODUCT_BANKS[(3 * k + i) % len(PRODUCT_BANKS)] for i in range(3)]
-            hold_ps, move_ps, gate_ps = [bank(number, name) for number, name in zip(numbers, ("hold_ps", "move_ps", "gate_ps"))]
+            if only is None:
+                hold_ps, move_ps, gate_ps = [bank(number, name) for number, name in zip(numbers, ("hold_ps", "move_ps", "gate_ps"))]
+            else:
+                hold_ps = move_ps = gate_ps = bank(number, "product_ps")
             passes = []
             for a in range(PASSES):
                 w4_codes = (w4_lo[:, a, :], w4_mid[:, a, :], w4_hi[:, a, 0 : 2 * P], w4_hi[:, a, 2 * P : 4 * P])[s]
@@ -222,7 +225,7 @@ def tile_list_tote_lane_features_kernel(
                 passes.append((2, a, gate_ps, w4_codes.bitcast(FP4X4), w4_s[:, a, rows], a == 0, final))
             if s > 0:
                 passes = [entry for product in range(3) for entry in passes if entry[0] == product]
-            return (hold_ps, move_ps, gate_ps), [entry + (entries,) for entry in passes]
+            return (hold_ps, move_ps, gate_ps), [entry + (entries,) for entry in passes if only in (None, entry[0])]
 
         def run(passes):
             for product, a, acc, codes, scales, first, final, entries in passes:
@@ -264,6 +267,35 @@ def tile_list_tote_lane_features_kernel(
                     nc.gpsimd.tensor_tensor(h[:], part[:], hold[:], ALU.add)
                 else:
                     last_step.extend((part, hold))
+            weighted[k] = h
+
+        parts = {}
+
+        def one_product(k, product, number):
+            banks, passes = plan(k, product, number)
+            run(passes)
+            if product == 2:
+                parts[k, 2] = ring.tile([P, HALF], F32, name="gate", bufs=CHUNKS)
+                nc.scalar.activation(out=parts[k, 2][:], in_=banks[2][:], func=ACT.Sigmoid)
+            else:
+                parts[k, product] = held(("hold%d", "h%d")[product] % k, [P, HALF], F32)
+                nc.scalar.activation(out=parts[k, product][:], in_=banks[product][:], func=ACT.Copy, scale=(-1.0, 1.0)[product])
+
+        def steps(k):
+            hold, h, gate = [parts[k, n] for n in range(3)]
+            part = held("part%d" % k, [P, HALF], F32, tag="part") if k >= WEIGHED_ON_GPSIMD else h
+            if k in DIFFERENCE_IN_PSUM:
+                nc.gpsimd.tensor_tensor(part[:], h[:], gate[:], ALU.mult)
+            else:
+                nc.gpsimd.tensor_tensor(part[:], h[:], hold[:], ALU.subtract)
+                nc.gpsimd.tensor_tensor(part[:], part[:], gate[:], ALU.mult)
+            if k == WEIGHED_ON_GPSIMD:
+                nc.gpsimd.tensor_tensor(part[:], part[:], hold[:], ALU.add)
+                nc.gpsimd.tensor_tensor(h[:], part[:], wgs_sb[ORDER[k][1]][:], ALU.mult)
+            elif k < CHUNKS - 1:
+                nc.gpsimd.tensor_tensor(h[:], part[:], hold[:], ALU.add)
+            else:
+                last_step.extend((part, hold))
             weighted[k] = h
 
         def wgs_to_psum(half):
@@ -327,14 +359,7 @@ def tile_list_tote_lane_features_kernel(
         wgs_to_psum(0)
         scatter_to_page(1)
         round_w1(3)
-        for k in range(2, CHUNKS - 1):
-            first_stage(k + 1)
-            scatter_to_page(k)
-        round_and_interleave(w2_g[:], w2_raw[:], 1.0)
         last = SLICES - 1
-        open_sums = {}
-        last_banks = SUM_BANKS + (WGS_BANKS[1], PRODUCT_BANKS[0])
-        back_banks = PRODUCT_BANKS[1:] + WGS_BANKS[:1]
         sums = {}
 
         def open_sum(s, q, number):
@@ -345,24 +370,56 @@ def tile_list_tote_lane_features_kernel(
             turn(sums[s, q], pages[s], q, False)
             round_sum(sums[s, q], s, q, nc.scalar.copy)
 
-        for s in (0, 1, last, last - 1):
+        def whole_sum(s, q, number):
+            open_sum(s, q, number)
+            close_sum(s, q)
+
+        for s in (0, last, 1):
             load_buf(s)
-        for q in range(QUARTERS):
-            open_sum(0, q, SUM_BANKS[q % 2])
-            close_sum(0, q)
-        for q in range(QUARTERS - 1):
-            open_sum(1, q, back_banks[q])
-        for q in range(QUARTERS):
-            open_sum(last, q, last_banks[q])
-            open_sums[q] = sums[last, q]
+        for k in (2, 3):
+            first_stage(k + 1)
+            scatter_to_page(k)
+        a, b, c, d = PRODUCT_BANKS
+        e, f = SUM_BANKS
+        whole_sum(0, 0, e)
+        whole_sum(0, 1, f)
+        one_product(5, 0, d)
+        whole_sum(0, 2, a)
+        one_product(5, 1, e)
+        whole_sum(0, 3, b)
+        one_product(5, 2, f)
+        steps(5)
+        scatter_to_page(4)
+        load_buf(last - 1)
+        open_sum(last, 0, c)
+        one_product(6, 1, a)
+        open_sum(last, 1, d)
+        one_product(6, 2, b)
+        open_sum(1, 0, e)
+        one_product(6, 0, f)
+        steps(6)
+        scatter_to_page(5)
+        open_sum(last, 2, WGS_BANKS[1])
+        for q, number in ((1, a), (2, b), (3, f)):
+            open_sum(1, q, number)
         close_sum(1, 0)
-        open_sum(1, QUARTERS - 1, back_banks[0])
-        for q in range(1, QUARTERS):
-            close_sum(1, q)
+        close_sum(1, 1)
+        one_product(7, 0, e)
+        close_sum(1, 2)
+        one_product(7, 1, a)
+        close_sum(1, 3)
+        one_product(7, 2, b)
+        steps(7)
+        scatter_to_page(6)
+        open_sum(last, 3, f)
+        last_banks = (c, d, WGS_BANKS[1], f)
+        back_banks = (e, a, b, WGS_BANKS[0])
         for q in range(QUARTERS):
             open_sum(last - 1, q, back_banks[q])
+        round_and_interleave(w2_g[:], w2_raw[:], 1.0)
         for q in range(QUARTERS):
             close_sum(last - 1, q)
+        open_sums = [sums[last, q] for q in range(QUARTERS)]
         weighted[CHUNKS - 1] = placed("h_last", [P, HALF], F32, AT_LAST_H)
         nc.gpsimd.tensor_tensor(weighted[CHUNKS - 1][:], last_step[0][:], last_step[1][:], ALU.add)
         scatter_to_page(CHUNKS - 1)

from contextlib import ExitStack

import concourse.mybir as mybir
from concourse.masks import make_identity

K, H, N, T, S, T2, P_OUT = 1024, 512, 384, 4096, 1024, 2048, 1024
FLOPS = 2 * (3 * K * H * S + H * N * T2)

F32 = mybir.dt.float32
BF16 = mybir.dt.bfloat16
I32 = mybir.dt.int32
U32 = mybir.dt.uint32
U16 = mybir.dt.uint16
U8 = mybir.dt.uint8
FP8X4 = mybir.dt.float8_e4m3fn_x4
FP4X4 = mybir.dt.float4_e2m1fn_x4
ALU = mybir.AluOpType
ACT = mybir.ActivationFunctionType

P = 128
PACK = 4
PASSES = K // (P * PACK)
QUADRANTS = 4
SLICES = H // P
BANK = 512
HALF = BANK
HALVES = S // HALF
HALF_COLS = HALF // 16
CHUNKS = SLICES * HALVES
QUARTERS = T2 // BANK
SCALE_ROW0 = P - PASSES * 16

ORDER = ((0, 0), (0, 1), (1, 0), (1, 1), (2, 0), (3, 0), (2, 1), (3, 1))

DIFFERENCE_IN_PSUM = (1, 3, 6)

WEIGHED_ON_GPSIMD = 6

WGS_BANKS = (0, 1)
PRODUCT_BANKS = (2, 3, 4, 5)
SUM_BANKS = (6, 7)

AT_WORDS = (8, 32)
AT_SCALES = 28.25
AT_W4_LO = 31.5
AT_W8_LO = 30.5
AT_W1 = (None, 24.5, 16, 32)
AT_WGS = (28.5, 12)
AT_W8_MID, AT_W4_MID, AT_W8_HI, AT_W4_HI = 8, 9, 21.5, 23.5
AT_W2 = 30.5
AT_BUF = (37, 4, 37, 47.75)
AT_Y0, AT_Y1, AT_WGO = AT_BUF[1], AT_BUF[3], AT_W2
AT_LAST_H = AT_BUF[2]


def tile_list_tote_lane_features_kernel(
    tc, tab_words, tab_scales, offs, w4_words, w4_scales, w8_words, w8_scales, w1, offs2, wgs, buf, w2, offs3, offs4, wgo, out
):
    nc = tc.nc
    with ExitStack() as ctx:
        keep = ctx.enter_context(tc.tile_pool(name="keep", bufs=1))
        ring = ctx.enter_context(tc.tile_pool(name="ring", bufs=4))
        arena = ctx.enter_context(tc.tile_pool(name="arena", bufs=1))
        psum = ctx.enter_context(tc.psum_pool(name="psum", bufs=1))

        def held(name, shape, dtype, tag=None):
            return keep.tile(shape, dtype, name=name, tag=tag or name, align_bytes=64)

        def placed(name, shape, dtype, kib):
            return arena.tile(shape, dtype, name=name, align_bytes=64, offset=int(kib * 1024))

        def bank(number, name):
            return psum.tile([P, BANK], F32, name=name, tag="bank%d" % number)

        def round_and_interleave(grouped, raw, sign):
            nc.scalar.activation(out=grouped.rearrange("p (c i) j -> p c j i", i=4), in_=raw.rearrange("p j (c i) -> p c j i", i=4),
                                 func=ACT.Copy, scale=sign)

        list1 = held("list1", [P, S // 16], U16)
        list2 = held("list2", [P, S // 16], U16)
        list3 = held("list3", [P, P_OUT // 16], U16)
        list4 = held("list4", [P, P_OUT // 16], U16)
        tab_s = placed("tab_s", [P, T], U8, AT_SCALES)
        w4_s = held("w4_s", [P, PASSES, H], U8)
        w8_s = held("w8_s", [P, PASSES, H], U8)
        v_s = held("v_s", [P, PASSES, S], U8)
        w1_raw0 = held("w1_raw0", [P, PASSES, PACK, P], F32)

        for plane in (w4_s, w8_s):
            nc.vector.memset(plane[:].rearrange("p a c -> p (a c)").bitcast(I32), 0)
        nc.vector.memset(tab_s[:].bitcast(I32)[0:SCALE_ROW0, :], 0)
        nc.vector.memset(v_s[:].rearrange("p a c -> p (a c)").bitcast(I32), 0)

        nc.sync.dma_start(list1[:], offs)
        nc.sync.dma_start(out=tab_s[:].bitcast(I32)[SCALE_ROW0:P, :], in_=tab_scales.bitcast(I32).rearrange("a g t -> g a t"))
        w1_rows = w1.rearrange("(a p j) c -> a p j c", a=PASSES, j=PACK)
        for a in range(PASSES):
            nc.scalar.dma_start(out=w1_raw0[:, a, :, :], in_=w1_rows[a][:, :, 0:P])
        w8_words_i = w8_words.rearrange("a p c j -> p a (c j)").bitcast(I32)
        w4_words_i = w4_words.rearrange("a p c -> p a c").bitcast(I32)
        nc.sync.dma_start(list2[:], offs2)
        nc.sync.dma_start(list3[:], offs3)
        tab_words_i = tab_words.rearrange("a p t j -> a p (t j)").bitcast(I32)
        tab_w0 = placed("tab_w0", [P, T], U32, AT_WORDS[0])
        nc.sync.dma_start(out=tab_w0[:].bitcast(I32), in_=tab_words_i[0])
        nc.sync.dma_start(list4[:], offs4)

        warm = held("warm", [P, 2], F32)
        nc.vector.memset(warm[:, 0:1], 0.0)
        nc.scalar.activation(out=warm[:, 1:2], in_=warm[:, 0:1], func=ACT.Sigmoid)

        for plane, scale_input, queue in ((w8_s, w8_scales, nc.gpsimd), (w4_s, w4_scales, nc.gpsimd)):
            for Q in range(QUADRANTS):
                queue.dma_start(
                    out=plane[:].bitcast(I32)[32 * Q : 32 * Q + 4, :, :],
                    in_=scale_input.rearrange("a g c -> g a c").bitcast(I32)[4 * Q : 4 * Q + 4, :, :],
                )

        ident = held("ident", [P, P], F32)
        make_identity(nc, ident[:])

        picked_s = held("picked_s", [P, S], U8)
        nc.vector.tensor_copy(picked_s[:], tab_s[:].indirect(list1[:]))

        def move_scale_rows(Q, queue):
            row = SCALE_ROW0 + 8 * Q
            queue.dma_start(out=v_s[:].rearrange("p a c -> p (a c)").bitcast(I32)[32 * Q : 32 * Q + 4, :], in_=picked_s[:].bitcast(I32)[row : row + 8, :])

        for Q in range(QUADRANTS - 1):
            move_scale_rows(Q, nc.scalar)
        tab_w1 = placed("tab_w1", [P, T], U32, AT_WORDS[1])
        nc.sync.dma_start(out=tab_w1[:].bitcast(I32)[:, 0 : T // 2], in_=tab_words_i[1][:, 0 : T // 2])
        move_scale_rows(QUADRANTS - 1, nc.sync)
        nc.sync.dma_start(out=tab_w1[:].bitcast(I32)[:, T // 2 : T], in_=tab_words_i[1][:, T // 2 : T])
        w8_lo = placed("w8_lo", [P, PASSES, P], U32, AT_W8_LO)
        nc.sync.dma_start(out=w8_lo[:].bitcast(I32), in_=w8_words_i[:, :, 0:P])
        w4_lo = placed("w4_lo", [P, PASSES, 2 * P], U8, AT_W4_LO)
        nc.sync.dma_start(out=w4_lo[:].bitcast(I32), in_=w4_words_i[:, :, 0 : P // 2])
        v_w = [held("v_w%d" % a, [P, S], U32) for a in range(PASSES)]
        for half in range(HALVES):
            offsets = list1[:, half * HALF_COLS : (half + 1) * HALF_COLS]
            nc.vector.tensor_copy(v_w[0][:, half * HALF : (half + 1) * HALF], tab_w0[:].indirect(offsets))

        w1_raw = [w1_raw0]

        def load_w1(s):
            w1_raw.append(placed("w1_raw%d" % s, [P, PASSES, PACK, P], F32, AT_W1[s]))
            for a in range(PASSES):
                nc.sync.dma_start(out=w1_raw[s][:, a, :, :], in_=w1_rows[a][:, :, s * P : (s + 1) * P])

        load_w1(1)
        wgs_sb = [placed("wgs_sb%d" % half, [P, HALF], F32, AT_WGS[half]) for half in range(HALVES)]
        for half in range(HALVES):
            nc.sync.dma_start(out=wgs_sb[half][:], in_=wgs[:, half * HALF : (half + 1) * HALF])
        w8_mid = placed("w8_mid", [P, PASSES, P], U32, AT_W8_MID)
        nc.sync.dma_start(out=w8_mid[:].bitcast(I32), in_=w8_words_i[:, :, P : 2 * P])
        w4_mid = placed("w4_mid", [P, PASSES, 2 * P], U8, AT_W4_MID)
        nc.sync.dma_start(out=w4_mid[:].bitcast(I32), in_=w4_words_i[:, :, P // 2 : P])
        load_w1(2)
        w8_hi = placed("w8_hi", [P, PASSES, 2 * P], U32, AT_W8_HI)
        nc.sync.dma_start(out=w8_hi[:].bitcast(I32), in_=w8_words_i[:, :, 2 * P : H])
        w4_hi = placed("w4_hi", [P, PASSES, 4 * P], U8, AT_W4_HI)
        nc.sync.dma_start(out=w4_hi[:].bitcast(I32), in_=w4_words_i[:, :, P : H // 2])

        w1_g, w1_c = {}, {}
        w1_s = held("w1_s", [P, SLICES, PASSES, P], U8)

        def round_w1(s):
            w1_g[s] = held("w1_g%d" % s, [P, PASSES, P, PACK], BF16)
            for a in range(PASSES):
                round_and_interleave(w1_g[s][:, a, :, :], w1_raw[s][:, a, :, :], -1.0)

        def quantise_w1(s, tag=None):
            w1_c[s] = held("w1_c%d" % s, [P, PASSES, P], U32, tag=tag)
            nc.vector.quantize_mx(
                out=w1_c[s][:].rearrange("p a c -> p (a c)").bitcast(FP8X4),
                scales=w1_s[:, s, :, :].rearrange("p a c -> p (a c)"),
                in_=w1_g[s][:].rearrange("p a c j -> p (a c j)"),
            )

        round_w1(0)
        quantise_w1(0)

        pages = [held("page%d" % s, [P, T2], F32, tag="w1_g0" if s == SLICES - 1 else None) for s in range(SLICES)]
        for s in range(SLICES - 1):
            for q in range(QUARTERS):
                nc.gpsimd.memset(pages[s][:, q * BANK : (q + 1) * BANK], 0.0)
        nc.vector.memset(pages[SLICES - 1][:].bitcast(I32), 0)

        for half in range(HALVES):
            offsets = list1[:, half * HALF_COLS : (half + 1) * HALF_COLS]
            nc.vector.tensor_copy(v_w[1][:, half * HALF : (half + 1) * HALF], tab_w1[:].indirect(offsets))

        load_w1(3)
        w2_raw = placed("w2_raw", [P, PACK, N], F32, AT_W2)
        nc.sync.dma_start(out=w2_raw[:], in_=w2.rearrange("(p j) n -> p j n", j=PACK))

        weighted = {}
        wgs_ps = {}
        last_step = []
        wgs_t = held("wgs_t", [P, S], F32, tag="w1_raw0")

        def plan(k, only=None, number=None):
            s, half = ORDER[k]
            entries = slice(half * HALF, (half + 1) * HALF)
            rows = slice(s * P, (s + 1) * P)
            if k == 1:
                numbers = PRODUCT_BANKS[3:] + SUM_BANKS
            else:
                numbers = [PRODUCT_BANKS[(3 * k + i) % len(PRODUCT_BANKS)] for i in range(3)]
            if only is None:
                hold_ps, move_ps, gate_ps = [bank(number, name) for number, name in zip(numbers, ("hold_ps", "move_ps", "gate_ps"))]
            else:
                hold_ps = move_ps = gate_ps = bank(number, "product_ps")
            passes = []
            for a in range(PASSES):
                w4_codes = (w4_lo[:, a, :], w4_mid[:, a, :], w4_hi[:, a, 0 : 2 * P], w4_hi[:, a, 2 * P : 4 * P])[s]
                w8_codes = (w8_lo[:, a, :], w8_mid[:, a, :], w8_hi[:, a, 0:P], w8_hi[:, a, P : 2 * P])[s]
                first, final = a == 0, a == PASSES - 1
                passes.append((0, a, hold_ps, w1_c[s][:, a, :].bitcast(FP8X4), w1_s[:, s, a, :], first, final))
                if k in DIFFERENCE_IN_PSUM:
                    passes.append((1, a, move_ps, w1_c[s][:, a, :].bitcast(FP8X4), w1_s[:, s, a, :], first, False))
                    first = False
                passes.append((1, a, move_ps, w8_codes.bitcast(FP8X4), w8_s[:, a, rows], first, final))
                passes.append((2, a, gate_ps, w4_codes.bitcast(FP4X4), w4_s[:, a, rows], a == 0, final))
            if s > 0:
                passes = [entry for product in range(3) for entry in passes if entry[0] == product]
            return (hold_ps, move_ps, gate_ps), [entry + (entries,) for entry in passes if only in (None, entry[0])]

        def run(passes):
            for product, a, acc, codes, scales, first, final, entries in passes:
                nc.tensor.matmul_mx(
                    out=acc[:], lhsT=codes, lhsT_scale=scales,
                    rhs=v_w[a][:, entries].bitcast(FP8X4), rhs_scale=v_s[:, a, entries],
                    start=first, stop=final,
                )

        begun = {}

        def first_stage(k):
            s, half = ORDER[k]
            (hold_ps, move_ps, gate_ps), passes = begun[k] if k in begun else plan(k)
            run(passes)
            hold = held("hold%d" % k, [P, HALF], F32)
            gate = ring.tile([P, HALF], F32, name="gate", bufs=CHUNKS)
            h = held("h%d" % k, [P, HALF], F32)
            nc.scalar.activation(out=hold[:], in_=hold_ps[:], func=ACT.Copy, scale=-1.0)
            if k == 0:
                nc.scalar.activation(out=gate[:], in_=gate_ps[:], func=ACT.Sigmoid)
                part = held("part", [P, HALF], F32)
                for target, first, other, op in ((part, move_ps, hold, ALU.subtract), (part, part, gate, ALU.mult), (part, part, hold, ALU.add), (h, part, wgs_sb[half], ALU.mult)):
                    for cols in (slice(0, HALF // 2), slice(HALF // 2, HALF)):
                        nc.vector.tensor_tensor(target[:, cols], first[:, cols], other[:, cols], op)
            else:
                nc.scalar.copy(out=h[:], in_=move_ps[:])
                nc.scalar.activation(out=gate[:], in_=gate_ps[:], func=ACT.Sigmoid)
                part = held("part%d" % k, [P, HALF], F32, tag="part") if k == 1 or k >= WEIGHED_ON_GPSIMD else h
                if k in DIFFERENCE_IN_PSUM:
                    nc.gpsimd.tensor_tensor(part[:], h[:], gate[:], ALU.mult)
                else:
                    nc.gpsimd.tensor_tensor(part[:], h[:], hold[:], ALU.subtract)
                    nc.gpsimd.tensor_tensor(part[:], part[:], gate[:], ALU.mult)
                if k == WEIGHED_ON_GPSIMD:
                    nc.gpsimd.tensor_tensor(part[:], part[:], hold[:], ALU.add)
                    nc.gpsimd.tensor_tensor(h[:], part[:], wgs_sb[half][:], ALU.mult)
                elif k < CHUNKS - 1:
                    nc.gpsimd.tensor_tensor(h[:], part[:], hold[:], ALU.add)
                else:
                    last_step.extend((part, hold))
            weighted[k] = h

        parts = {}

        def one_product(k, product, number):
            banks, passes = plan(k, product, number)
            run(passes)
            if product == 2:
                parts[k, 2] = ring.tile([P, HALF], F32, name="gate", bufs=CHUNKS)
                nc.scalar.activation(out=parts[k, 2][:], in_=banks[2][:], func=ACT.Sigmoid)
            else:
                parts[k, product] = held(("hold%d", "h%d")[product] % k, [P, HALF], F32)
                nc.scalar.activation(out=parts[k, product][:], in_=banks[product][:], func=ACT.Copy, scale=(-1.0, 1.0)[product])

        def steps(k):
            hold, h, gate = [parts[k, n] for n in range(3)]
            part = held("part%d" % k, [P, HALF], F32, tag="part") if k >= WEIGHED_ON_GPSIMD else h
            if k in DIFFERENCE_IN_PSUM:
                nc.gpsimd.tensor_tensor(part[:], h[:], gate[:], ALU.mult)
            else:
                nc.gpsimd.tensor_tensor(part[:], h[:], hold[:], ALU.subtract)
                nc.gpsimd.tensor_tensor(part[:], part[:], gate[:], ALU.mult)
            if k == WEIGHED_ON_GPSIMD:
                nc.gpsimd.tensor_tensor(part[:], part[:], hold[:], ALU.add)
                nc.gpsimd.tensor_tensor(h[:], part[:], wgs_sb[ORDER[k][1]][:], ALU.mult)
            elif k < CHUNKS - 1:
                nc.gpsimd.tensor_tensor(h[:], part[:], hold[:], ALU.add)
            else:
                last_step.extend((part, hold))
            weighted[k] = h

        def wgs_to_psum(half):
            turned = bank(WGS_BANKS[half], "wgs_turned")
            for b in range(HALF // P):
                nc.tensor.transpose(turned[:, b * P : (b + 1) * P], wgs_sb[half][:, b * P : (b + 1) * P], ident[:])
            nc.scalar.copy(out=wgs_t[:, half * HALF : (half + 1) * HALF], in_=turned[:])
            wgs_ps[half] = bank(WGS_BANKS[half], "wgs_ps")
            for b in range(HALF // P):
                col0 = half * HALF + b * P
                nc.tensor.transpose(wgs_ps[half][:, b * P : (b + 1) * P], wgs_t[:, col0 : col0 + P], ident[:])

        def scatter_to_page(k):
            s, half = ORDER[k]
            window = pages[s][:].indirect(list2[:, half * HALF_COLS : (half + 1) * HALF_COLS])
            if k < CHUNKS - 1:
                if k not in (0, WEIGHED_ON_GPSIMD):
                    nc.vector.tensor_tensor(weighted[k][:], weighted[k][:], wgs_ps[half][:], ALU.mult)
                if 1 <= k < SLICES - 1:
                    quantise_w1(k + 1, tag="hold%d" % k)
                nc.vector.tensor_copy(window, weighted[k][:])
            else:
                nc.vector.tensor_tensor(window, weighted[k][:], wgs_sb[half][:], ALU.mult)

        states = {}

        def load_buf(s):
            states[s] = placed("state%d" % s, [P, T2], F32, AT_BUF[s])
            nc.sync.dma_start(out=states[s][:], in_=buf[s * P : (s + 1) * P, :])

        z_t = [held("z_t%d" % q, [P, BANK // P, H], BF16) for q in range(QUARTERS)]

        def turn(acc, source, q, opens):
            for b in range(BANK // P):
                col0 = q * BANK + b * P
                nc.tensor.matmul(out=acc[:, b * P : (b + 1) * P], lhsT=source[:, col0 : col0 + P], rhs=ident[:],
                                 is_transpose=True, start=(opens and b == 0), stop=(not opens and b == BANK // P - 1))

        def round_sum(acc, s, q, copy):
            copy(
                out=z_t[q][:].rearrange("t b (u p e) -> t b u p e", u=2, e=2)[:, :, :, 32 * s : 32 * (s + 1), :],
                in_=acc[:].rearrange("t (b p u e) -> t b u p e", b=BANK // P, u=2, e=2),
            )

        w2_g = held("w2_g", [P, N, PACK], BF16)

        for k, early in ((0, 1), (1, 2)):
            banks, passes = plan(k)
            run(passes[:early])
            begun[k] = banks, passes[early:]
        banks, passes = begun[0]
        begun[0] = banks, [passes[n] for n in (0, 2, 3, 1, 4)]
        first_stage(0)
        round_w1(1)
        quantise_w1(1)
        first_stage(1)
        wgs_to_psum(1)
        scatter_to_page(0)
        round_w1(2)
        first_stage(2)
        wgs_to_psum(0)
        scatter_to_page(1)
        round_w1(3)
        last = SLICES - 1
        sums = {}

        def open_sum(s, q, number):
            sums[s, q] = bank(number, "z_ps")
            turn(sums[s, q], states[s], q, True)

        def close_sum(s, q):
            turn(sums[s, q], pages[s], q, False)
            round_sum(sums[s, q], s, q, nc.scalar.copy)

        def whole_sum(s, q, number):
            open_sum(s, q, number)
            close_sum(s, q)

        for s in (0, last, 1):
            load_buf(s)
        for k in (2, 3):
            first_stage(k + 1)
            scatter_to_page(k)
        a, b, c, d = PRODUCT_BANKS
        e, f = SUM_BANKS
        whole_sum(0, 0, e)
        whole_sum(0, 1, f)
        one_product(5, 0, d)
        whole_sum(0, 2, a)
        one_product(5, 1, e)
        whole_sum(0, 3, b)
        one_product(5, 2, f)
        steps(5)
        scatter_to_page(4)
        load_buf(last - 1)
        open_sum(last, 0, c)
        one_product(6, 1, a)
        open_sum(last, 1, d)
        one_product(6, 2, b)
        open_sum(1, 0, e)
        one_product(6, 0, f)
        steps(6)
        scatter_to_page(5)
        open_sum(last, 2, WGS_BANKS[1])
        for q, number in ((1, a), (2, b), (3, f)):
            open_sum(1, q, number)
        close_sum(1, 0)
        close_sum(1, 1)
        one_product(7, 0, e)
        close_sum(1, 2)
        one_product(7, 1, a)
        close_sum(1, 3)
        one_product(7, 2, b)
        steps(7)
        scatter_to_page(6)
        open_sum(last, 3, f)
        last_banks = (c, d, WGS_BANKS[1], f)
        back_banks = (e, a, b, WGS_BANKS[0])
        for q in range(QUARTERS):
            open_sum(last - 1, q, back_banks[q])
        round_and_interleave(w2_g[:], w2_raw[:], 1.0)
        for q in range(QUARTERS):
            close_sum(last - 1, q)
        open_sums = [sums[last, q] for q in range(QUARTERS)]
        weighted[CHUNKS - 1] = placed("h_last", [P, HALF], F32, AT_LAST_H)
        nc.gpsimd.tensor_tensor(weighted[CHUNKS - 1][:], last_step[0][:], last_step[1][:], ALU.add)
        scatter_to_page(CHUNKS - 1)
        w2_c = placed("w2_c", [P, N], U32, AT_LAST_H)
        w2_s = held("w2_s", [P, N], U8)
        for n0, n1 in ((0, 2 * P), (2 * P, N)):
            nc.vector.quantize_mx(out=w2_c[:, n0:n1].bitcast(FP8X4), scales=w2_s[:, n0:n1],
                                  in_=w2_g[:, n0:n1, :].rearrange("p c j -> p (c j)"))

        wgo_sb = placed("wgo_sb", [P, P_OUT], F32, AT_WGO)
        nc.sync.dma_start(out=wgo_sb[:], in_=wgo)

        lanes = [held("lanes0", [P, T2], F32, tag="hold%d" % (CHUNKS - 1))]
        for q in range(QUARTERS):
            nc.gpsimd.memset(lanes[0][:, q * BANK : (q + 1) * BANK], 0.0)

        z_c = held("z_c", [P, T2], U32)
        z_s = held("z_s", [P, T2], U8)
        ys = [placed("y0", [P, T2], F32, AT_Y0), placed("y1", [P, T2], F32, AT_Y1), held("y2", [P, T2], F32)]

        copies = (nc.scalar.copy, nc.vector.tensor_copy)
        for q in range(QUARTERS):
            turn(open_sums[q], pages[SLICES - 1], q, False)
            round_sum(open_sums[q], SLICES - 1, q, copies[q % 2])
        piece = 2 * P
        for step in range(T2 // piece):
            q, b0 = divmod(2 * step, BANK // P)
            pairs = z_t[q][:].bitcast(F32)
            back = bank((back_banks + last_banks)[step], "back_ps")
            for b in range(2):
                for u in range(2):
                    nc.tensor.transpose(back[:, (2 * b + u) * P : (2 * b + u + 1) * P], pairs[:, b0 + b, u * P : (u + 1) * P], ident[:])
            z_g = ring.tile([P, piece * PACK], BF16, name="z_g", align_bytes=64)
            copies[step in (1, 3)](out=z_g[:].bitcast(F32).rearrange("p (b t u) -> p b t u", b=2, u=2),
                             in_=back[:].rearrange("p (b u t) -> p b t u", b=2, u=2))
            cols = slice(step * piece, (step + 1) * piece)
            nc.vector.quantize_mx(out=z_c[:, cols].bitcast(FP8X4), scales=z_s[:, cols], in_=z_g[:])

        y_banks = 2 * (back_banks + last_banks)
        spans = [(q * BANK, BANK) for q in range(QUARTERS)]
        first_spans = spans[:-1] + [(T2 - 2 * piece, piece), (T2 - piece, piece)]
        work = [(n, span) for n in range(N // P) for span in (first_spans if n == 0 else spans)]
        for count, (n, (col0, width)) in enumerate(work):
            cols = slice(col0, col0 + width)
            y_ps = bank(y_banks[count], "y_ps")
            nc.tensor.matmul_mx(
                out=y_ps[:, 0:width], lhsT=w2_c[:, n * P : (n + 1) * P].bitcast(FP8X4), lhsT_scale=w2_s[:, n * P : (n + 1) * P],
                rhs=z_c[:, cols].bitcast(FP8X4), rhs_scale=z_s[:, cols], start=True, stop=True,
            )
            copy = copies[n == 0 and count not in (0, 2)]
            copy(out=ys[n][:, cols], in_=y_ps[:, 0:width])

        picked = []

        def pick(n):
            x = keep.tile([P, P_OUT], F32, name="x%d" % n)
            nc.vector.tensor_copy(x[:], ys[n][:].indirect(list3[:]))
            nc.scalar.activation(out=x[:], in_=x[:], func=ACT.Tanh)
            picked.append(x)
            if n > 0:
                lanes.append(placed("lanes1", [P, T2], F32, AT_Y1) if n == 1 else held("lanes2", [P, T2], F32, tag="y2"))
                nc.gpsimd.memset(lanes[n][:], 0.0)

        pick(0)
        for n in range(N // P):
            if n + 1 < N // P:
                pick(n + 1)
            nc.vector.tensor_tensor(lanes[n][:].indirect(list4[:]), picked[n][:], wgo_sb[:], ALU.mult)
            nc.sync.dma_start(out=out[n * P : (n + 1) * P, :], in_=lanes[n][:])
